import numpy as np, ml_dtypes
CORES = [10,34,74,98]
N = 4
BF = ml_dtypes.bfloat16
def gentries(a):
    return np.ascontiguousarray(a.reshape(8, 16, -1).transpose(0, 2, 1)).reshape(8, -1)
def gtable(e):
    e = np.asarray(e); return np.ascontiguousarray(e.reshape(8, -1, 16).transpose(0, 2, 1)).reshape(128, -1).astype(np.int32)
V, G, B, L, RO = 2048, 256, 1, 128, 3
W = V + B * G
def numbers(rng, ghost):
    s = (N, 8, V, 16)
    return np.where(rng.random(s) < ghost, rng.integers(V, W, s), rng.integers(0, V, s))
def image(t, nb):
    tw = np.concatenate([t, np.broadcast_to(np.arange(V, W), (N, 8, W - V))], axis=2)
    e = np.take_along_axis(tw, nb.reshape(N, 8, -1), 2).reshape(nb.shape)
    return np.take_along_axis(e, np.argsort(t, axis=-1)[..., None], 2)
def parts(rng, z, wild, mix):
    t = np.argsort(rng.random((N, 8, V)), axis=-1); nb = numbers(rng, 0.125)
    nz = np.where(rng.random(nb.shape) < wild, numbers(rng, 0.125), image(t, nb))
    x = np.clip(np.take_along_axis(z, t[:, :, None, :], 3) + rng.integers(-2, 3, z.shape), 0, 255)
    x = np.where(rng.random(z.shape) < 0.1, rng.integers(0, 256, z.shape), x)
    o = np.argsort(rng.random((N, 8, V)), axis=-1); m = t.copy()
    for r in range(N):
        for g in range(8):
            j = o[r, g, :int(V * mix[r, g])]; m[r, g, j] = t[r, g, np.roll(j, 1)]
    bx = np.ascontiguousarray(np.argsort(rng.random((N, 8, V)), axis=-1)[..., :G]); bz = np.take_along_axis(t, bx, 2)
    return {"x": x, "z": z, "nb": nb, "nz": nz, "m": m, "bx": bx, "bz": bz}
def pack(d):
    return {"x": np.ascontiguousarray(d["x"].reshape(N, 128, V)).astype(np.float32).astype(BF), "z": np.ascontiguousarray(d["z"].reshape(N, 128, V)).astype(np.float32).astype(BF),
            "nb": np.stack([gtable(a.reshape(8, -1)) for a in d["nb"]]), "nz": np.stack([gtable(a.reshape(8, -1)) for a in d["nz"]]),
            "m": d["m"].astype(np.int32), "im": np.argsort(d["m"], axis=-1).astype(np.int32),
            "bx": np.stack([gtable(a) for a in d["bx"]]), "bz": np.stack([gtable(a) for a in d["bz"]])}
def setup_inputs(rng):
    size = rng.permuted(np.tile(np.array([1, 1, 3, 3, 15, 63, 255, 255]), (N, 1)), axis=1)[:, :, None, None]
    z = rng.integers(0, size + 1, (N, 8, 16, V))
    wild = rng.choice(np.array([0.05, 0.2, 0.5, 1.0]), (N, 8, 1, 1)); mix = rng.choice(np.array([0.1, 0.3, 0.6, 1.0]), (N, 8))
    h = int(rng.integers(0, 8)); wild[:, h] = 0.0; mix[:, h] = 0.05
    return pack(parts(rng, z, wild, mix))
def setup_inputs_ties(rng):
    z = rng.integers(0, 2, (N, 8, 16, V)) * (rng.random((N, 8, 1, V)) < 0.5); z[:, 1, 1:] = 0
    d = parts(rng, z, rng.choice(np.array([0.2, 1.0]), (N, 8, 1, 1)), np.full((N, 8), 0.8))
    u = (np.arange(L) * (V // L))[1::2]
    for r in range(N):
        for g in (0, 2, 4, 6):
            s0 = np.flatnonzero(np.all(z[r, g] == 0, axis=0)); im = np.argsort(d["m"][r, g])
            d["nb"][r, g, u] = im[rng.choice(s0, (len(u), 16))]; d["nz"][r, g, d["m"][r, g, u]] = rng.choice(s0, (len(u), 16))
    d["nb"][:, 5] = rng.integers(0, V, (N, 1, 16))
    return pack(d)
def setup_inputs_crowd(rng):
    z = rng.integers(0, rng.choice(np.array([3, 15, 255]), (N, 8, 1, 1)) + 1, (N, 8, 16, V))
    d = parts(rng, z, np.ones((N, 8, 1, 1)), np.ones((N, 8)))
    for r in range(N):
        for g in range(8):
            n = (24, 160)[g % 2]
            s = np.concatenate([np.array([0, V - 1]), 1 + rng.permutation(V - 2)[:n - 2]]); e = np.concatenate([np.array([0, V - 1]), 1 + rng.permutation(V - 2)[:n - 2]])
            if g < 4: e = d["m"][r, g, s]
            ends = np.array([V, W - 1])
            d["nb"][r, g] = np.where(rng.random((V, 16)) < 0.05, rng.choice(ends, (V, 16)), rng.choice(s, (V, 16)))
            d["nz"][r, g] = np.where(rng.random((V, 16)) < 0.05, rng.choice(ends, (V, 16)), rng.choice(e, (V, 16)))
            d["bx"][r, g] = rng.choice(s, G); d["bz"][r, g] = rng.choice(e, G)
    return pack(d)
def setup_inputs_border(rng):
    z = rng.integers(0, rng.choice(np.array([3, 15, 255]), (N, 8, 1, 1)) + 1, (N, 8, 16, V))
    d = parts(rng, z, np.ones((N, 8, 1, 1)), np.ones((N, 8)))
    for r in range(N):
        for g in range(8):
            s = rng.permutation(V)[:160]; e = d["m"][r, g, s]
            d["nb"][r, g] = np.where(rng.random((V, 16)) < 0.3, rng.integers(V, W, (V, 16)), rng.choice(s, (V, 16)))
            d["nz"][r, g] = np.where(rng.random((V, 16)) < 0.3, rng.integers(V, W, (V, 16)), rng.choice(e, (V, 16)))
            d["bx"][r, g] = rng.choice(s, G); d["bz"][r, g] = rng.choice(e, G)
    d["bx"][:, :, 0] = 0; d["bx"][:, :, G - 1] = V - 1; d["bz"][:, :, 0] = V - 1; d["bz"][:, :, G - 1] = 0
    q = rng.permutation(8); d["nb"][:, q[0]] = rng.integers(V, W, (N, V, 16)); d["nz"][:, q[1]] = rng.integers(V, W, (N, V, 16))
    d["nb"][:, :, 0, :2] = np.array([V, W - 1])
    return pack(d)
def agree(d, r, g):
    t = np.concatenate([d["m"][r, g], np.arange(V, W)]); d["nz"][r, g, t[:V]] = t[d["nb"][r, g]]
def early(rng, d, r, g, n):
    st = np.arange(L) * (V // L); o = rng.permutation(np.setdiff1d(np.arange(V), np.concatenate([st, d["bx"][r, g]])))
    p = o[:2 * n]; a = d["nb"][r, g][st]; a[np.isin(a, p)] = o[2 * n]
    a[rng.permutation(L)[:n], rng.integers(0, 16, n)] = p[:n]; d["nb"][r, g, st] = a
    agree(d, r, g); t = d["m"][r, g].copy(); d["m"][r, g, p] = t[np.roll(p, n)]
def late(rng, d, r, g):
    st = np.arange(L) * (V // L); o = rng.permutation(np.setdiff1d(np.arange(V), np.concatenate([st, d["bx"][r, g], np.array([819, V - 1])])))
    p = o[:6].copy(); s = p[:3]; f = int(o[6]); b = o[7:7 + L].copy(); c = o[7 + L:7 + 2 * L].copy(); rest = o[7 + 2 * L:]
    j = 1 + rng.permutation(L - 1)[:3]; b[j[0]] = 819
    nb = d["nb"][r, g]; nb[np.isin(nb, p)] = f
    nb[p] = rng.choice(rest, (6, 16)); nb[s, rng.integers(0, 16, 3)] = f
    nb[st, 0] = b; nb[b, 0] = c; nb[819, 0] = rng.integers(V, W)
    nb[np.array([b[j[1]], c[j[2]], V - 1]), rng.integers(1, 16, 3)] = s
    agree(d, r, g); t = d["m"][r, g].copy(); z = d["z"][r, g]
    z[:] = rng.integers(0, 200, (16, 1)); z[:, t[s]] += rng.integers(1, 5, (16, 3)); z[int(rng.integers(0, 16)), t[f]] += rng.integers(1, 16)
    d["m"][r, g, p] = t[np.roll(p, 3)]
def setup_inputs_still(rng):
    z = rng.integers(0, 256, (N, 8, 16, V)); d = parts(rng, z, np.zeros((N, 8, 1, 1)), np.zeros((N, 8)))
    q, q2, q3 = [int(i) for i in rng.permutation(N)[:3]]; h, h2 = [int(i) for i in rng.permutation(8)[:2]]; st = np.arange(L) * (V // L)
    room = [L] + [(287 - L + i) // 5 for i in range(5)]
    for r in range(N):
        for g in range(8):
            if r == q or g == h: continue
            if r in (q2, q3):
                if g == h2: late(rng, d, r, g)
                elif r == q3: early(rng, d, r, g, room.pop())
                continue
            c = np.unique(d["nb"][r, g, st]); c = np.setdiff1d(c[c < V], np.concatenate([st, d["bx"][r, g]]))
            p = rng.permutation(c)[:2 * int(rng.integers(1, 4))]
            d["m"][r, g, p] = d["m"][r, g, p.reshape(-1, 2)[:, ::-1].reshape(-1)]
    return pack(d)
def setup_inputs_spread(rng):
    z = (np.exp2(8 * rng.random((N, 8, 1, V))) * rng.random((N, 8, 16, V)) * (rng.random((N, 8, 1, V)) > 0.0625)).astype(np.int64)
    wild = rng.choice(np.array([0.05, 0.3, 1.0]), (N, 8, 1, 1)); mix = rng.choice(np.array([0.2, 0.5, 1.0]), (N, 8))
    for h in rng.permutation(8)[:2]:
        u = rng.integers(0, 4, (N, 16, V)); z[:, h] = np.where(rng.random((N, 1, V)) < 0.5, u, 255 - u); wild[:, h] = 1.0; mix[:, h] = 1.0
    return pack(parts(rng, z, wild, mix))
def check_inputs(d):
    bad = []
    for k in ("x", "z"):
        a = np.asarray(d[k]).astype(np.float32)
        if not np.all((a >= 0) & (a <= 255) & (a == np.floor(a))): bad.append("whole numbers 0 to 255 in " + k)
    for k, hi in (("nb", W - 1), ("nz", W - 1), ("m", V - 1), ("im", V - 1), ("bx", V - 1), ("bz", V - 1)):
        if np.min(d[k]) < 0 or np.max(d[k]) > hi: bad.append("range of " + k)
    if not np.all(np.sort(d["m"], axis=-1) == np.arange(V)): bad.append("m is a bijection")
    elif not np.all(np.argsort(d["m"], axis=-1) == d["im"]): bad.append("im is the inverse of m")
    return bad
def reference(x, z, nb, nz, m, im, bx, bz):
    X = x.astype(np.float32).astype(np.int64).reshape(N, 8, 16, V); Z = z.astype(np.float32).astype(np.int64).reshape(N, 8, 16, V)
    nv = np.stack([gentries(a) for a in nb]).astype(np.int64).reshape(N, 8, V, 16); ns = np.stack([gentries(a) for a in nz]).astype(np.int64).reshape(N, 8, V, 16)
    M = m.astype(np.int64); I = im.astype(np.int64)
    b1 = np.stack([gentries(a) for a in bx]).astype(np.int64); b2 = np.stack([gentries(a) for a in bz]).astype(np.int64)
    lane = np.arange(L); v = np.tile(lane * (V // L), (N, 8, 1)); last = np.zeros(N, np.int64)
    for rnd in range(RO):
        Y = np.take_along_axis(Z, M[:, :, None, :], 3)
        ey = np.take_along_axis(Y, b1[:, :, None, :], 3); ez = np.take_along_axis(Z, b2[:, :, None, :], 3)
        YW = np.concatenate([Y] + [np.roll(ey, -d, axis=0) for d in range(1, B + 1)], axis=3)
        ZW = np.concatenate([Z] + [np.roll(ez, -d, axis=0) for d in range(1, B + 1)], axis=3)
        th = last & 31; last = np.zeros(N, np.int64)
        for r in range(N):
            for g in range(8):
                Yg, Zg, n1, n2, at = YW[r, g], ZW[r, g], nv[r, g], ns[r, g], v[r, g].copy()
                na = n1[at]; nq = n2[M[r, g, at]]
                D = np.add.reduce(np.abs(Yg[:, na] - Zg[:, nq]), axis=0); k = np.argmax(D, axis=1)
                a = na[lane, k]; q = nq[lane, k]; live = (D[lane, k] > 0) & (a < V) & (q < V)
                ac = np.minimum(a, V - 1); qc = np.minimum(q, V - 1); w = I[r, g, qc]; p = M[r, g, ac]
                Aa = Yg[:, n1[ac]]; Aw = Yg[:, n1[w]]; Ba = Zg[:, n2[p]]; Bw = Zg[:, n2[qc]]
                gain = np.add.reduce(np.abs(Aa - Ba) + np.abs(Aw - Bw) - np.abs(Aa - Bw) - np.abs(Aw - Ba), axis=(0, 2))
                prop = live & (gain > th[r])
                first = np.full(V, L); np.minimum.at(first, ac[prop], lane[prop]); np.minimum.at(first, w[prop], lane[prop])
                com = prop & (first[ac] >= lane) & (first[w] >= lane)
                last[r] += np.count_nonzero(com)
                v[r, g] = np.where(com, a, np.where(q < V, w, (5 * at + 1) & (V - 1)))
                a, w, p, q = a[com], w[com], p[com], q[com]
                M[r, g, a] = q; M[r, g, w] = p; I[r, g, q] = a; I[r, g, p] = w
                for vert, site in ((a, q), (w, p)):
                    old = Z[r, g][:, site]; Z[r, g][:, site] = old + np.clip(X[r, g][:, vert] - old, -1, 1)
    return {"mo": M.astype(np.float32), "zo": Z.reshape(N, 128, V).astype(np.float32).astype(BF)}

@@ -1,0 +1,503 @@
+from concourse.mybir import AluOpType as Op, AxisListType, ActivationFunctionType as Fn
+
+V, NB, L, RO = 2048, 256, 128, 3
+WIN = NB + V + NB
+CH = [(0, 32), (32, 64), (64, 96), (96, 128)]
+SCH = [(64, 96), (96, 128)]
+VCH = [(0, 32), (32, 64)]
+DS = [(48, 64), (64, 112), (112, 128)]
+DV = [(0, 32), (32, 48)]
+DCH = [(0, 32), (32, 64), (64, 96), (96, 112)]
+DY = (112, 128)
+DP = 64
+WD = 510.0
+PASS = float(2 ** 40)
+FAR = 1.0e6
+
+_B, _F, _H, _I, _U = "bfloat16", "float32", "float16", "int32", "uint16"
+SCRATCH = {}
+for _n, _w, _t in [
+    ("nbt", V, _I), ("nzt", V, _I), ("xt", V, _B),
+    ("z1", WIN, _B), ("z2", WIN, _B), ("z3", WIN, _B), ("y1", WIN, _B), ("y2", WIN, _B), ("y3", WIN, _B),
+    ("mt", NB + V, _F), ("it", NB + V, _F),
+    ("ml32", 128, _I), ("mlh", 128, _H), ("mlt", 128, _H), ("mlist", 128, _U),
+    ("m2", 128, _I), ("i2", 128, _I), ("m2h", 128, _H), ("i2h", 128, _H),
+    ("bx32", 16, _I), ("bz32", 16, _I), ("bxl", 16, _U), ("bzl", 16, _U),
+    ("gz", NB, _B), ("gy", NB, _B),
+    ("ones", 128, _B), ("idn", 128, _B), ("idm", 128, _B), ("bo8", 8, _B), ("gp", 8, _B), ("g1", 8, _B), ("gm", 8, _B),
+    ("fk", 2048, _B), ("au", 512, _B), ("auq", 256, _B), ("ej", 2048, _B),
+    ("bq0", 128, _B), ("bq", 128, _B), ("lj", 16, _F), ("lk", 16, _F),
+    ("tb0", 128, _B), ("tb", 128, _B), ("w1k", 1024, _B), ("dw", 1024, _B),
+    ("ms0", 72, _F), ("ms1", 72, _F), ("ms", 72, _F), ("c0", 128, _F), ("c1", 128, _F),
+    ("pi", 8, _I), ("pi2", 8, _I), ("pf", 8, _F), ("li", 16, _F), ("alt", 40, _F),
+    ("vl", 8, _U), ("vf", 8, _F), ("mvr", 128, _H), ("mvt", 128, _H), ("mvl", 8, _U),
+    ("nbv", 128, _U), ("nzv", 128, _U), ("cat", 256, _H), ("catt", 256, _H),
+    ("zg", 2048, _B), ("dd", 2048, _B), ("rr", 2048, _B),
+    ("db", 128, _F), ("old", 128, _H), ("s0", 256, _H), ("sc", 256, _H), ("sct", 256, _H),
+    ("l4", 32, _U), ("l4f", 32, _F), ("wp", 256, _H), ("wpt", 256, _H), ("raq", 256, _F), ("nm", 256, _H),
+    ("nba", 128, _U), ("nzq", 128, _U), ("nbw", 128, _U), ("nzp", 128, _U),
+    ("ga", 2048, _B), ("gw", 2048, _B), ("gb", 2048, _B),
+    ("m_1", 2048, _B), ("m_2", 2048, _B), ("m_3", 2048, _B), ("m_4", 2048, _B),
+    ("ka", 2048, _B), ("kw", 2048, _B), ("tc", 1024, _B), ("tk", 1024, _B),
+    ("xg", 256, _B), ("zd", 256, _B), ("zc", 256, _B), ("zn", 256, _B),
+    ("lv0", 8, _F), ("lv1", 8, _F), ("lv2", 8, _F), ("lv", 8, _B), ("thl", 8, _F), ("thm", 8, _F), ("thn", 8, _F), ("prop", 16, _B),
+    ("t6", 8, _F), ("sel", 72, _F), ("com", 40, _F), ("cm", 40, _F), ("off", 32, _U), ("n5", 40, _F), ("dl", 40, _F),
+    ("sv", 8, _I), ("sv2", 8, _I), ("qo", 8, _F), ("dws", 8, _F), ("dwq", 8, _F), ("cb", 8, _B),
+    ("cn", 8, _F), ("cni", 8, _I), ("cnj", 8, _I),
+]:
+    SCRATCH[_n] = ("sbuf", [128, _w], _t)
+for _n in ["p_a", "p_b", "p_d", "p_g", "p_l", "p_q", "p_t0", "p_t1"]:
+    SCRATCH[_n] = ("psum", [128, 512], "float32")
+
+DMAS = ["d_ml", "d_z", "d_bz", "d_bx", "d_m2", "d_i2", "d_nb", "d_nz", "d_x", "d_z2", "d_y2", "d_z3", "d_y3", "d_mo", "d_zo"]
+SEMAPHORES = ["V", "S", "P", "G"] + DMAS + ["%s%s%d" % (k, w, t) for k in ("arr", "snt") for w in ("z", "y") for t in (1, 2, 3)]
+
+
+def rank_program(g, core, T, topo):
+    rank = T.rank_of(core)
+    if rank is None:
+        return
+    n = len(T.cores)
+    dst = T.cores[(rank - 1) % n]
+    rid, pid = topo.addr(dst)[:2]
+    nout = len(topo.engines(core, dst))
+    nin = len(topo.engines(T.cores[(rank + 1) % n], core))
+
+    Q = {"V": g.vector, "S": g.scalar, "P": g.tensor, "G": g, "Y": g.sync}
+    count = {"V": 0, "S": 0, "P": 0, "G": 0}
+    known = {q: {} for q in Q}
+    clock = {}
+    acc = {}
+
+    def psum(name):
+        return name[:2] == "p_"
+
+    def meet(r1, r2):
+        if r1[1] >= r2[2] or r2[1] >= r1[2] or r1[3] >= r2[4] or r2[3] >= r1[4]:
+            return False
+        s = r1[5]
+        return not (s == r2[5] and s > 1 and (r1[3] - r2[3]) % s)
+
+    def order(q, reads, writes, me):
+        need = {}
+        for kind, regs in (("r", reads), ("w", writes)):
+            for r in regs:
+                for (e, k2, r2), idx in acc.get(r[0], {}).items():
+                    same = e == q
+                    if same and (q == "P" or k2 == "r"):
+                        continue
+                    if same or not psum(r[0]):
+                        if (kind == "r" and k2 == "r") or not meet(r, r2):
+                            continue
+                    if need.get(e, 0) < idx:
+                        need[e] = idx
+        kn = known[q]
+        for e in sorted(need, key=lambda e: -len(clock.get((e, need[e]), {}))):
+            if kn.get(e, 0) >= need[e]:
+                continue
+            Q[q].wait_ge(T.sem[e], need[e])
+            for e2, i2 in clock.get((e, need[e]), {}).items():
+                if kn.get(e2, 0) < i2:
+                    kn[e2] = i2
+            kn[e] = max(kn.get(e, 0), need[e])
+        e, idx = me
+        clock[(e, idx)] = dict(kn)
+        for kind, regs in (("r", reads), ("w", writes)):
+            for r in regs:
+                a = acc.setdefault(r[0], {})
+                if kind == "w" and r[5] == 1 and not psum(r[0]):
+                    for key in [k for k in a if k[2][1] >= r[1] and k[2][2] <= r[2] and k[2][3] >= r[3] and k[2][4] <= r[4] and k[0] != e]:
+                        if kn.get(key[0], 0) >= a[key]:
+                            del a[key]
+                a[(e, kind, r)] = idx
+
+    def R(name, c0=0, c1=None, step=1, p0=0, p1=128):
+        return (name, p0, p1, c0, SCRATCH[name][1][1] if c1 is None else c1, step)
+
+    def ap(r):
+        if r[0] == "ind":
+            return ap(r[1]).indirect(ap(r[2]))
+        t = T[r[0]]
+        return t[r[1]:r[2], r[3]:r[4]] if r[5] == 1 else t[r[1]:r[2], r[3]:r[4]:r[5]]
+
+    def ind(w, o):
+        return ("ind", w, o)
+
+    def split(outs, ins):
+        rd, wr = [], []
+        for r in outs:
+            if r[0] == "ind":
+                wr.append(r[1])
+                rd.append(r[2])
+            else:
+                wr.append(r)
+        for r in ins:
+            if r[0] == "ind":
+                rd += [r[1], r[2]]
+            else:
+                rd.append(r)
+        return rd, wr
+
+    def run(q, outs, ins, call):
+        rd, wr = split(outs, ins)
+        count[q] += 1
+        order(q, rd, wr, (q, count[q]))
+        call(Q[q]).then_inc(T.sem[q], 1)
+
+    def val(s):
+        return ap(s) if isinstance(s, tuple) else s
+
+    def tc(o, i):
+        run("V", [o], [i], lambda q: q.tensor_copy(ap(o), ap(i)))
+
+    def tt(o, a, b, op):
+        run("V", [o], [a, b], lambda q: q.tensor_tensor(ap(o), ap(a), ap(b), op))
+
+    def ts(o, i, s1, op0, s2=None, op1=None):
+        ins = [i] + [s for s in (s1, s2) if isinstance(s, tuple)]
+        if op1 is None:
+            run("V", [o], ins, lambda q: q.tensor_scalar(ap(o), ap(i), val(s1), None, op0))
+        else:
+            run("V", [o], ins, lambda q: q.tensor_scalar(ap(o), ap(i), val(s1), val(s2), op0, op1))
+
+    def scan(o, a, b, op0, op1):
+        run("V", [o], [a, b], lambda q: q.tensor_tensor_scan(ap(o), ap(a), ap(b), 0.0, op0, op1))
+
+    def tr(o, i):
+        run("V", [o], [i], lambda q: q.transpose(ap(o), ap(i)))
+
+    def ms(o, c):
+        run("V", [o], [], lambda q: q.memset(ap(o), c))
+
+    def act(o, i, scale=1.0, fn=Fn.Copy):
+        run("S", [o], [i], lambda q: q.activation(ap(o), ap(i), fn, 0.0, scale))
+
+    def mm(o, a, b, start=True, stop=True):
+        run("P", [o], [a, b], lambda q: q.matmul(ap(o), ap(a), ap(b), start, stop))
+
+    def iota(o, pat, base, cmul, flag=True):
+        if flag:
+            run("G", [o], [], lambda q: q.iota(ap(o), pat, base, cmul, allow_small_or_imprecise_dtypes=True))
+        else:
+            run("G", [o], [], lambda q: q.iota(ap(o), pat, base, cmul))
+
+    def aff(o, i, pat, op, fill, base, cmul):
+        run("G", [o], [i], lambda q: q.affine_select(ap(o), ap(i), pat, op, fill, base, cmul))
+
+    def dma(q, sem, pairs, total=None):
+        tot = 16 * (total or len(pairs))
+        for o, i in pairs:
+            rd, wr = split([o] if isinstance(o, tuple) else [], [i] if isinstance(i, tuple) else [])
+            order(q, rd, wr, (sem, tot))
+            Q[q].dma_start(val(o), val(i)).then_inc(T.sem[sem], 16)
+        count[sem] = tot
+
+    def send(w, t, src):
+        win = "%s%d" % (w, t)
+        snt, arr = "snt" + win, "arr" + win
+        order("G", [src], [], (snt, nout))
+        g.remote_dma(T[win][:, NB + V:WIN], ap(src), T.sem[arr], T.sem[snt], pid, rid, topo.mask(core, dst))
+        count[snt], count[arr] = nout, nin
+        acc.setdefault(win, {})[(arr, "w", R(win, NB + V, WIN))] = nin
+        clock[(arr, nin)] = {}
+
+    def own(name):
+        return R(name, NB, NB + V)
+
+    def full(name):
+        return R(name, NB, WIN)
+
+    def park(name):
+        return R(name, 0, NB + V)
+
+    pieces = [(R("ml32", 32 * c + 16 * h, 32 * c + 16 * h + 16), T.m[h::2, 512 * c:512 * c + 512]) for c in range(4) for h in range(2)]
+    dma("Y", "d_ml", pieces[:4], 8)
+    dma("S", "d_ml", pieces[4:], 8)
+    dma("S", "d_bz", [(R("bz32"), T.bz[:, :])])
+    dma("Y", "d_m2", [(R("m2"), T.m[:, :])])
+    dma("S", "d_z", [(own("z1"), T.z[:, :])])
+    dma("Y", "d_bx", [(R("bx32"), T.bx[:, :])])
+    dma("Y", "d_nz", [(R("nzt"), T.nz[:, :])])
+    dma("S", "d_nb", [(R("nbt"), T.nb[:, :])])
+    dma("Y", "d_i2", [(R("i2"), T.im[:, :])])
+    dma("Y", "d_x", [(R("xt"), T.x[:, :])])
+
+    ms(R("ones"), 1.0)
+    aff(R("bo8"), R("ones", 0, 8), [[-16, 8]], Op.is_ge, 0.0, 0, 1)
+    aff(R("g1"), R("bo8"), [[16, 8]], Op.is_ge, 0.0, 15, -1)
+    iota(R("pi"), [[0, 8]], 0, 1, False)
+    iota(R("li"), [[128, 2], [16, 8]], 0, 0)
+    iota(R("lj"), [[1, 16]], 0, 0)
+    aff(R("bq0"), R("ones"), [[-16, 8], [0, 16]], Op.is_ge, 0.0, 0, 1)
+    aff(R("bq"), R("bq0"), [[16, 8], [0, 16]], Op.is_ge, 0.0, 15, -1)
+    for u in range(2):
+        aff(R("auq", 128 * u, 128 * u + 128), R("ones"), [[-32, 4], [0, 2], [-1, 16]], Op.is_equal, 0.0, -16 * u, 1)
+        for h in range(2):
+            k = 128 * (2 * u + h)
+            aff(R("au", k, k + 128), R("auq", 128 * u, 128 * u + 128), [[0, 4], [1, 2], [0, 16]], Op.is_equal, 0.0, -h, 0)
+    iota(R("tb0"), [[0, 8], [-1, 16]], 15, 0)
+    ms(R("fk"), 0.0)
+    ts(R("pi2"), R("pi"), 15, Op.bitwise_and)
+    tc(R("pf"), R("pi2"))
+    ts(R("alt", 0, 16), R("li"), R("pf", 0, 1), Op.add)
+    ts(R("alt", 16, 32), R("li"), R("pf", 0, 1), Op.add)
+    ts(R("vf"), R("alt", 0, 8), 16.0, Op.mult)
+    tc(R("vl"), R("vf"))
+    ts(R("lk"), R("lj"), R("pf", 0, 1), Op.is_equal)
+    ts(R("gp"), R("g1"), 2.0, Op.mult)
+    ts(R("gm"), R("g1"), -2.0, Op.mult)
+    for k in range(16):
+        act(R("fk", 128 * k + k, 128 * k + 128, 16), R("g1"))
+    for k in range(16):
+        ts(R("ej", 128 * k, 128 * k + 128), R("bq"), R("lk", k, k + 1), Op.mult)
+    tc(R("mlh"), R("ml32"))
+    tr(R("mlt"), R("mlh"))
+    tc(R("mlist"), R("mlt"))
+    tc(R("bzl"), R("bz32"))
+    tc(R("bxl"), R("bx32"))
+    tc(R("m2h"), R("m2"))
+    act(R("gz"), ind(own("z1"), R("bzl")))
+    send("z", 1, R("gz"))
+    tc(R("y1", NB, NB + 1024), ind(own("z1"), R("mlist", 0, 64)))
+    act(R("y1", NB + 1024, NB + V), ind(own("z1"), R("mlist", 64, 128)))
+    act(R("gy"), ind(own("y1"), R("bxl")))
+    send("y", 1, R("gy"))
+    dma("Y", "d_z2", [(own("z2"), own("z1"))])
+    dma("Y", "d_y2", [(own("y2"), own("y1"))])
+
+    ts(R("tb"), R("tb0"), 1.0 / 2048, Op.mult)
+    ms(R("c0"), FAR)
+    aff(R("c1"), R("c0"), [[0, 8], [1, 16]], Op.not_equal, -1.0, 0, 0)
+    ms(R("w1k"), WD)
+    ms(R("ms0"), PASS)
+    ms(R("t6"), FAR)
+    aff(R("idn"), R("ones"), [[-1, 128]], Op.is_equal, 0.0, 0, 1)
+    aff(R("ms1"), R("ms0"), [[0, 8], [-16, 9]], Op.is_ge, 1.0, 16, 1)
+    aff(R("ms"), R("ms1"), [[0, 8], [16, 9]], Op.is_ge, 0.0, -1, -1)
+    aff(R("dw"), R("w1k"), [[-16, 8], [0, 8], [-1, 16]], Op.is_equal, 0.0, 0, 1)
+
+    def spread(half, tab):
+        for jb in range(4):
+            b = ("p_a", "p_b")[jb % 2]
+            for j in range(4):
+                J = 4 * jb + j
+                mm(R(b, 128 * j, 128 * j + 128), R("ej", 128 * J, 128 * J + 128), R(half))
+            act(R(tab, NB + 512 * jb, NB + 512 * jb + 512), R(b))
+
+    spread("m2h", "mt")
+
+    def lists(base, nx, src, at):
+        for u in range(2):
+            for h in range(2):
+                k = 128 * (2 * u + h)
+                mm(R("p_l", base + u, base + 8 * nx, 2), R("au", k, k + 128), R(src, 16 * h + at, 128 * nx, 32), h == 0, h == 1)
+
+    def cols(ln):
+        return 16 * ln[0], 16 * ln[1]
+
+    for t in range(1, RO + 1):
+        Y, Z = "y%d" % t, "z%d" % t
+        Yn, Zn = ("y%d" % (t + 1), "z%d" % (t + 1)) if t < RO else (Y, Z)
+        tc(R("mvr"), ind(own("mt"), R("vl")))
+        tr(R("mvt"), R("mvr"))
+        lists(0, 1, "mvt", 0)
+        if t > 1:
+            tc(R("nbv"), ind(R("nbt"), R("vl")))
+        tc(R("mvl"), R("p_l", 0, 8))
+        tc(R("nzv"), ind(R("nzt"), R("mvl")))
+        if t == 1:
+            ms(R("prop"), 0.0)
+            ts(R("idm"), R("idn"), -1.0, Op.mult)
+            tc(R("i2h"), R("i2"))
+            tc(R("nbv"), ind(R("nbt"), R("vl")))
+        ts(R("cat", 0, 128), R("nbv"), 2048.0, Op.min)
+        ts(R("cat", 128, 256), R("nzv"), 2048.0, Op.min)
+        tr(R("catt"), R("cat"))
+        for ln in DS:
+            act(R("zg", *cols(ln)), ind(full(Z), R("nzv", *ln)))
+        for ln in DV:
+            tc(R("zg", *cols(ln)), ind(full(Z), R("nzv", *ln)))
+        act(R("dd", *cols(DY)), ind(full(Y), R("nbv", *DY)))
+        yz = R("p_a", 0, 16 * (DY[1] - DY[0]))
+        mm(yz, R("idn"), R("dd", *cols(DY)), True, False)
+        mm(yz, R("idm"), R("zg", *cols(DY)), False, True)
+
+        def sums(e):
+            o = R("p_d", DP * e, DP * e + DP)
+            mm(o, R("tb"), R("ones", 0, DP), True, False)
+            for k in range(16):
+                mm(o, R("fk", 128 * k, 128 * k + 128), R("rr", 16 * DP * e + k, 16 * DP * (e + 1), 16), False, k == 15)
+
+        for x, ln in enumerate(DCH):
+            tt(R("dd", *cols(ln)), ind(full(Y), R("nbv", *ln)), R("zg", *cols(ln)), Op.subtract)
+            act(R("rr", *cols(ln)), R("dd", *cols(ln)), 1.0, Fn.Abs)
+            if x == 0:
+                act(R("rr", *cols(DY)), yz, 1.0, Fn.Abs)
+            if ln[1] == DP:
+                sums(0)
+        sums(1)
+        if t > 1:
+            tc(ind(park("it"), R("off", 0, 8)), R("raq", 0, 128))
+            tc(ind(park("it"), R("off", 8, 16)), R("wp", 0, 128))
+            tc(R("cb"), R("com", 0, 8))
+            mm(R("p_l", 80, 88), R("ones"), R("cb"))
+            run("V", [R("cn", 0, 1)], [R("p_l", 80, 88)],
+                lambda q: q.tensor_reduce(ap(R("cn", 0, 1)), ap(R("p_l", 80, 88)), AxisListType.X, Op.add))
+            tc(R("cni", 0, 1), R("cn", 0, 1))
+            ts(R("cnj", 0, 1), R("cni", 0, 1), 31, Op.bitwise_and)
+            ts(R("t6", 0, 1), R("cnj", 0, 1), FAR, Op.add)
+        else:
+            spread("i2h", "it")
+            ms(R("ka"), 0.0)
+            ms(R("kw"), 0.0)
+        tr(R("db"), R("p_d", 0, 128))
+        scan(R("p_q", 0, 128), R("c1"), R("db"), Op.min, Op.max)
+        tt(R("p_q", 128, 256), R("p_q", 0, 128), R("db"), Op.is_equal)
+        tt(R("old"), R("p_q", 0, 128), R("db"), Op.is_gt)
+        tt(R("s0", 0, 128), R("p_q", 128, 256), R("catt", 0, 128), Op.mult)
+        tt(R("s0", 128, 256), R("p_q", 128, 256), R("catt", 128, 256), Op.mult)
+        scan(R("sc", 0, 128), R("old"), R("s0", 0, 128), Op.mult, Op.add)
+        scan(R("sc", 128, 256), R("old"), R("s0", 128, 256), Op.mult, Op.add)
+        lists(16, 2, "sc", 15)
+        ts(R("l4", 0, 8), R("p_l", 16, 24), 2047.0, Op.min)
+        ts(R("l4", 16, 24), R("p_l", 24, 32), 2047.0, Op.min)
+        tc(R("nba"), ind(R("nbt"), R("l4", 0, 8)))
+        tc(R("wp", 0, 128), ind(own("it"), R("l4", 16, 24)))
+        tc(R("wp", 128, 256), ind(own("mt"), R("l4", 0, 8)))
+        tr(R("wpt"), R("wp"))
+        lists(32, 2, "wpt", 0)
+        tc(R("nzq"), ind(R("nzt"), R("l4", 16, 24)))
+        tr(R("sct"), R("sc"))
+        mm(R("p_d", 128, 384), R("ej", 128 * 15, 2048), R("sct"))
+        tc(R("l4", 8, 16), R("p_l", 32, 40))
+        tc(R("l4", 24, 32), R("p_l", 40, 48))
+        tc(R("nbw"), ind(R("nbt"), R("l4", 8, 16)))
+        tc(R("nzp"), ind(R("nzt"), R("l4", 24, 32)))
+
+        def fetch(o, win, lst, ln):
+            act(R(o, *cols(ln)), ind(full(win), R(lst, *ln)))
+
+        def fused(mx, src, ln):
+            tt(R(mx, *cols(ln)), ind(full(Z), R("nzq", *ln)), R(src, *cols(ln)), Op.max)
+
+        def gain(terms, o):
+            for x, (mx, wgt) in enumerate(terms):
+                for k in range(16):
+                    mm(o, R(mx, k, 2048, 16), R(wgt), x == 0 and k == 0, x == len(terms) - 1 and k == 15)
+
+        for ln in CH[:2]:
+            fetch("ga", Y, "nba", ln)
+        act(R("raq"), R("p_d", 128, 384))
+        for ln in CH[2:]:
+            fetch("ga", Y, "nba", ln)
+        for ln in CH:
+            fused("m_1", "ga", ln)
+        gain([("m_1", "gm")], R("p_g", 0, 8))
+        fetch("gw", Y, "nbw", CH[0])
+        act(R("xg"), ind(R("xt"), R("l4", 0, 16)))
+        for ln in CH[1:]:
+            fetch("gw", Y, "nbw", ln)
+        ts(R("l4f", 0, 8), R("p_l", 16, 24), 2047.0, Op.min)
+        ts(R("l4f", 16, 24), R("p_l", 24, 32), 2047.0, Op.min)
+        ts(R("qo"), R("p_l", 24, 32), 2048.0, Op.is_lt)
+        tc(R("l4f", 8, 16), R("p_l", 32, 40))
+        tc(R("l4f", 24, 32), R("p_l", 40, 48))
+        tc(R("nm", 0, 256, 2), R("raq", 0, 128))
+        tc(R("nm", 1, 256, 2), R("wp", 0, 128))
+        for c in range(8):
+            wd = 32 * (c + 1)
+            for kk, s in (("ka", c), ("kw", 8 + c)):
+                ts(R(kk, 256 * c, 256 * c + wd), R("nm", 0, wd), R("l4f", s, s + 1), Op.is_equal)
+            o = R("p_t%d" % (c // 4), 128 * (c % 4), 128 * (c % 4) + 128)
+            mm(o, R("idn"), R("dw", 128 * c, 128 * c + 128), True, False)
+            for x, (kk, y) in enumerate((("ka", 0), ("ka", 1), ("kw", 0), ("kw", 1))):
+                mm(o, R(kk, 256 * c + y, 256 * c + 256, 2), R("idn"), False, x == 3)
+        tt(R("lv0"), R("sc", 15, 128, 16), R("sc", 128 + 15, 256, 16), Op.max)
+        ts(R("lv1"), R("lv0"), 2048.0, Op.is_lt)
+        ts(R("lv2"), R("p_q", 15, 128, 16), 1.0, Op.is_ge)
+        tt(R("lv"), R("lv1"), R("lv2"), Op.mult)
+        for e in range(4):
+            for b in range(4):
+                mm(R("p_l", 64 + 2 * b, 66 + 2 * b, 1, 32 * e, 32 * e + 32), R("idn", 32 * b, 32 * b + 32), R("lv", 2 * e, 2 * e + 2))
+        for ln in CH[2:]:
+            fetch("gb", Z, "nzp", ln)
+        for x in range(2):
+            act(R("tc", 512 * x, 512 * x + 512), R("p_t%d" % x))
+        aff(R("tk"), R("tc"), [[16, 8], [0, 8], [1, 16]], Op.is_ge, 0.0, 0, -1)
+        for ln in CH[:2]:
+            fetch("gb", Z, "nzp", ln)
+        fused("m_2", "gw", CH[0])
+        if t < RO:
+            ts(R("sv"), R("vf"), 5.0, Op.mult, 1.0, Op.add)
+            ts(R("sv2"), R("sv"), 2047, Op.bitwise_and)
+            tt(R("dws"), R("l4f", 8, 16), R("sv2"), Op.subtract)
+            tt(R("dwq"), R("dws"), R("qo"), Op.mult)
+            tt(R("alt", 32, 40), R("dwq"), R("sv2"), Op.add)
+            tc(R("n5", 32, 40), R("l4f", 0, 8))
+        ts(R("n5", 0, 16), R("l4f", 16, 32), float(NB), Op.add)
+        ts(R("n5", 16, 32), R("l4f", 0, 16), float(NB), Op.add)
+        wide = 40 if t < RO else 32
+        tt(R("dl", 0, wide), R("n5", 0, wide), R("alt", 0, wide), Op.subtract)
+        ts(R("thl"), R("p_l", 64, 72), -FAR, Op.mult, R("t6", 0, 1), Op.add)
+        qp = R("l4", 16, 32)
+        tt(R("zd"), ind(own(Z), qp), R("xg"), Op.subtract)
+        for ln in CH[1:]:
+            fused("m_2", "gw", ln)
+        ts(R("zc"), R("zd"), -1.0, Op.max, 1.0, Op.min)
+        tt(R("zn"), ind(own(Z), qp), R("zc"), Op.subtract)
+        sb = ["p_t0", "p_t1", "p_b"]
+        uses = [0]
+
+        def on_s(ln):
+            for mx, src in (("m_3", "ga"), ("m_4", "gw")):
+                b = R(sb[uses[0] % 3], 0, 16 * (ln[1] - ln[0]))
+                uses[0] += 1
+                mm(b, R("idn"), R(src, *cols(ln)), True, False)
+                mm(b, R("idm"), R("gb", *cols(ln)), False, True)
+                act(R(mx, *cols(ln)), b, 1.0, Fn.Relu)
+
+        def on_v(ln, b):
+            b = R(b, 0, 16 * (ln[1] - ln[0]))
+            mm(b, R("idn"), R("gb", *cols(ln)))
+            tt(R("m_3", *cols(ln)), b, R("ga", *cols(ln)), Op.max)
+            tt(R("m_4", *cols(ln)), b, R("gw", *cols(ln)), Op.max)
+
+        on_s(SCH[0])
+        on_v(VCH[0], "p_a")
+        on_s(SCH[1])
+        on_v(VCH[1], "p_q")
+        gain([("m_2", "gp")], R("p_g", 8, 16))
+        tt(R("thm"), R("thl"), R("p_g", 0, 8), Op.subtract)
+        tt(R("thn"), R("thm"), R("p_g", 8, 16), Op.subtract)
+        gain([("m_3", "gp"), ("m_4", "gm")], R("p_d", 400, 408))
+        tt(R("prop", 1, 9), R("p_d", 400, 408), R("thn"), Op.is_gt)
+        for c in range(8):
+            mm(R("p_d", 9 * c, 9 * c + 9), R("tk", 128 * c, 128 * c + 128), R("prop", 0, 9))
+        scan(R("sel"), R("p_d", 0, 72), R("ms"), Op.max, Op.mult)
+        for x in range(wide // 8):
+            ts(R("com", 8 * x, 8 * x + 8), R("sel", 8, 72, 9), (WD + 2) * PASS, Op.is_equal)
+        tt(R("cm", 0, wide), R("com", 0, wide), R("dl", 0, wide), Op.mult)
+        tt(R("off"), R("cm", 0, 32), R("alt", 0, 32), Op.add)
+        tc(ind(park(Zn), R("off", 0, 16)), R("zn"))
+        if t < RO:
+            act(R("gz"), ind(own(Zn), R("bzl")))
+            send("z", t + 1, R("gz"))
+            tc(ind(park(Yn), R("off", 16, 32)), R("zn"))
+            act(R("gy"), ind(own(Yn), R("bxl")))
+            send("y", t + 1, R("gy"))
+            tt(R("vl"), R("cm", 32, 40), R("alt", 32, 40), Op.add)
+            tt(R("vf"), R("cm", 32, 40), R("alt", 32, 40), Op.add)
+        else:
+            dma("Y", "d_zo", [(T.zo[:, :], own(Zn))])
+        tc(ind(park("mt"), R("off", 16, 24)), R("raq", 128, 256))
+        tc(ind(park("mt"), R("off", 24, 32)), R("wp", 128, 256))
+        if t == 1:
+            dma("Y", "d_z3", [(own("z3"), own("z2"))])
+            dma("Y", "d_y3", [(own("y3"), own("y2"))])
+    order("Y", [own("mt")], [], ("d_mo", 16))
+    g.sync.dma_start(T.mo[:, :], T.mt[0:128:16, NB:NB + V]).then_inc(T.sem["d_mo"], 16)
+    count["d_mo"] = 16
+
+    for e in sorted(count):
+        if known["G"].get(e, 0) < count[e]:
+            g.wait_ge(T.sem[e], count[e])

@@ -2,55 +2,77 @@ from concourse.mybir import AluOpType as Op, AxisListType, ActivationFunctionTyp
 
 V, NB, L, RO = 2048, 256, 128, 3
 WIN = NB + V + NB
-CH = [(0, 32), (32, 64), (64, 96), (96, 128)]
-SCH = [(64, 96), (96, 128)]
-VCH = [(0, 32), (32, 64)]
-DS = [(48, 64), (64, 112), (112, 128)]
-DV = [(0, 32), (32, 48)]
-DCH = [(0, 32), (32, 64), (64, 96), (96, 112)]
-DY = (112, 128)
-DP = 64
-WD = 510.0
-PASS = float(2 ** 40)
-FAR = 1.0e6
+PAD = 16
+KEY = 65536.0
+BIG = 4096.0
+EPS = 2.0 ** -20
+FAR = 2.0 ** 20
+
+NAMING1 = {
+    "V": "mv mvl i2h|Z 64 128|im1 0 4|nbv1 0 64|Y 32 64|nbv1 64 128|im1 8 12|Y 96 128|Y 64 96|cat|max 96 128|next",
+    "S": "nzv|Z 0 64|im1 4 8|Y 0 32|abs 0 32|abs 32 64|abs 64 96|im1 12 16",
+    "P": "rank|imP 0 4|imP 4 8|imP 8 12|imP 12 16|zP 96 128|sumz 96 128|diff 0 32|diff 32 64|sum 0 32|sum 32 64|sumy 96 128|diff 64 96|catT|"
+         "summ 96 128|sum 64 96",
+}
+NAMING = {
+    "V": "mv mvl im cat|Z 64 128|Y 32 64|Y 64 96|Y 96 128|max 96 128|next th",
+    "S": "nbv nzv|Z 0 64|Y 0 32|abs 0 32|abs 32 64|abs 64 96",
+    "P": "count catT rank|zP 96 128|sumz 96 128|diff 0 32|diff 32 64|diff 64 96|sum 0 32|sum 32 64|sumy 96 128|sum 64 96|summ 96 128",
+}
+GAINS = {
+    "V": "w wl names p same pl|f1 0 32|qp|f1 32 64|f1 64 128|f3 0 64|f2 64 128|f2 0 32|f4 0 32|f4 32 64|f2 32 64|alt|prop 0 128",
+    "S": "nba a|A 0 32|nzq|A 32 64|nbw|A 64 128|nzp|B 64 128|W 64 128|tc0|W 0 32|r3 64 96|r3 96 128|W 32 64|tc1|r4 64 96|r4 96 128|"
+         "x zq places sign",
+    "P": "void sameT zero|d3 64 96|d3 96 128|g1 0 128|d4 64 96|d4 96 128|g3 0 128|g4 0 128|g2 0 128 stop|dz|lower 0 128",
+    "G": "mask0 mask1",
+}
 
 _B, _F, _H, _I, _U = "bfloat16", "float32", "float16", "int32", "uint16"
 SCRATCH = {}
 for _n, _w, _t in [
-    ("nbt", V, _I), ("nzt", V, _I), ("xt", V, _B),
+    ("nbt", V + PAD, _I), ("nzt", V + PAD, _I), ("xt", V + PAD, _B), ("idt", V + PAD, _F),
     ("z1", WIN, _B), ("z2", WIN, _B), ("z3", WIN, _B), ("y1", WIN, _B), ("y2", WIN, _B), ("y3", WIN, _B),
-    ("mt", NB + V, _F), ("it", NB + V, _F),
-    ("ml32", 128, _I), ("mlh", 128, _H), ("mlt", 128, _H), ("mlist", 128, _U),
+    ("mt", NB + V + PAD, _F), ("it", NB + V + PAD, _F),
+    ("mr", 128, _I), ("mlh", 128, _H), ("mlt", 128, _H), ("mlist", 128, _U),
     ("m2", 128, _I), ("i2", 128, _I), ("m2h", 128, _H), ("i2h", 128, _H),
     ("bx32", 16, _I), ("bz32", 16, _I), ("bxl", 16, _U), ("bzl", 16, _U),
     ("gz", NB, _B), ("gy", NB, _B),
-    ("ones", 128, _B), ("idn", 128, _B), ("idm", 128, _B), ("bo8", 8, _B), ("gp", 8, _B), ("g1", 8, _B), ("gm", 8, _B),
-    ("fk", 2048, _B), ("au", 512, _B), ("auq", 256, _B), ("ej", 2048, _B),
-    ("bq0", 128, _B), ("bq", 128, _B), ("lj", 16, _F), ("lk", 16, _F),
-    ("tb0", 128, _B), ("tb", 128, _B), ("w1k", 1024, _B), ("dw", 1024, _B),
-    ("ms0", 72, _F), ("ms1", 72, _F), ("ms", 72, _F), ("c0", 128, _F), ("c1", 128, _F),
-    ("pi", 8, _I), ("pi2", 8, _I), ("pf", 8, _F), ("li", 16, _F), ("alt", 40, _F),
-    ("vl", 8, _U), ("vf", 8, _F), ("mvr", 128, _H), ("mvt", 128, _H), ("mvl", 8, _U),
-    ("nbv", 128, _U), ("nzv", 128, _U), ("cat", 256, _H), ("catt", 256, _H),
-    ("zg", 2048, _B), ("dd", 2048, _B), ("rr", 2048, _B),
-    ("db", 128, _F), ("old", 128, _H), ("s0", 256, _H), ("sc", 256, _H), ("sct", 256, _H),
-    ("l4", 32, _U), ("l4f", 32, _F), ("wp", 256, _H), ("wpt", 256, _H), ("raq", 256, _F), ("nm", 256, _H),
+    ("ones", 1024, _B), ("idn", 128, _B), ("idm", 128, _B), ("ide", 128, _B), ("idf", 128, _B),
+    ("gk", 8, _B), ("gk2", 8, _B), ("gkm", 8, _B), ("gp", 20, _B), ("gm", 20, _B),
+    ("ej", 2048, _B), ("bq", 128, _B), ("sel", 1024, _B), ("tb", 128, _B),
+    ("pi", 8, _I), ("pa", 8, _I), ("pf", 8, _F), ("cor0", 8, _F), ("cor", 8, _F), ("lk", 16, _F),
+    ("i16", 128, _F), ("g8", 128, _F), ("gq", 128, _F), ("p10", 160, _F), ("t0", 160, _F), ("t1", 160, _F),
+    ("s8", 128, _F), ("s16", 128, _F), ("c1", 128, _F), ("mz", 160, _F), ("my", 160, _F), ("mv", 160, _F),
+    ("li", 16, _F), ("alt", 16, _F),
+    ("vl", 8, _U), ("mvr", 128, _F), ("mvs", 128, _F), ("mvl", 8, _U),
+    ("nbv", 128, _U), ("nzv", 128, _U), ("cat", 256, _H),
+    ("zg", 2048, _B), ("yg", 2048, _B), ("rr", 2048, _B),
+    ("mx", 128, _F), ("gap", 128, _F), ("d1", 256, _F), ("sc", 256, _H), ("ls", 128, _F),
+    ("l4", 32, _U), ("l4f", 32, _F), ("rw", 512, _F), ("ws", 256, _F), ("nm", 256, _H),
     ("nba", 128, _U), ("nzq", 128, _U), ("nbw", 128, _U), ("nzp", 128, _U),
-    ("ga", 2048, _B), ("gw", 2048, _B), ("gb", 2048, _B),
+    ("ga", 2048, _B), ("gw", 2048, _B), ("gb", 2048, _B), ("gc", 2048, _B),
     ("m_1", 2048, _B), ("m_2", 2048, _B), ("m_3", 2048, _B), ("m_4", 2048, _B),
-    ("ka", 2048, _B), ("kw", 2048, _B), ("tc", 1024, _B), ("tk", 1024, _B),
-    ("xg", 256, _B), ("zd", 256, _B), ("zc", 256, _B), ("zn", 256, _B),
-    ("lv0", 8, _F), ("lv1", 8, _F), ("lv2", 8, _F), ("lv", 8, _B), ("thl", 8, _F), ("thm", 8, _F), ("thn", 8, _F), ("prop", 16, _B),
-    ("t6", 8, _F), ("sel", 72, _F), ("com", 40, _F), ("cm", 40, _F), ("off", 32, _U), ("n5", 40, _F), ("dl", 40, _F),
-    ("sv", 8, _I), ("sv2", 8, _I), ("qo", 8, _F), ("dws", 8, _F), ("dwq", 8, _F), ("cb", 8, _B),
-    ("cn", 8, _F), ("cni", 8, _I), ("cnj", 8, _I),
+    ("ka", 2048, _B), ("kw", 2048, _B), ("tc", 1024, _B), ("tl", 1024, _B), ("tk", 1024, _B),
+    ("xg", 256, _B), ("zq", 256, _B), ("sg", 256, _B),
+    ("v0", 8, _F), ("v1", 8, _F), ("void", 8, _B), ("prop", 24, _B), ("th", 8, _F),
+    ("sz", 160, _F), ("sy", 160, _F), ("sv", 160, _F), ("oz", 16, _U), ("oy", 16, _U),
+    ("n5", 8, _I), ("n6", 8, _I), ("a0", 8, _F), ("a1", 8, _F), ("av", 8, _F), ("cb", 8, _B),
+    ("cn", 8, _F), ("cq", 8, _I),
 ]:
     SCRATCH[_n] = ("sbuf", [128, _w], _t)
-for _n in ["p_a", "p_b", "p_d", "p_g", "p_l", "p_q", "p_t0", "p_t1"]:
+for _n in ["p_a", "p_b", "p_d", "p_g", "p_l", "p_n", "p_t0", "p_t1"]:
     SCRATCH[_n] = ("psum", [128, 512], "float32")
 
-DMAS = ["d_ml", "d_z", "d_bz", "d_bx", "d_m2", "d_i2", "d_nb", "d_nz", "d_x", "d_z2", "d_y2", "d_z3", "d_y3", "d_mo", "d_zo"]
+DMAS = ["d_mr", "d_z", "d_bz", "d_bx", "d_m2", "d_i2", "d_nb0", "d_nb1", "d_nz", "d_x", "d_z2", "d_y2", "d_z3", "d_y3", "d_mo", "d_zo"]
 SEMAPHORES = ["V", "S", "P", "G"] + DMAS + ["%s%s%d" % (k, w, t) for k in ("arr", "snt") for w in ("z", "y") for t in (1, 2, 3)]
+
+
+def steps_of(text):
+    out = []
+    for part in text.split("|"):
+        w = part.split()
+        out += [(w[0], int(w[1]), int(w[2])) + tuple(w[3:])] if len(w) > 1 and w[1].isdigit() else [(x,) for x in w]
+    return out
 
 
 def rank_program(g, core, T, topo):
@@ -68,15 +90,26 @@ def rank_program(g, core, T, topo):
     known = {q: {} for q in Q}
     clock = {}
     acc = {}
+    held = []
 
     def psum(name):
         return name[:2] == "p_"
 
     def meet(r1, r2):
-        if r1[1] >= r2[2] or r2[1] >= r1[2] or r1[3] >= r2[4] or r2[3] >= r1[4]:
+        if r1[0] != r2[0] or r1[1] >= r2[2] or r2[1] >= r1[2] or r1[3] >= r2[4] or r2[3] >= r1[4]:
             return False
         s = r1[5]
         return not (s == r2[5] and s > 1 and (r1[3] - r2[3]) % s)
+
+    def wait(q, e, idx):
+        kn = known[q]
+        if kn.get(e, 0) >= idx:
+            return
+        Q[q].wait_ge(T.sem[e], idx)
+        for e2, i2 in clock.get((e, idx), {}).items():
+            if kn.get(e2, 0) < i2:
+                kn[e2] = i2
+        kn[e] = idx
 
     def order(q, reads, writes, me):
         need = {}
@@ -84,7 +117,7 @@ def rank_program(g, core, T, topo):
             for r in regs:
                 for (e, k2, r2), idx in acc.get(r[0], {}).items():
                     same = e == q
-                    if same and (q == "P" or k2 == "r"):
+                    if same and q == "P":
                         continue
                     if same or not psum(r[0]):
                         if (kind == "r" and k2 == "r") or not meet(r, r2):
@@ -93,13 +126,7 @@ def rank_program(g, core, T, topo):
                         need[e] = idx
         kn = known[q]
         for e in sorted(need, key=lambda e: -len(clock.get((e, need[e]), {}))):
-            if kn.get(e, 0) >= need[e]:
-                continue
-            Q[q].wait_ge(T.sem[e], need[e])
-            for e2, i2 in clock.get((e, need[e]), {}).items():
-                if kn.get(e2, 0) < i2:
-                    kn[e2] = i2
-            kn[e] = max(kn.get(e, 0), need[e])
+            wait(q, e, need[e])
         e, idx = me
         clock[(e, idx)] = dict(kn)
         for kind, regs in (("r", reads), ("w", writes)):
@@ -138,11 +165,42 @@ def rank_program(g, core, T, topo):
                 rd.append(r)
         return rd, wr
 
-    def run(q, outs, ins, call):
-        rd, wr = split(outs, ins)
+    def issue(q, rd, wr, call):
         count[q] += 1
         order(q, rd, wr, (q, count[q]))
         call(Q[q]).then_inc(T.sem[q], 1)
+
+    def run(q, outs, ins, call):
+        rd, wr = split(outs, ins)
+        if held:
+            held[-1].append((q, rd, wr, call))
+        else:
+            issue(q, rd, wr, call)
+
+    def phase(plan, makers):
+        lines = {q: steps_of(text) for q, text in plan.items()}
+        made = []
+        for block in makers:
+            block = block if isinstance(block, list) else [block]
+            todo = [(s[1:2], x, q, s, f) for x, (name, f) in enumerate(block) for q in lines for s in lines[q] if s[0] == name]
+            for _, _, q, s, f in sorted(todo, key=lambda e: e[:2]):
+                held.append([])
+                f(q, *s[1:])
+                made.append((q, s, held.pop()))
+        before = {}
+        for x, (q, s, calls) in enumerate(made):
+            rd = [r for c in calls for r in c[1]]
+            wr = [r for c in calls for r in c[2]]
+            before[q, s] = [(q2, s2) for q2, s2, c2 in made[:x] if q2 != q and any(
+                meet(a, b) for c in c2 for a, bs in [(a, rd + wr) for a in c[2]] + [(a, wr) for a in c[1]] for b in bs)]
+        calls = {(q, s): c for q, s, c in made}
+        done = set()
+        while any(lines.values()):
+            q = [q for q in lines if lines[q] and all(b in done for b in before[q, lines[q][0]])][0]
+            s = lines[q].pop(0)
+            for c in calls[q, s]:
+                issue(*c)
+            done.add((q, s))
 
     def val(s):
         return ap(s) if isinstance(s, tuple) else s
@@ -169,8 +227,11 @@ def rank_program(g, core, T, topo):
     def ms(o, c):
         run("V", [o], [], lambda q: q.memset(ap(o), c))
 
-    def act(o, i, scale=1.0, fn=Fn.Copy):
-        run("S", [o], [i], lambda q: q.activation(ap(o), ap(i), fn, 0.0, scale))
+    def act(o, i, fn=Fn.Copy, bias=0.0, scale=1.0):
+        run("S", [o], [i], lambda q: q.activation(ap(o), ap(i), fn, bias, scale))
+
+    def cp(q, o, i):
+        (tc if q == "V" else act)(o, i)
 
     def mm(o, a, b, start=True, stop=True):
         run("P", [o], [a, b], lambda q: q.matmul(ap(o), ap(a), ap(b), start, stop))
@@ -184,8 +245,8 @@ def rank_program(g, core, T, topo):
     def aff(o, i, pat, op, fill, base, cmul):
         run("G", [o], [i], lambda q: q.affine_select(ap(o), ap(i), pat, op, fill, base, cmul))
 
-    def dma(q, sem, pairs, total=None):
-        tot = 16 * (total or len(pairs))
+    def dma(q, sem, pairs):
+        tot = 16 * len(pairs)
         for o, i in pairs:
             rd, wr = split([o] if isinstance(o, tuple) else [], [i] if isinstance(i, tuple) else [])
             order(q, rd, wr, (sem, tot))
@@ -205,76 +266,62 @@ def rank_program(g, core, T, topo):
         return R(name, NB, NB + V)
 
     def full(name):
-        return R(name, NB, WIN)
+        return R(name, NB)
 
     def park(name):
         return R(name, 0, NB + V)
 
-    pieces = [(R("ml32", 32 * c + 16 * h, 32 * c + 16 * h + 16), T.m[h::2, 512 * c:512 * c + 512]) for c in range(4) for h in range(2)]
-    dma("Y", "d_ml", pieces[:4], 8)
-    dma("S", "d_ml", pieces[4:], 8)
-    dma("S", "d_bz", [(R("bz32"), T.bz[:, :])])
-    dma("Y", "d_m2", [(R("m2"), T.m[:, :])])
-    dma("S", "d_z", [(own("z1"), T.z[:, :])])
-    dma("Y", "d_bx", [(R("bx32"), T.bx[:, :])])
-    dma("Y", "d_nz", [(R("nzt"), T.nz[:, :])])
-    dma("S", "d_nb", [(R("nbt"), T.nb[:, :])])
-    dma("Y", "d_i2", [(R("i2"), T.im[:, :])])
-    dma("Y", "d_x", [(R("xt"), T.x[:, :])])
+    def C(name, a, b):
+        return R(name, 16 * a, 16 * b)
 
-    ms(R("ones"), 1.0)
-    aff(R("bo8"), R("ones", 0, 8), [[-16, 8]], Op.is_ge, 0.0, 0, 1)
-    aff(R("g1"), R("bo8"), [[16, 8]], Op.is_ge, 0.0, 15, -1)
-    iota(R("pi"), [[0, 8]], 0, 1, False)
+    dma("S", "d_mr", [(R("mr", 64 * h, 64 * h + 64), T.m[h::2, :]) for h in range(2)])
+    dma("Y", "d_bz", [(R("bz32"), T.bz[:, :])])
+    dma("Y", "d_z", [(own("z1"), T.z[:, :])])
+    dma("Y", "d_bx", [(R("bx32"), T.bx[:, :])])
+    dma("Y", "d_m2", [(R("m2"), T.m[:, :])])
+    dma("Y", "d_nz", [(R("nzt", 0, V), T.nz[:, :])])
+    dma("Y", "d_i2", [(R("i2"), T.im[:, :])])
+
+    def load_nb(h):
+        dma("Y", "d_nb%d" % h, [(R("nbt", 1024 * h, 1024 * h + 1024), T.nb[:, 1024 * h:1024 * h + 1024])])
+
+    I_, IM, G_, GM = [R("pf", k, k + 1) for k in (0, 1, 4, 6)]
+    iota(R("pi", 0, 4), [[112, 2], [15, 2]], 0, 1, False)
+    iota(R("i16"), [[0, 8], [1, 16]], 0, 0)
+    iota(R("gq"), [[1, 8], [0, 16]], 0, 0)
+    iota(R("g8"), [[0, 16], [1, 8]], 0, 0)
     iota(R("li"), [[128, 2], [16, 8]], 0, 0)
-    iota(R("lj"), [[1, 16]], 0, 0)
-    aff(R("bq0"), R("ones"), [[-16, 8], [0, 16]], Op.is_ge, 0.0, 0, 1)
-    aff(R("bq"), R("bq0"), [[16, 8], [0, 16]], Op.is_ge, 0.0, 15, -1)
-    for u in range(2):
-        aff(R("auq", 128 * u, 128 * u + 128), R("ones"), [[-32, 4], [0, 2], [-1, 16]], Op.is_equal, 0.0, -16 * u, 1)
-        for h in range(2):
-            k = 128 * (2 * u + h)
-            aff(R("au", k, k + 128), R("auq", 128 * u, 128 * u + 128), [[0, 4], [1, 2], [0, 16]], Op.is_equal, 0.0, -h, 0)
-    iota(R("tb0"), [[0, 8], [-1, 16]], 15, 0)
-    ms(R("fk"), 0.0)
-    ts(R("pi2"), R("pi"), 15, Op.bitwise_and)
-    tc(R("pf"), R("pi2"))
-    ts(R("alt", 0, 16), R("li"), R("pf", 0, 1), Op.add)
-    ts(R("alt", 16, 32), R("li"), R("pf", 0, 1), Op.add)
-    ts(R("vf"), R("alt", 0, 8), 16.0, Op.mult)
-    tc(R("vl"), R("vf"))
-    ts(R("lk"), R("lj"), R("pf", 0, 1), Op.is_equal)
-    ts(R("gp"), R("g1"), 2.0, Op.mult)
-    ts(R("gm"), R("g1"), -2.0, Op.mult)
-    for k in range(16):
-        act(R("fk", 128 * k + k, 128 * k + 128, 16), R("g1"))
+    iota(R("p10"), [[0, 16], [1, 10]], 0, 0)
+    ms(R("ones"), 1.0)
+    aff(R("idn"), R("ones", 0, 128), [[-1, 128]], Op.is_equal, 0.0, 0, 1)
+    for h in range(2):
+        act(R("kw", 1024 * h, 1024 * h + 1024), R("ones"), scale=0.0)
+    ts(R("pa", 0, 4), R("pi", 0, 4), 15, Op.bitwise_and)
+    ts(R("pa", 4, 8), R("pi", 0, 4), 4, Op.logical_shift_right, 7, Op.bitwise_and)
+    ms(R("ka"), 0.0)
+    tc(R("pf"), R("pa"))
+    ts(R("lk"), R("i16", 0, 16), I_, Op.is_equal)
+    ts(R("bq"), R("gq"), G_, Op.is_equal)
     for k in range(16):
         ts(R("ej", 128 * k, 128 * k + 128), R("bq"), R("lk", k, k + 1), Op.mult)
-    tc(R("mlh"), R("ml32"))
+    for h in range(2):
+        for b in range(4):
+            tc(R("mlh", 32 * b + 16 * h, 32 * b + 16 * h + 16), R("mr", 64 * h + 16 * b, 64 * h + 16 * b + 16))
     tr(R("mlt"), R("mlh"))
-    tc(R("mlist"), R("mlt"))
     tc(R("bzl"), R("bz32"))
-    tc(R("bxl"), R("bx32"))
-    tc(R("m2h"), R("m2"))
+    for b in range(4):
+        tc(R("mlist", b, 128, 4), R("mlt", 32 * b, 32 * b + 32))
     act(R("gz"), ind(own("z1"), R("bzl")))
     send("z", 1, R("gz"))
-    tc(R("y1", NB, NB + 1024), ind(own("z1"), R("mlist", 0, 64)))
-    act(R("y1", NB + 1024, NB + V), ind(own("z1"), R("mlist", 64, 128)))
+    tc(R("y1", NB, NB + 1152), ind(own("z1"), R("mlist", 0, 72)))
+    act(R("y1", NB + 1152, NB + V), ind(own("z1"), R("mlist", 72, 128)))
+    tc(R("bxl"), R("bx32"))
+    tc(R("m2h"), R("m2"))
     act(R("gy"), ind(own("y1"), R("bxl")))
     send("y", 1, R("gy"))
-    dma("Y", "d_z2", [(own("z2"), own("z1"))])
-    dma("Y", "d_y2", [(own("y2"), own("y1"))])
-
-    ts(R("tb"), R("tb0"), 1.0 / 2048, Op.mult)
-    ms(R("c0"), FAR)
-    aff(R("c1"), R("c0"), [[0, 8], [1, 16]], Op.not_equal, -1.0, 0, 0)
-    ms(R("w1k"), WD)
-    ms(R("ms0"), PASS)
-    ms(R("t6"), FAR)
-    aff(R("idn"), R("ones"), [[-1, 128]], Op.is_equal, 0.0, 0, 1)
-    aff(R("ms1"), R("ms0"), [[0, 8], [-16, 9]], Op.is_ge, 1.0, 16, 1)
-    aff(R("ms"), R("ms1"), [[0, 8], [16, 9]], Op.is_ge, 0.0, -1, -1)
-    aff(R("dw"), R("w1k"), [[-16, 8], [0, 8], [-1, 16]], Op.is_equal, 0.0, 0, 1)
+    wait("Y", "S", count["S"])
+    for h in range(2):
+        load_nb(h)
 
     def spread(half, tab):
         for jb in range(4):
@@ -284,220 +331,267 @@ def rank_program(g, core, T, topo):
                 mm(R(b, 128 * j, 128 * j + 128), R("ej", 128 * J, 128 * J + 128), R(half))
             act(R(tab, NB + 512 * jb, NB + 512 * jb + 512), R(b))
 
+    def picks(o, it, at, before):
+        ts(R("t0", 0, 128), R(it), at, Op.is_equal, BIG, Op.mult)
+        ts(R("t1", 0, 128), R(it), before, Op.is_equal, -2 * BIG, Op.mult)
+        tt(R(o), R("t0", 0, 128), R("t1", 0, 128), Op.add)
+
+    aff(R("sel"), R("ones"), [[-16, 8], [0, 8], [-1, 16]], Op.is_equal, 0.0, 0, 1)
+    iota(R("idt"), [[1, V + PAD]], 0, 0)
+    for tab in ("mt", "it"):
+        ms(R(tab, NB + V), 0.0)
+    ms(R("nbt", V), 0)
+    ms(R("nzt", V), 0)
+    ms(R("xt", V), 0.0)
+    picks("s16", "i16", I_, IM)
+    ts(R("cor0", 0, 2), R("pf", 0, 8, 4), 0.0, Op.is_equal, 2 * BIG, Op.mult)
+    ts(R("cor", 0, 2), R("cor0", 0, 2), -BIG, Op.add)
+    C16, C8 = R("cor", 0, 1), R("cor", 1, 2)
+    ts(R("alt"), R("li"), I_, Op.add)
+    ts(R("vl"), R("alt", 0, 8), 16.0, Op.mult)
     spread("m2h", "mt")
+    wait("Y", "d_nb1", 16)
+    dma("Y", "d_x", [(R("xt", 0, V), T.x[:, :])])
+    ts(R("gk"), R("g8", 0, 8), G_, Op.is_equal, KEY, Op.mult)
+    ts(R("gk2"), R("g8", 0, 8), G_, Op.is_equal, 2 * KEY, Op.mult)
+    ts(R("gkm"), R("g8", 0, 8), G_, Op.is_equal, -KEY, Op.mult)
+    ts(R("tb"), R("i16"), -32.0, Op.mult, 480.0, Op.add)
+    ts(R("t0", 0, 128), R("i16"), 0.0, Op.not_equal, 2.0 ** 30, Op.mult)
+    ts(R("c1"), R("t0", 0, 128), -1.0, Op.add)
+    picks("s8", "g8", G_, GM)
+    ts(R("t0"), R("p10"), -1.0, Op.add, G_, Op.is_equal)
+    ts(R("gp"), R("t0", 0, 20), 2.0, Op.mult)
+    ts(R("gm"), R("t0", 0, 20), -2.0, Op.mult)
+    ts(R("t1"), R("t0"), 1 / EPS - 1, Op.mult)
+    ts(R("t0"), R("p10"), G_, Op.not_equal)
+    for o in ("mz", "my", "mv"):
+        tt(R(o), R("t0"), R("t1"), Op.add)
+    for o, s in (("idm", -1.0), ("ide", -EPS), ("idf", -FAR)):
+        ts(R(o), R("idn"), s, Op.mult)
+    ms(R("th"), 0.0)
 
-    def lists(base, nx, src, at):
-        for u in range(2):
-            for h in range(2):
-                k = 128 * (2 * u + h)
-                mm(R("p_l", base + u, base + 8 * nx, 2), R("au", k, k + 128), R(src, 16 * h + at, 128 * nx, 32), h == 0, h == 1)
+    def to_list(o, row, tmp):
+        scan(tmp, row, R("s16"), Op.max, Op.add)
+        ts(o, (tmp[0], 0, 128, tmp[3] + 15, tmp[4], 16), C16, Op.add)
 
-    def cols(ln):
-        return 16 * ln[0], 16 * ln[1]
+    A_, W_, Q_, P_ = [R("l4", 8 * k, 8 * k + 8) for k in range(4)]
+    rA, rW, rQ, rP = [R("rw", 128 * k, 128 * k + 128) for k in range(4)]
 
     for t in range(1, RO + 1):
         Y, Z = "y%d" % t, "z%d" % t
         Yn, Zn = ("y%d" % (t + 1), "z%d" % (t + 1)) if t < RO else (Y, Z)
-        tc(R("mvr"), ind(own("mt"), R("vl")))
-        tr(R("mvt"), R("mvr"))
-        lists(0, 1, "mvt", 0)
-        if t > 1:
-            tc(R("nbv"), ind(R("nbt"), R("vl")))
-        tc(R("mvl"), R("p_l", 0, 8))
-        tc(R("nzv"), ind(R("nzt"), R("mvl")))
-        if t == 1:
-            ms(R("prop"), 0.0)
-            ts(R("idm"), R("idn"), -1.0, Op.mult)
-            tc(R("i2h"), R("i2"))
-            tc(R("nbv"), ind(R("nbt"), R("vl")))
-        ts(R("cat", 0, 128), R("nbv"), 2048.0, Op.min)
-        ts(R("cat", 128, 256), R("nzv"), 2048.0, Op.min)
-        tr(R("catt"), R("cat"))
-        for ln in DS:
-            act(R("zg", *cols(ln)), ind(full(Z), R("nzv", *ln)))
-        for ln in DV:
-            tc(R("zg", *cols(ln)), ind(full(Z), R("nzv", *ln)))
-        act(R("dd", *cols(DY)), ind(full(Y), R("nbv", *DY)))
-        yz = R("p_a", 0, 16 * (DY[1] - DY[0]))
-        mm(yz, R("idn"), R("dd", *cols(DY)), True, False)
-        mm(yz, R("idm"), R("zg", *cols(DY)), False, True)
+        first, last = t == 1, t == RO
 
-        def sums(e):
-            o = R("p_d", DP * e, DP * e + DP)
-            mm(o, R("tb"), R("ones", 0, DP), True, False)
+        def nbv1(q, a, b):
+            cp(q, R("nbv", a, b), R("nbt", 16 * a, 16 * b, 16))
+
+        def im1(q, a, b):
+            bk = ("p_g", "p_l")[a // 4 % 2]
+            if q == "P":
+                for J in range(a, b):
+                    mm(R(bk, 128 * (J - a), 128 * (J - a + 1)), R("ej", 128 * J, 128 * J + 128), R("i2h"))
+            else:
+                cp(q, R("it", NB + 128 * a, NB + 128 * b), R(bk))
+
+        def im(q):
+            if not first:
+                tc(ind(park("it"), R("oz")), R("rw", 0, 256))
+                ts(R("cb"), R("sv", 9, 160, 20), 0.5, Op.is_ge)
+
+        def th(q):
+            if not first:
+                run("V", [R("cn", 0, 1)], [R("p_l", 200, 208)],
+                    lambda e: e.tensor_reduce(ap(R("cn", 0, 1)), ap(R("p_l", 200, 208)), AxisListType.X, Op.add))
+                ts(R("cq", 0, 1), R("cn", 0, 1), 1.0 / 32, Op.mult, -31.0 / 64, Op.add)
+                ts(R("th", 0, 1), R("cq", 0, 1), -32.0, Op.mult, R("cn", 0, 1), Op.add)
+
+        def sums(src, wgt, a, b, stop):
             for k in range(16):
-                mm(o, R("fk", 128 * k, 128 * k + 128), R("rr", 16 * DP * e + k, 16 * DP * (e + 1), 16), False, k == 15)
+                mm(R("p_d", k, 128, 16, a, b), R(src, 16 * a + k, 16 * b, 16), R(wgt), False, stop and k == 15)
 
-        for x, ln in enumerate(DCH):
-            tt(R("dd", *cols(ln)), ind(full(Y), R("nbv", *ln)), R("zg", *cols(ln)), Op.subtract)
-            act(R("rr", *cols(ln)), R("dd", *cols(ln)), 1.0, Fn.Abs)
-            if x == 0:
-                act(R("rr", *cols(DY)), yz, 1.0, Fn.Abs)
-            if ln[1] == DP:
-                sums(0)
-        sums(1)
-        if t > 1:
-            tc(ind(park("it"), R("off", 0, 8)), R("raq", 0, 128))
-            tc(ind(park("it"), R("off", 8, 16)), R("wp", 0, 128))
-            tc(R("cb"), R("com", 0, 8))
-            mm(R("p_l", 80, 88), R("ones"), R("cb"))
-            run("V", [R("cn", 0, 1)], [R("p_l", 80, 88)],
-                lambda q: q.tensor_reduce(ap(R("cn", 0, 1)), ap(R("p_l", 80, 88)), AxisListType.X, Op.add))
-            tc(R("cni", 0, 1), R("cn", 0, 1))
-            ts(R("cnj", 0, 1), R("cni", 0, 1), 31, Op.bitwise_and)
-            ts(R("t6", 0, 1), R("cnj", 0, 1), FAR, Op.add)
-        else:
-            spread("i2h", "it")
-            ms(R("ka"), 0.0)
-            ms(R("kw"), 0.0)
-        tr(R("db"), R("p_d", 0, 128))
-        scan(R("p_q", 0, 128), R("c1"), R("db"), Op.min, Op.max)
-        tt(R("p_q", 128, 256), R("p_q", 0, 128), R("db"), Op.is_equal)
-        tt(R("old"), R("p_q", 0, 128), R("db"), Op.is_gt)
-        tt(R("s0", 0, 128), R("p_q", 128, 256), R("catt", 0, 128), Op.mult)
-        tt(R("s0", 128, 256), R("p_q", 128, 256), R("catt", 128, 256), Op.mult)
-        scan(R("sc", 0, 128), R("old"), R("s0", 0, 128), Op.mult, Op.add)
-        scan(R("sc", 128, 256), R("old"), R("s0", 128, 256), Op.mult, Op.add)
-        lists(16, 2, "sc", 15)
-        ts(R("l4", 0, 8), R("p_l", 16, 24), 2047.0, Op.min)
-        ts(R("l4", 16, 24), R("p_l", 24, 32), 2047.0, Op.min)
-        tc(R("nba"), ind(R("nbt"), R("l4", 0, 8)))
-        tc(R("wp", 0, 128), ind(own("it"), R("l4", 16, 24)))
-        tc(R("wp", 128, 256), ind(own("mt"), R("l4", 0, 8)))
-        tr(R("wpt"), R("wp"))
-        lists(32, 2, "wpt", 0)
-        tc(R("nzq"), ind(R("nzt"), R("l4", 16, 24)))
-        tr(R("sct"), R("sc"))
-        mm(R("p_d", 128, 384), R("ej", 128 * 15, 2048), R("sct"))
-        tc(R("l4", 8, 16), R("p_l", 32, 40))
-        tc(R("l4", 24, 32), R("p_l", 40, 48))
-        tc(R("nbw"), ind(R("nbt"), R("l4", 8, 16)))
-        tc(R("nzp"), ind(R("nzt"), R("l4", 24, 32)))
+        def nbank(a, b):
+            return R(("p_a", "p_b", "p_t0", "p_t1")[a // 32], 16 * (a % 32), 16 * (a % 32 + b - a))
 
-        def fetch(o, win, lst, ln):
-            act(R(o, *cols(ln)), ind(full(win), R(lst, *ln)))
+        def fallback(q):
+            if not last:
+                ts(R("n5"), R("vl"), 5.0, Op.mult, 1.0, Op.add)
+                ts(R("n6"), R("n5"), 2047, Op.bitwise_and)
 
-        def fused(mx, src, ln):
-            tt(R(mx, *cols(ln)), ind(full(Z), R("nzq", *ln)), R(src, *cols(ln)), Op.max)
-
-        def gain(terms, o):
-            for x, (mx, wgt) in enumerate(terms):
-                for k in range(16):
-                    mm(o, R(mx, k, 2048, 16), R(wgt), x == 0 and k == 0, x == len(terms) - 1 and k == 15)
-
-        for ln in CH[:2]:
-            fetch("ga", Y, "nba", ln)
-        act(R("raq"), R("p_d", 128, 384))
-        for ln in CH[2:]:
-            fetch("ga", Y, "nba", ln)
-        for ln in CH:
-            fused("m_1", "ga", ln)
-        gain([("m_1", "gm")], R("p_g", 0, 8))
-        fetch("gw", Y, "nbw", CH[0])
-        act(R("xg"), ind(R("xt"), R("l4", 0, 16)))
-        for ln in CH[1:]:
-            fetch("gw", Y, "nbw", ln)
-        ts(R("l4f", 0, 8), R("p_l", 16, 24), 2047.0, Op.min)
-        ts(R("l4f", 16, 24), R("p_l", 24, 32), 2047.0, Op.min)
-        ts(R("qo"), R("p_l", 24, 32), 2048.0, Op.is_lt)
-        tc(R("l4f", 8, 16), R("p_l", 32, 40))
-        tc(R("l4f", 24, 32), R("p_l", 40, 48))
-        tc(R("nm", 0, 256, 2), R("raq", 0, 128))
-        tc(R("nm", 1, 256, 2), R("wp", 0, 128))
-        for c in range(8):
-            wd = 32 * (c + 1)
-            for kk, s in (("ka", c), ("kw", 8 + c)):
-                ts(R(kk, 256 * c, 256 * c + wd), R("nm", 0, wd), R("l4f", s, s + 1), Op.is_equal)
-            o = R("p_t%d" % (c // 4), 128 * (c % 4), 128 * (c % 4) + 128)
-            mm(o, R("idn"), R("dw", 128 * c, 128 * c + 128), True, False)
-            for x, (kk, y) in enumerate((("ka", 0), ("ka", 1), ("kw", 0), ("kw", 1))):
-                mm(o, R(kk, 256 * c + y, 256 * c + 256, 2), R("idn"), False, x == 3)
-        tt(R("lv0"), R("sc", 15, 128, 16), R("sc", 128 + 15, 256, 16), Op.max)
-        ts(R("lv1"), R("lv0"), 2048.0, Op.is_lt)
-        ts(R("lv2"), R("p_q", 15, 128, 16), 1.0, Op.is_ge)
-        tt(R("lv"), R("lv1"), R("lv2"), Op.mult)
-        for e in range(4):
-            for b in range(4):
-                mm(R("p_l", 64 + 2 * b, 66 + 2 * b, 1, 32 * e, 32 * e + 32), R("idn", 32 * b, 32 * b + 32), R("lv", 2 * e, 2 * e + 2))
-        for ln in CH[2:]:
-            fetch("gb", Z, "nzp", ln)
+        phase(NAMING1 if first else NAMING, [
+            ("i2h", lambda q: cp(q, R("i2h"), R("i2"))),
+            [("imP", im1), ("im1", im1)],
+            ("mv", lambda q: cp(q, R("mvr"), ind(full("mt"), R("vl")))),
+            ("mvl", lambda q: to_list(R("mvl"), R("mvr"), R("mvs"))),
+            ("nbv1", nbv1),
+            ("nbv", lambda q: first or cp(q, R("nbv"), ind(R("nbt"), R("vl")))),
+            ("nzv", lambda q: cp(q, R("nzv"), ind(R("nzt"), R("mvl")))),
+            ("im", im),
+            ("count", lambda q: first or mm(R("p_l", 200, 208), R("ones", 0, 128), R("cb"))),
+            ("th", th),
+            ("cat", lambda q: [ts(R("cat", 128 * x, 128 * x + 128), R(s), 2048.0, Op.min) for x, s in enumerate(("nbv", "nzv"))]),
+            ("catT", lambda q: [mm(R("p_n", 128 * x, 128 * x + 128), R("cat", 128 * x, 128 * x + 128), R("idn")) for x in range(2)]),
+            ("rank", lambda q: mm(R("p_d", 0, 128), R("ones", 0, 128), R("tb"), True, False)),
+            ("Z", lambda q, a, b: cp(q, C("zg", a, b), ind(full(Z), R("nzv", a, b)))),
+            ("Y", lambda q, a, b: cp(q, C("yg", a, b), ind(full(Y), R("nbv", a, b)))),
+            ("diff", lambda q, a, b: [mm(nbank(a, b), R("idn"), C("yg", a, b), True, False), mm(nbank(a, b), R("idm"), C("zg", a, b), False, True)]),
+            ("abs", lambda q, a, b: act(C("rr", a, b), nbank(a, b), Fn.Abs)),
+            ("dY", lambda q, a, b: tt(C("yg", a, b), ind(full(Y), R("nbv", a, b)), C("zg", a, b), Op.subtract)),
+            ("absd", lambda q, a, b: act(C("rr", a, b), C("yg", a, b), Fn.Abs)),
+            ("relu", lambda q, a, b: ts(C("rr", a, b), C("yg", a, b), 0.0, Op.max)),
+            ("sum", lambda q, a, b: sums("rr", "gk", a, b, True)),
+            ("zP", lambda q, a, b: mm(nbank(a, b), R("idn"), C("zg", a, b))),
+            ("max", lambda q, a, b: tt(C("rr", a, b), nbank(a, b), C("yg", a, b), Op.max)),
+            ("sumz", lambda q, a, b: sums("zg", "gkm", a, b, False)),
+            ("sumy", lambda q, a, b: sums("yg", "gkm", a, b, False)),
+            ("summ", lambda q, a, b: sums("rr", "gk2", a, b, True)),
+            ("next", fallback),
+        ])
+        if not last:
+            wait("Y", "snt" + Y, nout)
+            dma("Y", "d_" + Zn, [(own(Zn), own(Z))])
+            dma("Y", "d_" + Yn, [(own(Yn), own(Y))])
+        scan(R("mx"), R("c1"), R("p_d", 0, 128), Op.min, Op.max)
+        tt(R("gap"), R("mx"), R("p_d", 0, 128), Op.subtract)
         for x in range(2):
-            act(R("tc", 512 * x, 512 * x + 512), R("p_t%d" % x))
-        aff(R("tk"), R("tc"), [[16, 8], [0, 8], [1, 16]], Op.is_ge, 0.0, 0, -1)
-        for ln in CH[:2]:
-            fetch("gb", Z, "nzp", ln)
-        fused("m_2", "gw", CH[0])
-        if t < RO:
-            ts(R("sv"), R("vf"), 5.0, Op.mult, 1.0, Op.add)
-            ts(R("sv2"), R("sv"), 2047, Op.bitwise_and)
-            tt(R("dws"), R("l4f", 8, 16), R("sv2"), Op.subtract)
-            tt(R("dwq"), R("dws"), R("qo"), Op.mult)
-            tt(R("alt", 32, 40), R("dwq"), R("sv2"), Op.add)
-            tc(R("n5", 32, 40), R("l4f", 0, 8))
-        ts(R("n5", 0, 16), R("l4f", 16, 32), float(NB), Op.add)
-        ts(R("n5", 16, 32), R("l4f", 0, 16), float(NB), Op.add)
-        wide = 40 if t < RO else 32
-        tt(R("dl", 0, wide), R("n5", 0, wide), R("alt", 0, wide), Op.subtract)
-        ts(R("thl"), R("p_l", 64, 72), -FAR, Op.mult, R("t6", 0, 1), Op.add)
-        qp = R("l4", 16, 32)
-        tt(R("zd"), ind(own(Z), qp), R("xg"), Op.subtract)
-        for ln in CH[1:]:
-            fused("m_2", "gw", ln)
-        ts(R("zc"), R("zd"), -1.0, Op.max, 1.0, Op.min)
-        tt(R("zn"), ind(own(Z), qp), R("zc"), Op.subtract)
-        sb = ["p_t0", "p_t1", "p_b"]
-        uses = [0]
-
-        def on_s(ln):
-            for mx, src in (("m_3", "ga"), ("m_4", "gw")):
-                b = R(sb[uses[0] % 3], 0, 16 * (ln[1] - ln[0]))
-                uses[0] += 1
-                mm(b, R("idn"), R(src, *cols(ln)), True, False)
-                mm(b, R("idm"), R("gb", *cols(ln)), False, True)
-                act(R(mx, *cols(ln)), b, 1.0, Fn.Relu)
-
-        def on_v(ln, b):
-            b = R(b, 0, 16 * (ln[1] - ln[0]))
-            mm(b, R("idn"), R("gb", *cols(ln)))
-            tt(R("m_3", *cols(ln)), b, R("ga", *cols(ln)), Op.max)
-            tt(R("m_4", *cols(ln)), b, R("gw", *cols(ln)), Op.max)
-
-        on_s(SCH[0])
-        on_v(VCH[0], "p_a")
-        on_s(SCH[1])
-        on_v(VCH[1], "p_q")
-        gain([("m_2", "gp")], R("p_g", 8, 16))
-        tt(R("thm"), R("thl"), R("p_g", 0, 8), Op.subtract)
-        tt(R("thn"), R("thm"), R("p_g", 8, 16), Op.subtract)
-        gain([("m_3", "gp"), ("m_4", "gm")], R("p_d", 400, 408))
-        tt(R("prop", 1, 9), R("p_d", 400, 408), R("thn"), Op.is_gt)
+            tt(R("d1", 128 * x, 128 * x + 128), R("p_n", 128 * x, 128 * x + 128), R("gap"), Op.subtract)
+        for x in range(2):
+            scan(R("sc", 128 * x, 128 * x + 128), R("gap"), R("d1", 128 * x, 128 * x + 128), Op.min, Op.max)
         for c in range(8):
-            mm(R("p_d", 9 * c, 9 * c + 9), R("tk", 128 * c, 128 * c + 128), R("prop", 0, 9))
-        scan(R("sel"), R("p_d", 0, 72), R("ms"), Op.max, Op.mult)
-        for x in range(wide // 8):
-            ts(R("com", 8 * x, 8 * x + 8), R("sel", 8, 72, 9), (WD + 2) * PASS, Op.is_equal)
-        tt(R("cm", 0, wide), R("com", 0, wide), R("dl", 0, wide), Op.mult)
-        tt(R("off"), R("cm", 0, 32), R("alt", 0, 32), Op.add)
-        tc(ind(park(Zn), R("off", 0, 16)), R("zn"))
-        if t < RO:
+            mm(R("p_l", 16 * c, 16 * c + 16), R("sel", 128 * c, 128 * c + 128), R("sc", 15, 256, 16))
+        tt(R("v0"), R("sc", 15, 128, 16), R("sc", 128 + 15, 256, 16), Op.max)
+        ts(R("v1"), R("mx", 15, 128, 16), KEY, Op.is_ge, 2048.0, Op.mult)
+        tt(R("void"), R("v1"), R("v0"), Op.is_le)
+        scan(R("ls"), R("p_l", 0, 128), R("s8"), Op.max, Op.add)
+        ts(A_, R("ls", 7, 128, 16), C8, Op.add)
+        ts(Q_, R("ls", 15, 128, 16), C8, Op.add)
+
+        def names(q):
+            cp(q, R("l4f", 0, 16), R("l4", 0, 16))
+            cp(q, R("nm", 1, 256, 2), rW)
+
+        def same(q):
+            for c in range(8):
+                for kk, s in (("ka", c), ("kw", 8 + c)):
+                    ts(R(kk, 256 * c, 256 * c + 32 * (c + 1)), R("nm", 0, 32 * (c + 1)), R("l4f", s, s + 1), Op.is_equal)
+
+        def same_turned(q):
+            for c in range(8):
+                o = R("p_t%d" % (c // 4), 128 * (c % 4), 128 * (c % 4) + 128)
+                for x, (kk, y) in enumerate((("ka", 0), ("ka", 1), ("kw", 0), ("kw", 1))):
+                    mm(o, R(kk, 256 * c + y, 256 * c + 256, 2), R("ide"), x == 0, x == 3)
+
+        def mask(x):
+            h = (512 * x, 512 * x + 512)
+            aff(R("tl", *h), R("tc", *h), [[16, 4], [0, 8], [1, 16]], Op.is_gt, 0.0, 64 * x, -1)
+            aff(R("tk", *h), R("tl", *h), [[16, 4], [0, 8], [1, 16]], Op.not_equal, EPS, 64 * x, -1)
+
+        def fetch(o, win, lst):
+            return lambda q, a, b: cp(q, C(o, a, b), ind(full(win), R(lst, a, b)))
+
+        def bank(x, a, b):
+            return R((("p_a", "p_d"), ("p_b", "p_n"))[x][a // 32 % 2], 16 * (a % 32), 16 * (a % 32 + b - a))
+
+        def lift(x, src):
+            return lambda q, a, b: mm(bank(x, a, b), R("idn"), C(src, a, b))
+
+        def larger(mx, x, src):
+            return lambda q, a, b: tt(C(mx, a, b), bank(x, a, b), C(src, a, b), Op.max)
+
+        def gain(mx, wgt):
+            return lambda q, a, b, flag="": [mm(R("p_g", 0, 20, 1, a, b), R(mx, 16 * a + k, 16 * b, 16), R(wgt), False,
+                                                flag == "stop" and k == 15) for k in range(16)]
+
+        def fused(mx, lst, src):
+            return lambda q, a, b: tt(C(mx, a, b), ind(full(Z), R(lst, a, b)), C(src, a, b), Op.max)
+
+        def diff(x, src, sub):
+            return lambda q, a, b: [mm(bank(x, a, b), R("idn"), C(src, a, b), True, False), mm(bank(x, a, b), R("idm"), C(sub, a, b), False, True)]
+
+        def relu(x, mx):
+            return lambda q, a, b: act(C(mx, a, b), bank(x, a, b), Fn.Relu)
+
+        def moved(q):
+            mm(R("p_t0", 0, 256), R("idn"), R("xg"), True, False)
+            mm(R("p_t0", 0, 256), R("idm"), R("zq"), False, True)
+
+        def places(q):
+            for o, k in (("mz", 16), ("my", 0)):
+                for r in range(2):
+                    act(R(o, 9 + 10 * r, 160, 20), R("l4f", k + 8 * r, k + 8 * r + 8), bias=float(NB))
+
+        def other(q):
+            if not last:
+                ts(R("a0"), R("l4f", 16, 24), -2047.5, Op.add, 2 * BIG, Op.mult)
+                tt(R("a1"), R("a0"), R("n6"), Op.min)
+                tt(R("av"), R("a1"), R("l4f", 8, 16), Op.max)
+                tt(R("mv", 19, 160, 20), R("l4f", 0, 8), R("av"), Op.subtract)
+
+        def lower(q, a, b):
+            for c in range(a // 16, 8):
+                mm(R("p_l", 20 * c, 20 * c + 20), R("tk", 128 * c, 128 * c + 128, 1, a, b), R("prop", 0, 20, 1, a, b), False, b == L and c == 7)
+
+        phase(GAINS, [
+            ("nba", lambda q: cp(q, R("nba"), ind(R("nbt"), A_))),
+            ("a", lambda q: cp(q, R("nm", 0, 256, 2), ind(R("idt"), A_))),
+            ("w", lambda q: cp(q, rW, ind(full("it"), Q_))),
+            ("p", lambda q: cp(q, rP, ind(full("mt"), A_))),
+            ("wl", lambda q: to_list(W_, rW, R("ws", 0, 128))),
+            ("pl", lambda q: to_list(P_, rP, R("ws", 128, 256))),
+            ("nzq", lambda q: cp(q, R("nzq"), ind(R("nzt"), Q_))),
+            ("nbw", lambda q: cp(q, R("nbw"), ind(R("nbt"), W_))),
+            ("nzp", lambda q: cp(q, R("nzp"), ind(R("nzt"), P_))),
+            ("names", names), ("same", same), ("sameT", same_turned),
+            ("qp", lambda q: cp(q, R("l4f", 16, 32), R("l4", 16, 32))),
+            ("tc0", lambda q: cp(q, R("tc", 0, 512), R("p_t0"))),
+            ("tc1", lambda q: cp(q, R("tc", 512, 1024), R("p_t1"))),
+            ("mask0", lambda q: mask(0)), ("mask1", lambda q: mask(1)),
+            ("A", fetch("ga", Y, "nba")), ("W", fetch("gw", Y, "nbw")), ("B", fetch("gb", Z, "nzp")), ("C", fetch("gc", Z, "nzq")),
+            [("cP", lift(0, "gc")), ("bP", lift(1, "gb")), ("m1", larger("m_1", 0, "ga")), ("m2", larger("m_2", 0, "gw")),
+             ("m3", larger("m_3", 1, "ga")), ("m4", larger("m_4", 1, "gw")),
+             ("d1", diff(0, "ga", "gc")), ("r1", relu(0, "m_1")), ("d2", diff(1, "gw", "gc")), ("r2", relu(1, "m_2")),
+             ("d3", diff(0, "ga", "gb")), ("r3", relu(0, "m_3")), ("d4", diff(1, "gw", "gb")), ("r4", relu(1, "m_4"))],
+            ("f1", fused("m_1", "nzq", "ga")), ("f2", fused("m_2", "nzq", "gw")),
+            ("f3", fused("m_3", "nzp", "ga")), ("f4", fused("m_4", "nzp", "gw")),
+            ("x", lambda q: cp(q, R("xg"), ind(R("xt"), R("l4", 0, 16)))),
+            ("zq", lambda q: cp(q, R("zq"), ind(full(Z), R("l4", 16, 32)))),
+            ("dz", moved),
+            ("sign", lambda q: act(R("sg"), R("p_t0", 0, 256), Fn.Sign)),
+            ("places", places), ("alt", other),
+            ("void", lambda q: [mm(R("p_g", 0, 20), R("idn"), R("ka", 32, 52), True, False)]
+             + [mm(R("p_g", 1 + 10 * r, 9 + 10 * r), R("idf"), R("void"), False, False) for r in range(2)]),
+            ("g1", gain("m_1", "gm")),
+            ("g2", gain("m_2", "gp")), ("g3", gain("m_3", "gp")), ("g4", gain("m_4", "gm")),
+            ("zero", lambda q: mm(R("p_l", 0, 160), R("idn"), R("ka", 32, 192), True, False)),
+            ("prop", lambda q, a, b: ts(R("prop", 0, 20, 1, a, b), R("p_g", 0, 20, 1, a, b), R("th", 0, 1, 1, a, b), Op.is_gt)),
+            ("lower", lower),
+        ])
+
+        def offsets(o, s, m):
+            scan(R(s), R("p_l", 0, 160), R(m), Op.max, Op.mult)
+            for r in range(2):
+                tt(R(o, 8 * r, 8 * r + 8), R(s, 9 + 10 * r, 160, 20), R("alt", 8 * r, 8 * r + 8), Op.max)
+
+        offsets("oz", "sz", "mz")
+        act(rQ, ind(R("idt"), Q_))
+        tt(ind(park(Zn), R("oz")), R("zq"), R("sg"), Op.add)
+        if not last:
+            act(rA, R("nm", 0, 256, 2))
             act(R("gz"), ind(own(Zn), R("bzl")))
             send("z", t + 1, R("gz"))
-            tc(ind(park(Yn), R("off", 16, 32)), R("zn"))
-            act(R("gy"), ind(own(Yn), R("bxl")))
-            send("y", t + 1, R("gy"))
-            tt(R("vl"), R("cm", 32, 40), R("alt", 32, 40), Op.add)
-            tt(R("vf"), R("cm", 32, 40), R("alt", 32, 40), Op.add)
         else:
             dma("Y", "d_zo", [(T.zo[:, :], own(Zn))])
-        tc(ind(park("mt"), R("off", 16, 24)), R("raq", 128, 256))
-        tc(ind(park("mt"), R("off", 24, 32)), R("wp", 128, 256))
-        if t == 1:
-            dma("Y", "d_z3", [(own("z3"), own("z2"))])
-            dma("Y", "d_y3", [(own("y3"), own("y2"))])
+        offsets("oy", "sy", "my")
+        if not last:
+            tt(ind(park(Yn), R("oy")), R("zq"), R("sg"), Op.add)
+            act(R("gy"), ind(own(Yn), R("bxl")))
+            send("y", t + 1, R("gy"))
+            scan(R("sv"), R("p_l", 0, 160), R("mv"), Op.max, Op.mult)
+        tc(ind(park("mt"), R("oy")), R("rw", 256, 512))
+        if not last:
+            tt(R("vl"), R("sv", 19, 160, 20), R("av"), Op.add)
     order("Y", [own("mt")], [], ("d_mo", 16))
     g.sync.dma_start(T.mo[:, :], T.mt[0:128:16, NB:NB + V]).then_inc(T.sem["d_mo"], 16)
     count["d_mo"] = 16
 
     for e in sorted(count):
-        if known["G"].get(e, 0) < count[e]:
-            g.wait_ge(T.sem[e], count[e])
+        wait("G", e, count[e])

@@ -7,24 +7,26 @@ KEY = 65536.0
 BIG = 4096.0
 EPS = 2.0 ** -20
 FAR = 2.0 ** 20
+OFF = 32.0
+WHOLE = 1.5 * 2 ** 23
 
 NAMING1 = {
-    "V": "mv mvl i2h|Z 64 128|im1 0 4|nbv1 0 64|Y 32 64|nbv1 64 128|im1 8 12|Y 96 128|Y 64 96|cat|max 96 128|next",
-    "S": "nzv|Z 0 64|im1 4 8|Y 0 32|abs 0 32|abs 32 64|abs 64 96|im1 12 16",
-    "P": "rank|imP 0 4|imP 4 8|imP 8 12|imP 12 16|zP 96 128|sumz 96 128|diff 0 32|diff 32 64|sum 0 32|sum 32 64|sumy 96 128|diff 64 96|catT|"
-         "summ 96 128|sum 64 96",
+    "V": "mv mvl nzv kn kp|Z 64 128|nbv1 0 64|Y 32 64|nbv1 64 128|Y 96 128|cat|max 96 128|max 64 96|next kg",
+    "S": "im1 0 1|im1 1 2|Z 0 64|Y 0 32|Y 64 96|abs 0 32|abs 32 64|im1 2 3|im1 3 4",
+    "P": "imP 0 1|imP 1 2|rank|imP 2 3|imP 3 4|zP 64 96|zP 96 128|sumz 64 128|diff 0 32|diff 32 64|sum 0 32|catT|sumy 64 128|sum 32 64|summ 64 128",
 }
 NAMING = {
-    "V": "mv mvl im cat|Z 64 128|Y 32 64|Y 64 96|Y 96 128|max 96 128|next th",
-    "S": "nbv nzv|Z 0 64|Y 0 32|abs 0 32|abs 32 64|abs 64 96",
+    "V": "oz newz oy newy sv vl newm mv mvl nzv cb cat|Z 64 128|Y 32 64|Y 64 96|Y 96 128|max 96 128|next th",
+    "S": "rq ra gz gy nbv|Z 0 64|Y 0 32|abs 0 32|abs 32 64|abs 64 96|im",
     "P": "count catT rank|zP 96 128|sumz 96 128|diff 0 32|diff 32 64|diff 64 96|sum 0 32|sum 32 64|sumy 96 128|sum 64 96|summ 96 128",
+    "G": "sendz sendy",
 }
 GAINS = {
     "V": "w wl names p same pl|f1 0 32|qp|f1 32 64|f1 64 128|f3 0 64|f2 64 128|f2 0 32|f4 0 32|f4 32 64|f2 32 64|alt|prop 0 128",
-    "S": "nba a|A 0 32|nzq|A 32 64|nbw|A 64 128|nzp|B 64 128|W 64 128|tc0|W 0 32|r3 64 96|r3 96 128|W 32 64|tc1|r4 64 96|r4 96 128|"
+    "S": "nba a|A 0 32|nzq|A 32 64|nbw|A 64 128|nzp|B 64 128|W 64 128|tc1|W 0 32|r3 64 96|r3 96 128|W 32 64|tc0|r4 64 96|r4 96 128|"
          "x zq places sign",
     "P": "void sameT zero|d3 64 96|d3 96 128|g1 0 128|d4 64 96|d4 96 128|g3 0 128|g4 0 128|g2 0 128 stop|dz|lower 0 128",
-    "G": "mask0 mask1",
+    "G": "mask1 mask0",
 }
 
 _B, _F, _H, _I, _U = "bfloat16", "float32", "float16", "int32", "uint16"
@@ -39,9 +41,9 @@ for _n, _w, _t in [
     ("gz", NB, _B), ("gy", NB, _B),
     ("ones", 1024, _B), ("idn", 128, _B), ("idm", 128, _B), ("ide", 128, _B), ("idf", 128, _B),
     ("gk", 8, _B), ("gk2", 8, _B), ("gkm", 8, _B), ("gp", 20, _B), ("gm", 20, _B),
-    ("ej", 2048, _B), ("bq", 128, _B), ("sel", 1024, _B), ("tb", 128, _B),
-    ("pi", 8, _I), ("pa", 8, _I), ("pf", 8, _F), ("cor0", 8, _F), ("cor", 8, _F), ("lk", 16, _F),
-    ("i16", 128, _F), ("g8", 128, _F), ("gq", 128, _F), ("p10", 160, _F), ("t0", 160, _F), ("t1", 160, _F),
+    ("ej", 2048, _B), ("e4", 512, _B), ("sel", 1024, _B), ("tb", 128, _B),
+    ("pi", 8, _I), ("pa", 8, _I), ("pf", 8, _F), ("cor0", 8, _F), ("cor", 8, _F), ("pq", 8, _F),
+    ("i16", 128, _F), ("g8", 128, _F), ("p10", 160, _F), ("t0", 160, _F), ("t1", 160, _F), ("t2", 160, _F),
     ("s8", 128, _F), ("s16", 128, _F), ("c1", 128, _F), ("mz", 160, _F), ("my", 160, _F), ("mv", 160, _F),
     ("li", 16, _F), ("alt", 16, _F),
     ("vl", 8, _U), ("mvr", 128, _F), ("mvs", 128, _F), ("mvl", 8, _U),
@@ -52,7 +54,7 @@ for _n, _w, _t in [
     ("nba", 128, _U), ("nzq", 128, _U), ("nbw", 128, _U), ("nzp", 128, _U),
     ("ga", 2048, _B), ("gw", 2048, _B), ("gb", 2048, _B), ("gc", 2048, _B),
     ("m_1", 2048, _B), ("m_2", 2048, _B), ("m_3", 2048, _B), ("m_4", 2048, _B),
-    ("ka", 2048, _B), ("kw", 2048, _B), ("tc", 1024, _B), ("tl", 1024, _B), ("tk", 1024, _B),
+    ("ka", 1152, _B), ("kw", 1152, _B), ("zero", 160, _B), ("tc", 1024, _B), ("tl", 1024, _B), ("tk", 1024, _B),
     ("xg", 256, _B), ("zq", 256, _B), ("sg", 256, _B),
     ("v0", 8, _F), ("v1", 8, _F), ("void", 8, _B), ("prop", 24, _B), ("th", 8, _F),
     ("sz", 160, _F), ("sy", 160, _F), ("sv", 160, _F), ("oz", 16, _U), ("oy", 16, _U),
@@ -82,8 +84,7 @@ def rank_program(g, core, T, topo):
     n = len(T.cores)
     dst = T.cores[(rank - 1) % n]
     rid, pid = topo.addr(dst)[:2]
-    nout = len(topo.engines(core, dst))
-    nin = len(topo.engines(T.cores[(rank + 1) % n], core))
+    src_core = T.cores[(rank + 1) % n]
 
     Q = {"V": g.vector, "S": g.scalar, "P": g.tensor, "G": g, "Y": g.sync}
     count = {"V": 0, "S": 0, "P": 0, "G": 0}
@@ -199,7 +200,10 @@ def rank_program(g, core, T, topo):
             q = [q for q in lines if lines[q] and all(b in done for b in before[q, lines[q][0]])][0]
             s = lines[q].pop(0)
             for c in calls[q, s]:
-                issue(*c)
+                if c[0] == "send":
+                    send(*c[3])
+                else:
+                    issue(*c)
             done.add((q, s))
 
     def val(s):
@@ -255,12 +259,16 @@ def rank_program(g, core, T, topo):
 
     def send(w, t, src):
         win = "%s%d" % (w, t)
+        if held:
+            held[-1].append(("send", [src], [R(win, NB + V, WIN)], (w, t, src)))
+            return
         snt, arr = "snt" + win, "arr" + win
-        order("G", [src], [], (snt, nout))
-        g.remote_dma(T[win][:, NB + V:WIN], ap(src), T.sem[arr], T.sem[snt], pid, rid, topo.mask(core, dst))
-        count[snt], count[arr] = nout, nin
-        acc.setdefault(win, {})[(arr, "w", R(win, NB + V, WIN))] = nin
-        clock[(arr, nin)] = {}
+        mine, theirs = topo.engines(core, dst), topo.engines(src_core, core)
+        order("G", [src], [], (snt, len(mine)))
+        g.remote_dma(T[win][:, NB + V:WIN], ap(src), T.sem[arr], T.sem[snt], pid, rid, sum(1 << e for e in mine))
+        count[snt], count[arr] = len(mine), len(theirs)
+        acc.setdefault(win, {})[(arr, "w", R(win, NB + V, WIN))] = len(theirs)
+        clock[(arr, len(theirs))] = {}
 
     def own(name):
         return R(name, NB, NB + V)
@@ -279,100 +287,123 @@ def rank_program(g, core, T, topo):
     dma("Y", "d_z", [(own("z1"), T.z[:, :])])
     dma("Y", "d_bx", [(R("bx32"), T.bx[:, :])])
     dma("Y", "d_m2", [(R("m2"), T.m[:, :])])
-    dma("Y", "d_nz", [(R("nzt", 0, V), T.nz[:, :])])
     dma("Y", "d_i2", [(R("i2"), T.im[:, :])])
+    dma("Y", "d_nz", [(R("nzt", 0, V), T.nz[:, :])])
 
     def load_nb(h):
         dma("Y", "d_nb%d" % h, [(R("nbt", 1024 * h, 1024 * h + 1024), T.nb[:, 1024 * h:1024 * h + 1024])])
 
     I_, IM, G_, GM = [R("pf", k, k + 1) for k in (0, 1, 4, 6)]
     iota(R("pi", 0, 4), [[112, 2], [15, 2]], 0, 1, False)
+    iota(R("pq", 0, 4), [[-4, 4]], 0, 1)
+    iota(R("e4"), [[1, 4], [16, 8], [0, 16]], 0, 0)
     iota(R("i16"), [[0, 8], [1, 16]], 0, 0)
-    iota(R("gq"), [[1, 8], [0, 16]], 0, 0)
-    iota(R("g8"), [[0, 16], [1, 8]], 0, 0)
     iota(R("li"), [[128, 2], [16, 8]], 0, 0)
-    iota(R("p10"), [[0, 16], [1, 10]], 0, 0)
+    iota(R("g8"), [[0, 16], [1, 8]], 0, 0)
     ms(R("ones"), 1.0)
     aff(R("idn"), R("ones", 0, 128), [[-1, 128]], Op.is_equal, 0.0, 0, 1)
-    for h in range(2):
-        act(R("kw", 1024 * h, 1024 * h + 1024), R("ones"), scale=0.0)
     ts(R("pa", 0, 4), R("pi", 0, 4), 15, Op.bitwise_and)
     ts(R("pa", 4, 8), R("pi", 0, 4), 4, Op.logical_shift_right, 7, Op.bitwise_and)
-    ms(R("ka"), 0.0)
+    ms(R("mt", NB + V), 0.0)
+    act(R("it", NB + V), R("ones", 0, PAD), Fn.Silu, scale=OFF)
+    ms(R("nzt", V), 0)
+    ms(R("nbt", V), 0)
+    ms(R("xt", V), 0.0)
+    ms(R("zero"), 0.0)
+    ms(R("th"), 0.0)
     tc(R("pf"), R("pa"))
-    ts(R("lk"), R("i16", 0, 16), I_, Op.is_equal)
-    ts(R("bq"), R("gq"), G_, Op.is_equal)
-    for k in range(16):
-        ts(R("ej", 128 * k, 128 * k + 128), R("bq"), R("lk", k, k + 1), Op.mult)
-    for h in range(2):
-        for b in range(4):
-            tc(R("mlh", 32 * b + 16 * h, 32 * b + 16 * h + 16), R("mr", 64 * h + 16 * b, 64 * h + 16 * b + 16))
-    tr(R("mlt"), R("mlh"))
-    tc(R("bzl"), R("bz32"))
-    for b in range(4):
-        tc(R("mlist", b, 128, 4), R("mlt", 32 * b, 32 * b + 32))
-    act(R("gz"), ind(own("z1"), R("bzl")))
-    send("z", 1, R("gz"))
-    tc(R("y1", NB, NB + 1152), ind(own("z1"), R("mlist", 0, 72)))
-    act(R("y1", NB + 1152, NB + V), ind(own("z1"), R("mlist", 72, 128)))
-    tc(R("bxl"), R("bx32"))
-    tc(R("m2h"), R("m2"))
-    act(R("gy"), ind(own("y1"), R("bxl")))
-    send("y", 1, R("gy"))
-    wait("Y", "S", count["S"])
-    for h in range(2):
-        load_nb(h)
+    ts(R("cor0", 0, 2), R("pf", 0, 8, 4), 0.0, Op.is_equal, 2 * BIG, Op.mult)
+    ts(R("cor", 0, 2), R("cor0", 0, 2), -BIG, Op.add)
+    C16, C8 = R("cor", 0, 1), R("cor", 1, 2)
 
-    def spread(half, tab):
-        for jb in range(4):
-            b = ("p_a", "p_b")[jb % 2]
-            for j in range(4):
-                J = 4 * jb + j
-                mm(R(b, 128 * j, 128 * j + 128), R("ej", 128 * J, 128 * J + 128), R(half))
-            act(R(tab, NB + 512 * jb, NB + 512 * jb + 512), R(b))
+    def rows(jb):
+        ts(R("ej", 512 * jb, 512 * jb + 512), R("e4"), R("pq", jb, jb + 1), Op.is_equal)
 
     def picks(o, it, at, before):
         ts(R("t0", 0, 128), R(it), at, Op.is_equal, BIG, Op.mult)
         ts(R("t1", 0, 128), R(it), before, Op.is_equal, -2 * BIG, Op.mult)
         tt(R(o), R("t0", 0, 128), R("t1", 0, 128), Op.add)
 
-    aff(R("sel"), R("ones"), [[-16, 8], [0, 8], [-1, 16]], Op.is_equal, 0.0, 0, 1)
-    iota(R("idt"), [[1, V + PAD]], 0, 0)
-    for tab in ("mt", "it"):
-        ms(R(tab, NB + V), 0.0)
-    ms(R("nbt", V), 0)
-    ms(R("nzt", V), 0)
-    ms(R("xt", V), 0.0)
+    rows(0)
+    tc(R("bzl"), R("bz32"))
+    for h in range(2):
+        for b in range(4):
+            tc(R("mlh", 32 * b + 16 * h, 32 * b + 16 * h + 16), R("mr", 64 * h + 16 * b, 64 * h + 16 * b + 16))
+    tr(R("mlt"), R("mlh"))
+    for b in range(4):
+        tc(R("mlist", b, 128, 4), R("mlt", 32 * b, 32 * b + 32))
+    rows(1)
+    act(R("gz"), ind(own("z1"), R("bzl")))
+    send("z", 1, R("gz"))
+    iota(R("p10"), [[0, 16], [1, 10]], 0, 0)
+    tc(R("y1", NB, NB + 1024), ind(own("z1"), R("mlist", 0, 64)))
+    act(R("y1", NB + 1024, NB + V), ind(own("z1"), R("mlist", 64, 128)))
+    tc(R("m2h"), R("m2"))
+    tc(R("bxl"), R("bx32"))
+    rows(2)
+    rows(3)
+    tc(R("i2h"), R("i2"))
     picks("s16", "i16", I_, IM)
-    ts(R("cor0", 0, 2), R("pf", 0, 8, 4), 0.0, Op.is_equal, 2 * BIG, Op.mult)
-    ts(R("cor", 0, 2), R("cor0", 0, 2), -BIG, Op.add)
-    C16, C8 = R("cor", 0, 1), R("cor", 1, 2)
     ts(R("alt"), R("li"), I_, Op.add)
     ts(R("vl"), R("alt", 0, 8), 16.0, Op.mult)
-    spread("m2h", "mt")
+    act(R("gy"), ind(own("y1"), R("bxl")))
+    send("y", 1, R("gy"))
+    wait("Y", "S", count["S"])
+    for h in range(2):
+        load_nb(h)
+    aff(R("sel"), R("ones"), [[-16, 8], [0, 8], [-1, 16]], Op.is_equal, 0.0, 0, 1)
+    iota(R("idt"), [[1, V + PAD]], 0, 0)
     wait("Y", "d_nb1", 16)
     dma("Y", "d_x", [(R("xt", 0, V), T.x[:, :])])
-    ts(R("gk"), R("g8", 0, 8), G_, Op.is_equal, KEY, Op.mult)
-    ts(R("gk2"), R("g8", 0, 8), G_, Op.is_equal, 2 * KEY, Op.mult)
-    ts(R("gkm"), R("g8", 0, 8), G_, Op.is_equal, -KEY, Op.mult)
-    ts(R("tb"), R("i16"), -32.0, Op.mult, 480.0, Op.add)
-    ts(R("t0", 0, 128), R("i16"), 0.0, Op.not_equal, 2.0 ** 30, Op.mult)
-    ts(R("c1"), R("t0", 0, 128), -1.0, Op.add)
-    picks("s8", "g8", G_, GM)
-    ts(R("t0"), R("p10"), -1.0, Op.add, G_, Op.is_equal)
-    ts(R("gp"), R("t0", 0, 20), 2.0, Op.mult)
-    ts(R("gm"), R("t0", 0, 20), -2.0, Op.mult)
-    ts(R("t1"), R("t0"), 1 / EPS - 1, Op.mult)
-    ts(R("t0"), R("p10"), G_, Op.not_equal)
-    for o in ("mz", "my", "mv"):
-        tt(R(o), R("t0"), R("t1"), Op.add)
-    for o, s in (("idm", -1.0), ("ide", -EPS), ("idf", -FAR)):
-        ts(R(o), R("idn"), s, Op.mult)
-    ms(R("th"), 0.0)
 
-    def to_list(o, row, tmp):
+    def plus(q, o, i, c):
+        if q == "V":
+            ts(o, i, c, Op.add)
+        else:
+            act(o, i, bias=c)
+
+    def spread(q, half, tab, off, bk, jb):
+        if q == "P":
+            for j in range(4):
+                mm(R(bk, 128 * j, 128 * j + 128), R("ej", 512 * jb + 128 * j, 512 * jb + 128 * j + 128), R(half))
+        else:
+            plus(q, R(tab, NB + 512 * jb, NB + 512 * jb + 512), R(bk), off)
+
+    for jb, bk in enumerate(("p_a", "p_b", "p_t0", "p_t1")):
+        spread("P", "m2h", "mt", 0.0, bk, jb)
+        spread("SSVV"[jb], "m2h", "mt", 0.0, bk, jb)
+
+    def naming_constants(q):
+        ts(R("gk"), R("g8", 0, 8), G_, Op.is_equal, KEY, Op.mult)
+        ts(R("gk2"), R("g8", 0, 8), G_, Op.is_equal, 2 * KEY, Op.mult)
+        ts(R("gkm"), R("g8", 0, 8), G_, Op.is_equal, -KEY, Op.mult)
+        ts(R("tb"), R("i16"), -32.0, Op.mult, 480.0, Op.add)
+        ts(R("idm"), R("idn"), -1.0, Op.mult)
+
+    def pick_constants(q):
+        picks("s8", "g8", G_, GM)
+        ts(R("c1"), R("i16"), 0.0, Op.not_equal)
+
+    def gain_constants(q):
+        ts(R("t0"), R("p10"), -1.0, Op.add, G_, Op.is_equal)
+        ts(R("t2"), R("p10"), G_, Op.not_equal)
+        ts(R("t1"), R("t0"), 1 / EPS - 1, Op.mult)
+        ts(R("gp"), R("t0", 0, 20), 2.0, Op.mult)
+        ts(R("gm"), R("t0", 0, 20), -2.0, Op.mult)
+        tt(R("mz"), R("t2"), R("t1"), Op.add)
+        for o, s in (("ide", -EPS), ("idf", -FAR)):
+            ts(R(o), R("idn"), s, Op.mult)
+        for o in ("my", "mv"):
+            tc(R(o), R("mz"))
+
+    def to_list(o, row, tmp, shift=0.0):
         scan(tmp, row, R("s16"), Op.max, Op.add)
-        ts(o, (tmp[0], 0, 128, tmp[3] + 15, tmp[4], 16), C16, Op.add)
+        ts(o, (tmp[0], 0, 128, tmp[3] + 15, tmp[4], 16), C16, Op.add, shift, Op.add)
+
+    def offsets(o, s, m):
+        scan(R(s), R("p_l", 0, 160), R(m), Op.max, Op.mult)
+        for r in range(2):
+            tt(R(o, 8 * r, 8 * r + 8), R(s, 9 + 10 * r, 160, 20), R("alt", 8 * r, 8 * r + 8), Op.max)
 
     A_, W_, Q_, P_ = [R("l4", 8 * k, 8 * k + 8) for k in range(4)]
     rA, rW, rQ, rP = [R("rw", 128 * k, 128 * k + 128) for k in range(4)]
@@ -385,18 +416,12 @@ def rank_program(g, core, T, topo):
         def nbv1(q, a, b):
             cp(q, R("nbv", a, b), R("nbt", 16 * a, 16 * b, 16))
 
-        def im1(q, a, b):
-            bk = ("p_g", "p_l")[a // 4 % 2]
-            if q == "P":
-                for J in range(a, b):
-                    mm(R(bk, 128 * (J - a), 128 * (J - a + 1)), R("ej", 128 * J, 128 * J + 128), R("i2h"))
-            else:
-                cp(q, R("it", NB + 128 * a, NB + 128 * b), R(bk))
-
         def im(q):
-            if not first:
+            if q == "V":
                 tc(ind(park("it"), R("oz")), R("rw", 0, 256))
-                ts(R("cb"), R("sv", 9, 160, 20), 0.5, Op.is_ge)
+            else:
+                run("S", [ind(park("it"), R("oz"))], [R("rw", 0, 256)],
+                    lambda e: e.activation(ap(ind(park("it"), R("oz"))), ap(R("rw", 0, 256)), Fn.Silu))
 
         def th(q):
             if not first:
@@ -418,14 +443,29 @@ def rank_program(g, core, T, topo):
                 ts(R("n6"), R("n5"), 2047, Op.bitwise_and)
 
         phase(NAMING1 if first else NAMING, [
-            ("i2h", lambda q: cp(q, R("i2h"), R("i2"))),
-            [("imP", im1), ("im1", im1)],
+            ("kn", naming_constants), ("kp", pick_constants), ("kg", gain_constants),
+            [("imP", lambda q, a, b: spread(q, "i2h", "it", OFF, ("p_g", "p_l")[a % 2], a)),
+             ("im1", lambda q, a, b: spread(q, "i2h", "it", OFF, ("p_g", "p_l")[a % 2], a))],
+            ("oz", lambda q: offsets("oz", "sz", "mz")),
+            ("oy", lambda q: offsets("oy", "sy", "my")),
+            ("rq", lambda q: cp(q, rQ, ind(R("idt"), Q_))),
+            ("ra", lambda q: plus(q, rA, R("nm", 0, 256, 2), OFF)),
+            ("newz", lambda q: tt(ind(park(Z), R("oz")), R("zq"), R("sg"), Op.add)),
+            ("newy", lambda q: tt(ind(park(Y), R("oy")), R("zq"), R("sg"), Op.add)),
+            ("gz", lambda q: cp(q, R("gz"), ind(own(Z), R("bzl")))),
+            ("gy", lambda q: cp(q, R("gy"), ind(own(Y), R("bxl")))),
+            ("sendz", lambda q: send("z", t, R("gz"))),
+            ("sendy", lambda q: send("y", t, R("gy"))),
+            ("sv", lambda q: scan(R("sv"), R("p_l", 0, 160), R("mv"), Op.max, Op.mult)),
+            ("vl", lambda q: tt(R("vl"), R("sv", 19, 160, 20), R("av"), Op.add)),
+            ("newm", lambda q: tc(ind(park("mt"), R("oy")), R("rw", 256, 512))),
             ("mv", lambda q: cp(q, R("mvr"), ind(full("mt"), R("vl")))),
             ("mvl", lambda q: to_list(R("mvl"), R("mvr"), R("mvs"))),
             ("nbv1", nbv1),
             ("nbv", lambda q: first or cp(q, R("nbv"), ind(R("nbt"), R("vl")))),
             ("nzv", lambda q: cp(q, R("nzv"), ind(R("nzt"), R("mvl")))),
             ("im", im),
+            ("cb", lambda q: ts(R("cb"), R("sv", 9, 160, 20), 0.5, Op.is_ge)),
             ("count", lambda q: first or mm(R("p_l", 200, 208), R("ones", 0, 128), R("cb"))),
             ("th", th),
             ("cat", lambda q: [ts(R("cat", 128 * x, 128 * x + 128), R(s), 2048.0, Op.min) for x, s in enumerate(("nbv", "nzv"))]),
@@ -447,10 +487,10 @@ def rank_program(g, core, T, topo):
             ("next", fallback),
         ])
         if not last:
-            wait("Y", "snt" + Y, nout)
+            wait("Y", "snt" + Y, count["snt" + Y])
             dma("Y", "d_" + Zn, [(own(Zn), own(Z))])
             dma("Y", "d_" + Yn, [(own(Yn), own(Y))])
-        scan(R("mx"), R("c1"), R("p_d", 0, 128), Op.min, Op.max)
+        scan(R("mx"), R("c1"), R("p_d", 0, 128), Op.mult, Op.max)
         tt(R("gap"), R("mx"), R("p_d", 0, 128), Op.subtract)
         for x in range(2):
             tt(R("d1", 128 * x, 128 * x + 128), R("p_n", 128 * x, 128 * x + 128), R("gap"), Op.subtract)
@@ -467,18 +507,20 @@ def rank_program(g, core, T, topo):
 
         def names(q):
             cp(q, R("l4f", 0, 16), R("l4", 0, 16))
-            cp(q, R("nm", 1, 256, 2), rW)
+            ts(R("nm", 1, 256, 2), rW, WHOLE - OFF, Op.add, WHOLE, Op.subtract)
 
         def same(q):
-            for c in range(8):
+            for c in reversed(range(8)):
+                at = 16 * c * (c + 1)
                 for kk, s in (("ka", c), ("kw", 8 + c)):
-                    ts(R(kk, 256 * c, 256 * c + 32 * (c + 1)), R("nm", 0, 32 * (c + 1)), R("l4f", s, s + 1), Op.is_equal)
+                    ts(R(kk, at, at + 32 * (c + 1)), R("nm", 0, 32 * (c + 1)), R("l4f", s, s + 1), Op.is_equal)
 
         def same_turned(q):
-            for c in range(8):
+            for c in reversed(range(8)):
                 o = R("p_t%d" % (c // 4), 128 * (c % 4), 128 * (c % 4) + 128)
+                at = 16 * c * (c + 1)
                 for x, (kk, y) in enumerate((("ka", 0), ("ka", 1), ("kw", 0), ("kw", 1))):
-                    mm(o, R(kk, 256 * c + y, 256 * c + 256, 2), R("ide"), x == 0, x == 3)
+                    mm(o, R(kk, at + y, at + 256, 2), R("ide"), x == 0, x == 3)
 
         def mask(x):
             h = (512 * x, 512 * x + 512)
@@ -517,7 +559,7 @@ def rank_program(g, core, T, topo):
         def places(q):
             for o, k in (("mz", 16), ("my", 0)):
                 for r in range(2):
-                    act(R(o, 9 + 10 * r, 160, 20), R("l4f", k + 8 * r, k + 8 * r + 8), bias=float(NB))
+                    plus(q, R(o, 9 + 10 * r, 160, 20), R("l4f", k + 8 * r, k + 8 * r + 8), float(NB))
 
         def other(q):
             if not last:
@@ -535,7 +577,7 @@ def rank_program(g, core, T, topo):
             ("a", lambda q: cp(q, R("nm", 0, 256, 2), ind(R("idt"), A_))),
             ("w", lambda q: cp(q, rW, ind(full("it"), Q_))),
             ("p", lambda q: cp(q, rP, ind(full("mt"), A_))),
-            ("wl", lambda q: to_list(W_, rW, R("ws", 0, 128))),
+            ("wl", lambda q: to_list(W_, rW, R("ws", 0, 128), 0.25 - OFF)),
             ("pl", lambda q: to_list(P_, rP, R("ws", 128, 256))),
             ("nzq", lambda q: cp(q, R("nzq"), ind(R("nzt"), Q_))),
             ("nbw", lambda q: cp(q, R("nbw"), ind(R("nbt"), W_))),
@@ -557,38 +599,21 @@ def rank_program(g, core, T, topo):
             ("dz", moved),
             ("sign", lambda q: act(R("sg"), R("p_t0", 0, 256), Fn.Sign)),
             ("places", places), ("alt", other),
-            ("void", lambda q: [mm(R("p_g", 0, 20), R("idn"), R("ka", 32, 52), True, False)]
+            ("void", lambda q: [mm(R("p_g", 0, 20), R("idn"), R("zero", 0, 20), True, False)]
              + [mm(R("p_g", 1 + 10 * r, 9 + 10 * r), R("idf"), R("void"), False, False) for r in range(2)]),
             ("g1", gain("m_1", "gm")),
             ("g2", gain("m_2", "gp")), ("g3", gain("m_3", "gp")), ("g4", gain("m_4", "gm")),
-            ("zero", lambda q: mm(R("p_l", 0, 160), R("idn"), R("ka", 32, 192), True, False)),
+            ("zero", lambda q: mm(R("p_l", 0, 160), R("idn"), R("zero"), True, False)),
             ("prop", lambda q, a, b: ts(R("prop", 0, 20, 1, a, b), R("p_g", 0, 20, 1, a, b), R("th", 0, 1, 1, a, b), Op.is_gt)),
             ("lower", lower),
         ])
 
-        def offsets(o, s, m):
-            scan(R(s), R("p_l", 0, 160), R(m), Op.max, Op.mult)
-            for r in range(2):
-                tt(R(o, 8 * r, 8 * r + 8), R(s, 9 + 10 * r, 160, 20), R("alt", 8 * r, 8 * r + 8), Op.max)
-
-        offsets("oz", "sz", "mz")
-        act(rQ, ind(R("idt"), Q_))
-        tt(ind(park(Zn), R("oz")), R("zq"), R("sg"), Op.add)
-        if not last:
-            act(rA, R("nm", 0, 256, 2))
-            act(R("gz"), ind(own(Zn), R("bzl")))
-            send("z", t + 1, R("gz"))
-        else:
-            dma("Y", "d_zo", [(T.zo[:, :], own(Zn))])
-        offsets("oy", "sy", "my")
-        if not last:
-            tt(ind(park(Yn), R("oy")), R("zq"), R("sg"), Op.add)
-            act(R("gy"), ind(own(Yn), R("bxl")))
-            send("y", t + 1, R("gy"))
-            scan(R("sv"), R("p_l", 0, 160), R("mv"), Op.max, Op.mult)
-        tc(ind(park("mt"), R("oy")), R("rw", 256, 512))
-        if not last:
-            tt(R("vl"), R("sv", 19, 160, 20), R("av"), Op.add)
+    offsets("oz", "sz", "mz")
+    act(rQ, ind(R("idt"), Q_))
+    tt(ind(park(Z), R("oz")), R("zq"), R("sg"), Op.add)
+    dma("Y", "d_zo", [(T.zo[:, :], own(Z))])
+    offsets("oy", "sy", "my")
+    tc(ind(park("mt"), R("oy")), R("rw", 256, 512))
     order("Y", [own("mt")], [], ("d_mo", 16))
     g.sync.dma_start(T.mo[:, :], T.mt[0:128:16, NB:NB + V]).then_inc(T.sem["d_mo"], 16)
     count["d_mo"] = 16

@@ -11,19 +11,19 @@ OFF = 32.0
 WHOLE = 1.5 * 2 ** 23
 
 NAMING1 = {
-    "V": "mv mvl nzv kn kp|Z 64 128|nbv1 0 64|Y 32 64|nbv1 64 128|Y 96 128|cat|max 96 128|max 64 96|next kg",
-    "S": "im1 0 1|im1 1 2|Z 0 64|Y 0 32|Y 64 96|abs 0 32|abs 32 64|im1 2 3|im1 3 4",
-    "P": "imP 0 1|imP 1 2|rank|imP 2 3|imP 3 4|zP 64 96|zP 96 128|sumz 64 128|diff 0 32|diff 32 64|sum 0 32|catT|sumy 64 128|sum 32 64|summ 64 128",
+    "V": "gk mv mvs mvl nzv kp|Z 64 128|nbv1 0 64|Y 32 64|nbv1 64 128|Y 96 128|max 96 128|max 64 96|kg|im1 3 4|n6",
+    "S": "wn|im1 0 1|Z 0 64|im1 1 2|Y 0 32|Y 64 96|cat|abs 0 32|abs 32 64|n5|im1 2 3|wg",
+    "P": "imP 0 1|imP 1 2|rank|imP 2 3|imP 3 4|zP 64 96|zP 96 128|sumz 64 128|diff 0 32|diff 32 64|catT|sum 0 32|sumy 64 128|sum 32 64|summ 64 128",
 }
 NAMING = {
-    "V": "oz newz oy newy sv vl newm mv mvl nzv cb cat|Z 64 128|Y 32 64|Y 64 96|Y 96 128|max 96 128|next th",
-    "S": "rq ra gz gy nbv|Z 0 64|Y 0 32|abs 0 32|abs 32 64|abs 64 96|im",
-    "P": "count catT rank|zP 96 128|sumz 96 128|diff 0 32|diff 32 64|diff 64 96|sum 0 32|sum 32 64|sumy 96 128|sum 64 96|summ 96 128",
+    "V": "sz oz newz sy sv oy vl newy newm mv mvs mvl nzv|Z 64 128|dY 64 128|relu 64 128|max 32 64|n6",
+    "S": "rq ra gz gy nbv cb n5 th cat|Z 0 64|Y 0 32|Y 32 64|abs 0 32|im",
+    "P": "count catT rank|zP 32 64|sumz 32 64|diff 0 32|sumy 64 128|sumy 32 64|sum 0 32|summ 64 128|summ 32 64",
     "G": "sendz sendy",
 }
 GAINS = {
-    "V": "w wl names p same pl|f1 0 32|qp|f1 32 64|f1 64 128|f3 0 64|f2 64 128|f2 0 32|f4 0 32|f4 32 64|f2 32 64|alt|prop 0 128",
-    "S": "nba a|A 0 32|nzq|A 32 64|nbw|A 64 128|nzp|B 64 128|W 64 128|tc1|W 0 32|r3 64 96|r3 96 128|W 32 64|tc0|r4 64 96|r4 96 128|"
+    "V": "w p ws ps nm wl pl aw same|f1 0 32|f1 32 64|f1 64 128|f3 0 64|f2 64 128|f2 0 32|f4 0 32|f4 32 64|f2 32 64|a1 av dv|prop 0 128",
+    "S": "nba a|A 0 32|nzq|A 32 64|nbw|A 64 128|nzp|W 64 128|B 64 128|tc1|W 0 32|tc0|r3 64 96|W 32 64|r3 96 128|a0|r4 64 96|r4 96 128|"
          "x zq places sign",
     "P": "void sameT zero|d3 64 96|d3 96 128|g1 0 128|d4 64 96|d4 96 128|g3 0 128|g4 0 128|g2 0 128 stop|dz|lower 0 128",
     "G": "mask1 mask0",
@@ -39,7 +39,7 @@ for _n, _w, _t in [
     ("m2", 128, _I), ("i2", 128, _I), ("m2h", 128, _H), ("i2h", 128, _H),
     ("bx32", 16, _I), ("bz32", 16, _I), ("bxl", 16, _U), ("bzl", 16, _U),
     ("gz", NB, _B), ("gy", NB, _B),
-    ("ones", 1024, _B), ("idn", 128, _B), ("idm", 128, _B), ("ide", 128, _B), ("idf", 128, _B),
+    ("ones", 1024, _B), ("idn", 128, _B), ("idm", 128, _B), ("ide", 128, _B), ("id3", 128, _B), ("idf", 128, _B),
     ("gk", 8, _B), ("gk2", 8, _B), ("gkm", 8, _B), ("gp", 20, _B), ("gm", 20, _B),
     ("ej", 2048, _B), ("e4", 512, _B), ("sel", 1024, _B), ("tb", 128, _B),
     ("pi", 8, _I), ("pa", 8, _I), ("pf", 8, _F), ("cor0", 8, _F), ("cor", 8, _F), ("pq", 8, _F),
@@ -54,9 +54,9 @@ for _n, _w, _t in [
     ("nba", 128, _U), ("nzq", 128, _U), ("nbw", 128, _U), ("nzp", 128, _U),
     ("ga", 2048, _B), ("gw", 2048, _B), ("gb", 2048, _B), ("gc", 2048, _B),
     ("m_1", 2048, _B), ("m_2", 2048, _B), ("m_3", 2048, _B), ("m_4", 2048, _B),
-    ("ka", 1152, _B), ("kw", 1152, _B), ("zero", 160, _B), ("tc", 1024, _B), ("tl", 1024, _B), ("tk", 1024, _B),
+    ("ka", 1152, _B), ("kw", 1152, _B), ("zero", 160, _B), ("tc", 1024, _B), ("tk", 1024, _B),
     ("xg", 256, _B), ("zq", 256, _B), ("sg", 256, _B),
-    ("v0", 8, _F), ("v1", 8, _F), ("void", 8, _B), ("prop", 24, _B), ("th", 8, _F),
+    ("void", 24, _B), ("cs", 8, _F), ("prop", 24, _B), ("th", 8, _F),
     ("sz", 160, _F), ("sy", 160, _F), ("sv", 160, _F), ("oz", 16, _U), ("oy", 16, _U),
     ("n5", 8, _I), ("n6", 8, _I), ("a0", 8, _F), ("a1", 8, _F), ("av", 8, _F), ("cb", 8, _B),
     ("cn", 8, _F), ("cq", 8, _I),
@@ -304,13 +304,9 @@ def rank_program(g, core, T, topo):
     aff(R("idn"), R("ones", 0, 128), [[-1, 128]], Op.is_equal, 0.0, 0, 1)
     ts(R("pa", 0, 4), R("pi", 0, 4), 15, Op.bitwise_and)
     ts(R("pa", 4, 8), R("pi", 0, 4), 4, Op.logical_shift_right, 7, Op.bitwise_and)
-    ms(R("mt", NB + V), 0.0)
     act(R("it", NB + V), R("ones", 0, PAD), Fn.Silu, scale=OFF)
+    ms(R("mt", NB + V), 0.0)
     ms(R("nzt", V), 0)
-    ms(R("nbt", V), 0)
-    ms(R("xt", V), 0.0)
-    ms(R("zero"), 0.0)
-    ms(R("th"), 0.0)
     tc(R("pf"), R("pa"))
     ts(R("cor0", 0, 2), R("pf", 0, 8, 4), 0.0, Op.is_equal, 2 * BIG, Op.mult)
     ts(R("cor", 0, 2), R("cor0", 0, 2), -BIG, Op.add)
@@ -328,21 +324,19 @@ def rank_program(g, core, T, topo):
     tc(R("bzl"), R("bz32"))
     for h in range(2):
         for b in range(4):
-            tc(R("mlh", 32 * b + 16 * h, 32 * b + 16 * h + 16), R("mr", 64 * h + 16 * b, 64 * h + 16 * b + 16))
+            cp("VVVVVVSS"[4 * h + b], R("mlh", 32 * b + 16 * h, 32 * b + 16 * h + 16), R("mr", 64 * h + 16 * b, 64 * h + 16 * b + 16))
     tr(R("mlt"), R("mlh"))
     for b in range(4):
         tc(R("mlist", b, 128, 4), R("mlt", 32 * b, 32 * b + 32))
-    rows(1)
     act(R("gz"), ind(own("z1"), R("bzl")))
     send("z", 1, R("gz"))
     iota(R("p10"), [[0, 16], [1, 10]], 0, 0)
     tc(R("y1", NB, NB + 1024), ind(own("z1"), R("mlist", 0, 64)))
     act(R("y1", NB + 1024, NB + V), ind(own("z1"), R("mlist", 64, 128)))
-    tc(R("m2h"), R("m2"))
     tc(R("bxl"), R("bx32"))
-    rows(2)
-    rows(3)
-    tc(R("i2h"), R("i2"))
+    tc(R("m2h"), R("m2"))
+    for jb in range(1, 4):
+        rows(jb)
     picks("s16", "i16", I_, IM)
     ts(R("alt"), R("li"), I_, Op.add)
     ts(R("vl"), R("alt", 0, 8), 16.0, Op.mult)
@@ -371,14 +365,28 @@ def rank_program(g, core, T, topo):
 
     for jb, bk in enumerate(("p_a", "p_b", "p_t0", "p_t1")):
         spread("P", "m2h", "mt", 0.0, bk, jb)
-        spread("SSVV"[jb], "m2h", "mt", 0.0, bk, jb)
+        spread("SSSV"[jb], "m2h", "mt", 0.0, bk, jb)
 
-    def naming_constants(q):
-        ts(R("gk"), R("g8", 0, 8), G_, Op.is_equal, KEY, Op.mult)
-        ts(R("gk2"), R("g8", 0, 8), G_, Op.is_equal, 2 * KEY, Op.mult)
-        ts(R("gkm"), R("g8", 0, 8), G_, Op.is_equal, -KEY, Op.mult)
-        ts(R("tb"), R("i16"), -32.0, Op.mult, 480.0, Op.add)
-        ts(R("idm"), R("idn"), -1.0, Op.mult)
+    def naming_weights(q):
+        act(R("i2h"), R("i2"))
+        act(R("gk2"), R("gk"), scale=2.0)
+        act(R("gkm"), R("gk"), scale=-1.0)
+        act(R("tb"), R("i16"), bias=480.0, scale=-32.0)
+        act(R("idm"), R("idn"), scale=-1.0)
+
+    def gain_weights(q):
+        for o, s in (("ide", -EPS), ("id3", 3 * EPS), ("idf", -16 * FAR)):
+            act(R(o), R("idn"), scale=s)
+        for o in (R("nbt", V), R("zero")):
+            act(o, R("ones", 0, o[4] - o[3]), scale=0.0)
+
+    def commit_weights():
+        for o, s in (("gp", 2.0), ("gm", -2.0)):
+            ts(R(o), R("t0", 0, 20), s, Op.mult)
+        for o in ("my", "mv"):
+            act(R(o), R("mz"))
+        for o in (R("xt", V), R("th")):
+            ms(o, 0.0)
 
     def pick_constants(q):
         picks("s8", "g8", G_, GM)
@@ -388,20 +396,18 @@ def rank_program(g, core, T, topo):
         ts(R("t0"), R("p10"), -1.0, Op.add, G_, Op.is_equal)
         ts(R("t2"), R("p10"), G_, Op.not_equal)
         ts(R("t1"), R("t0"), 1 / EPS - 1, Op.mult)
-        ts(R("gp"), R("t0", 0, 20), 2.0, Op.mult)
-        ts(R("gm"), R("t0", 0, 20), -2.0, Op.mult)
         tt(R("mz"), R("t2"), R("t1"), Op.add)
-        for o, s in (("ide", -EPS), ("idf", -FAR)):
-            ts(R(o), R("idn"), s, Op.mult)
-        for o in ("my", "mv"):
-            tc(R(o), R("mz"))
 
-    def to_list(o, row, tmp, shift=0.0):
+    def own_row(tmp, row):
         scan(tmp, row, R("s16"), Op.max, Op.add)
+
+    def to_list(o, tmp, shift=0.0):
         ts(o, (tmp[0], 0, 128, tmp[3] + 15, tmp[4], 16), C16, Op.add, shift, Op.add)
 
-    def offsets(o, s, m):
+    def own_group(s, m):
         scan(R(s), R("p_l", 0, 160), R(m), Op.max, Op.mult)
+
+    def offsets(o, s):
         for r in range(2):
             tt(R(o, 8 * r, 8 * r + 8), R(s, 9 + 10 * r, 160, 20), R("alt", 8 * r, 8 * r + 8), Op.max)
 
@@ -424,11 +430,11 @@ def rank_program(g, core, T, topo):
                     lambda e: e.activation(ap(ind(park("it"), R("oz"))), ap(R("rw", 0, 256)), Fn.Silu))
 
         def th(q):
-            if not first:
-                run("V", [R("cn", 0, 1)], [R("p_l", 200, 208)],
-                    lambda e: e.tensor_reduce(ap(R("cn", 0, 1)), ap(R("p_l", 200, 208)), AxisListType.X, Op.add))
-                ts(R("cq", 0, 1), R("cn", 0, 1), 1.0 / 32, Op.mult, -31.0 / 64, Op.add)
-                ts(R("th", 0, 1), R("cq", 0, 1), -32.0, Op.mult, R("cn", 0, 1), Op.add)
+            cn, cq = R("cn", 0, 1), R("cq", 0, 1)
+            run("S", [R("cs"), cn], [R("p_l", 200, 208)],
+                lambda e: e.activation(ap(R("cs")), ap(R("p_l", 200, 208)), Fn.Copy, 0.0, 1.0, accum_out=ap(cn)))
+            act(cq, cn, bias=-31.0 / 64, scale=1.0 / 32)
+            run("S", [R("th", 0, 1)], [cq, cn], lambda e: e.activation(ap(R("th", 0, 1)), ap(cq), Fn.Identity, ap(cn), -32.0))
 
         def sums(src, wgt, a, b, stop):
             for k in range(16):
@@ -437,17 +443,14 @@ def rank_program(g, core, T, topo):
         def nbank(a, b):
             return R(("p_a", "p_b", "p_t0", "p_t1")[a // 32], 16 * (a % 32), 16 * (a % 32 + b - a))
 
-        def fallback(q):
-            if not last:
-                ts(R("n5"), R("vl"), 5.0, Op.mult, 1.0, Op.add)
-                ts(R("n6"), R("n5"), 2047, Op.bitwise_and)
 
         phase(NAMING1 if first else NAMING, [
-            ("kn", naming_constants), ("kp", pick_constants), ("kg", gain_constants),
+            ("gk", lambda q: ts(R("gk"), R("g8", 0, 8), G_, Op.is_equal, KEY, Op.mult)),
+            ("wn", naming_weights), ("kp", pick_constants), ("kg", gain_constants), ("wg", gain_weights),
             [("imP", lambda q, a, b: spread(q, "i2h", "it", OFF, ("p_g", "p_l")[a % 2], a)),
              ("im1", lambda q, a, b: spread(q, "i2h", "it", OFF, ("p_g", "p_l")[a % 2], a))],
-            ("oz", lambda q: offsets("oz", "sz", "mz")),
-            ("oy", lambda q: offsets("oy", "sy", "my")),
+            ("sz", lambda q: own_group("sz", "mz")), ("oz", lambda q: offsets("oz", "sz")),
+            ("sy", lambda q: own_group("sy", "my")), ("oy", lambda q: offsets("oy", "sy")),
             ("rq", lambda q: cp(q, rQ, ind(R("idt"), Q_))),
             ("ra", lambda q: plus(q, rA, R("nm", 0, 256, 2), OFF)),
             ("newz", lambda q: tt(ind(park(Z), R("oz")), R("zq"), R("sg"), Op.add)),
@@ -456,19 +459,19 @@ def rank_program(g, core, T, topo):
             ("gy", lambda q: cp(q, R("gy"), ind(own(Y), R("bxl")))),
             ("sendz", lambda q: send("z", t, R("gz"))),
             ("sendy", lambda q: send("y", t, R("gy"))),
-            ("sv", lambda q: scan(R("sv"), R("p_l", 0, 160), R("mv"), Op.max, Op.mult)),
+            ("sv", lambda q: own_group("sv", "mv")),
             ("vl", lambda q: tt(R("vl"), R("sv", 19, 160, 20), R("av"), Op.add)),
             ("newm", lambda q: tc(ind(park("mt"), R("oy")), R("rw", 256, 512))),
             ("mv", lambda q: cp(q, R("mvr"), ind(full("mt"), R("vl")))),
-            ("mvl", lambda q: to_list(R("mvl"), R("mvr"), R("mvs"))),
+            ("mvs", lambda q: own_row(R("mvs"), R("mvr"))), ("mvl", lambda q: to_list(R("mvl"), R("mvs"))),
             ("nbv1", nbv1),
             ("nbv", lambda q: first or cp(q, R("nbv"), ind(R("nbt"), R("vl")))),
             ("nzv", lambda q: cp(q, R("nzv"), ind(R("nzt"), R("mvl")))),
             ("im", im),
-            ("cb", lambda q: ts(R("cb"), R("sv", 9, 160, 20), 0.5, Op.is_ge)),
+            ("cb", lambda q: cp(q, R("cb"), R("sv", 9, 160, 20))),
             ("count", lambda q: first or mm(R("p_l", 200, 208), R("ones", 0, 128), R("cb"))),
             ("th", th),
-            ("cat", lambda q: [ts(R("cat", 128 * x, 128 * x + 128), R(s), 2048.0, Op.min) for x, s in enumerate(("nbv", "nzv"))]),
+            ("cat", lambda q: [cp(q, R("cat", 128 * x, 128 * x + 128), R(s)) for x, s in enumerate(("nbv", "nzv"))]),
             ("catT", lambda q: [mm(R("p_n", 128 * x, 128 * x + 128), R("cat", 128 * x, 128 * x + 128), R("idn")) for x in range(2)]),
             ("rank", lambda q: mm(R("p_d", 0, 128), R("ones", 0, 128), R("tb"), True, False)),
             ("Z", lambda q, a, b: cp(q, C("zg", a, b), ind(full(Z), R("nzv", a, b)))),
@@ -484,7 +487,8 @@ def rank_program(g, core, T, topo):
             ("sumz", lambda q, a, b: sums("zg", "gkm", a, b, False)),
             ("sumy", lambda q, a, b: sums("yg", "gkm", a, b, False)),
             ("summ", lambda q, a, b: sums("rr", "gk2", a, b, True)),
-            ("next", fallback),
+            ("n5", lambda q: last or act(R("n5"), R("vl"), bias=1.0, scale=5.0)),
+            ("n6", lambda q: last or ts(R("n6"), R("n5"), 2047, Op.bitwise_and)),
         ])
         if not last:
             wait("Y", "snt" + Y, count["snt" + Y])
@@ -498,16 +502,13 @@ def rank_program(g, core, T, topo):
             scan(R("sc", 128 * x, 128 * x + 128), R("gap"), R("d1", 128 * x, 128 * x + 128), Op.min, Op.max)
         for c in range(8):
             mm(R("p_l", 16 * c, 16 * c + 16), R("sel", 128 * c, 128 * c + 128), R("sc", 15, 256, 16))
-        tt(R("v0"), R("sc", 15, 128, 16), R("sc", 128 + 15, 256, 16), Op.max)
-        ts(R("v1"), R("mx", 15, 128, 16), KEY, Op.is_ge, 2048.0, Op.mult)
-        tt(R("void"), R("v1"), R("v0"), Op.is_le)
+        act(R("void", 0, 8), R("mx", 15, 128, 16), Fn.Relu, 1.0, -1.0 / KEY)
+        act(R("void", 8, 24), R("sc", 15, 256, 16), Fn.Relu, 1.0 - V)
+        if first:
+            commit_weights()
         scan(R("ls"), R("p_l", 0, 128), R("s8"), Op.max, Op.add)
-        ts(A_, R("ls", 7, 128, 16), C8, Op.add)
-        ts(Q_, R("ls", 15, 128, 16), C8, Op.add)
-
-        def names(q):
-            cp(q, R("l4f", 0, 16), R("l4", 0, 16))
-            ts(R("nm", 1, 256, 2), rW, WHOLE - OFF, Op.add, WHOLE, Op.subtract)
+        ts(A_, R("ls", 7, 128, 16), C8, Op.add, float(V), Op.min)
+        ts(Q_, R("ls", 15, 128, 16), C8, Op.add, float(V), Op.min)
 
         def same(q):
             for c in reversed(range(8)):
@@ -519,13 +520,13 @@ def rank_program(g, core, T, topo):
             for c in reversed(range(8)):
                 o = R("p_t%d" % (c // 4), 128 * (c % 4), 128 * (c % 4) + 128)
                 at = 16 * c * (c + 1)
+                mm(o, R("id3"), R("sel", 128 * c, 128 * c + 128), True, False)
                 for x, (kk, y) in enumerate((("ka", 0), ("ka", 1), ("kw", 0), ("kw", 1))):
-                    mm(o, R(kk, at + y, at + 256, 2), R("ide"), x == 0, x == 3)
+                    mm(o, R(kk, at + y, at + 256, 2), R("ide"), False, x == 3)
 
         def mask(x):
             h = (512 * x, 512 * x + 512)
-            aff(R("tl", *h), R("tc", *h), [[16, 4], [0, 8], [1, 16]], Op.is_gt, 0.0, 64 * x, -1)
-            aff(R("tk", *h), R("tl", *h), [[16, 4], [0, 8], [1, 16]], Op.not_equal, EPS, 64 * x, -1)
+            aff(R("tk", *h), R("tc", *h), [[16, 4], [0, 8], [1, 16]], Op.is_ge, 0.0, 64 * x, -1)
 
         def fetch(o, win, lst):
             return lambda q, a, b: cp(q, C(o, a, b), ind(full(win), R(lst, a, b)))
@@ -559,14 +560,7 @@ def rank_program(g, core, T, topo):
         def places(q):
             for o, k in (("mz", 16), ("my", 0)):
                 for r in range(2):
-                    plus(q, R(o, 9 + 10 * r, 160, 20), R("l4f", k + 8 * r, k + 8 * r + 8), float(NB))
-
-        def other(q):
-            if not last:
-                ts(R("a0"), R("l4f", 16, 24), -2047.5, Op.add, 2 * BIG, Op.mult)
-                tt(R("a1"), R("a0"), R("n6"), Op.min)
-                tt(R("av"), R("a1"), R("l4f", 8, 16), Op.max)
-                tt(R("mv", 19, 160, 20), R("l4f", 0, 8), R("av"), Op.subtract)
+                    plus(q, R(o, 9 + 10 * r, 160, 20), R("l4", k + 8 * r, k + 8 * r + 8), float(NB))
 
         def lower(q, a, b):
             for c in range(a // 16, 8):
@@ -577,13 +571,14 @@ def rank_program(g, core, T, topo):
             ("a", lambda q: cp(q, R("nm", 0, 256, 2), ind(R("idt"), A_))),
             ("w", lambda q: cp(q, rW, ind(full("it"), Q_))),
             ("p", lambda q: cp(q, rP, ind(full("mt"), A_))),
-            ("wl", lambda q: to_list(W_, rW, R("ws", 0, 128), 0.25 - OFF)),
-            ("pl", lambda q: to_list(P_, rP, R("ws", 128, 256))),
+            ("ws", lambda q: own_row(R("ws", 0, 128), rW)), ("wl", lambda q: to_list(W_, R("ws", 0, 128), 0.25 - OFF)),
+            ("ps", lambda q: own_row(R("ws", 128, 256), rP)), ("pl", lambda q: to_list(P_, R("ws", 128, 256))),
             ("nzq", lambda q: cp(q, R("nzq"), ind(R("nzt"), Q_))),
             ("nbw", lambda q: cp(q, R("nbw"), ind(R("nbt"), W_))),
             ("nzp", lambda q: cp(q, R("nzp"), ind(R("nzt"), P_))),
-            ("names", names), ("same", same), ("sameT", same_turned),
-            ("qp", lambda q: cp(q, R("l4f", 16, 32), R("l4", 16, 32))),
+            ("aw", lambda q: cp(q, R("l4f", 0, 16), R("l4", 0, 16))),
+            ("nm", lambda q: ts(R("nm", 1, 256, 2), rW, WHOLE - OFF, Op.add, WHOLE, Op.subtract)),
+            ("same", same), ("sameT", same_turned),
             ("tc0", lambda q: cp(q, R("tc", 0, 512), R("p_t0"))),
             ("tc1", lambda q: cp(q, R("tc", 512, 1024), R("p_t1"))),
             ("mask0", lambda q: mask(0)), ("mask1", lambda q: mask(1)),
@@ -598,9 +593,13 @@ def rank_program(g, core, T, topo):
             ("zq", lambda q: cp(q, R("zq"), ind(full(Z), R("l4", 16, 32)))),
             ("dz", moved),
             ("sign", lambda q: act(R("sg"), R("p_t0", 0, 256), Fn.Sign)),
-            ("places", places), ("alt", other),
+            ("a0", lambda q: last or act(R("a0"), Q_, bias=-2047.5 * 2 * BIG, scale=2 * BIG)),
+            ("places", places),
+            ("a1", lambda q: last or tt(R("a1"), R("a0"), R("n6"), Op.min)),
+            ("av", lambda q: last or tt(R("av"), R("a1"), R("l4f", 8, 16), Op.max)),
+            ("dv", lambda q: last or tt(R("mv", 19, 160, 20), R("l4f", 0, 8), R("av"), Op.subtract)),
             ("void", lambda q: [mm(R("p_g", 0, 20), R("idn"), R("zero", 0, 20), True, False)]
-             + [mm(R("p_g", 1 + 10 * r, 9 + 10 * r), R("idf"), R("void"), False, False) for r in range(2)]),
+             + [mm(R("p_g", 1 + 10 * r, 9 + 10 * r), R("idf"), R("void", 8 * x, 8 * x + 8), False, False) for r in range(2) for x in range(3)]),
             ("g1", gain("m_1", "gm")),
             ("g2", gain("m_2", "gp")), ("g3", gain("m_3", "gp")), ("g4", gain("m_4", "gm")),
             ("zero", lambda q: mm(R("p_l", 0, 160), R("idn"), R("zero"), True, False)),
@@ -608,11 +607,13 @@ def rank_program(g, core, T, topo):
             ("lower", lower),
         ])
 
-    offsets("oz", "sz", "mz")
+    own_group("sz", "mz")
+    own_group("sy", "my")
+    offsets("oz", "sz")
+    offsets("oy", "sy")
     act(rQ, ind(R("idt"), Q_))
     tt(ind(park(Z), R("oz")), R("zq"), R("sg"), Op.add)
     dma("Y", "d_zo", [(T.zo[:, :], own(Z))])
-    offsets("oy", "sy", "my")
     tc(ind(park("mt"), R("oy")), R("rw", 256, 512))
     order("Y", [own("mt")], [], ("d_mo", 16))
     g.sync.dma_start(T.mo[:, :], T.mt[0:128:16, NB:NB + V]).then_inc(T.sem["d_mo"], 16)

@@ -11,20 +11,21 @@ OFF = 32.0
 WHOLE = 1.5 * 2 ** 23
 
 NAMING1 = {
-    "V": "gk mv mvs mvl nzv kp|Z 64 128|nbv1 0 64|Y 32 64|nbv1 64 128|Y 96 128|max 96 128|max 64 96|kg|im1 3 4|n6",
-    "S": "wn|im1 0 1|Z 0 64|im1 1 2|Y 0 32|Y 64 96|cat|abs 0 32|abs 32 64|n5|im1 2 3|wg",
-    "P": "imP 0 1|imP 1 2|rank|imP 2 3|imP 3 4|zP 64 96|zP 96 128|sumz 64 128|diff 0 32|diff 32 64|catT|sum 0 32|sumy 64 128|sum 32 64|summ 64 128",
+    "V": "i2h mv mvs mvl nzv|im1 1 2|Z 0 64|dY 0 64|relu 0 64|max 64 96|n6 idt",
+    "S": "wn wk s8|im1 0 1|nbv1 0 64|c1 n5|Z 64 128|nbv1 64 128|Y 96 128|Y 64 96|abs 96 128|cat|im1 3 4|im1 2 3|wg wp",
+    "P": "gcP|imP 0 1|imP 1 2|rank|imP 2 3|mzP|imP 3 4|zP 64 96|sumz 64 96|diff 96 128|sumy 0 64|sumy 64 96|summ 0 64|sum 96 128|summ 64 96|catT",
 }
 NAMING = {
-    "V": "sz oz newz sy sv oy vl newy newm mv mvs mvl nzv|Z 64 128|dY 64 128|relu 64 128|max 32 64|n6",
-    "S": "rq ra gz gy nbv cb n5 th cat|Z 0 64|Y 0 32|Y 32 64|abs 0 32|im",
-    "P": "count catT rank|zP 32 64|sumz 32 64|diff 0 32|sumy 64 128|sumy 32 64|sum 0 32|summ 64 128|summ 32 64",
+    "V": "sz oz newz sy oy newy sv vl mv mvs mvl nzv|whole 0 68|Z 64 128|dY 64 128|relu 64 128|max 32 64|n6|whole 68 96",
+    "S": "rq ra gz newm gy nbv cb n5|Z 0 64|Y 0 32|Y 32 64|abs 0 32|cat im th",
+    "P": "count rank|zP 32 64|sumz 32 64|diff 0 32|sumy 32 64|sumy 64 128|sum 0 32|summ 64 128|summ 32 64|catT",
     "G": "sendz sendy",
 }
+PIECES = [(96, 112), (112, 128)]
 GAINS = {
-    "V": "w p ws ps nm wl pl aw same|f1 0 32|f1 32 64|f1 64 128|f3 0 64|f2 64 128|f2 0 32|f4 0 32|f4 32 64|f2 32 64|a1 av dv|prop 0 128",
-    "S": "nba a|A 0 32|nzq|A 32 64|nbw|A 64 128|nzp|W 64 128|B 64 128|tc1|W 0 32|tc0|r3 64 96|W 32 64|r3 96 128|a0|r4 64 96|r4 96 128|"
-         "x zq places sign",
+    "V": "w af nzq nm ws|ka 7 8|wl|ka 6 7|wf|ka 0 6|kw 0 8|f1 0 64|f3 0 64|f1 64 128|f2 64 128|f4 0 64|f2 0 64|a1 av dv|prop 0 128",
+    "S": "p a nba|A 0 64|nbw nzp|A 64 128|W 64 128|B 64 128|W 0 64|tc1 tc0|r3 64 96|r3 96 128|r4 64 96|r4 96 128|"
+         "a0 pairs x zq places sign",
     "P": "void sameT zero|d3 64 96|d3 96 128|g1 0 128|d4 64 96|d4 96 128|g3 0 128|g4 0 128|g2 0 128 stop|dz|lower 0 128",
     "G": "mask1 mask0",
 }
@@ -34,25 +35,25 @@ SCRATCH = {}
 for _n, _w, _t in [
     ("nbt", V + PAD, _I), ("nzt", V + PAD, _I), ("xt", V + PAD, _B), ("idt", V + PAD, _F),
     ("z1", WIN, _B), ("z2", WIN, _B), ("z3", WIN, _B), ("y1", WIN, _B), ("y2", WIN, _B), ("y3", WIN, _B),
-    ("mt", NB + V + PAD, _F), ("it", NB + V + PAD, _F),
+    ("mt", NB + V + PAD, _F), ("it", NB + V + PAD, _F), ("mw", NB + V, _F),
     ("mr", 128, _I), ("mlh", 128, _H), ("mlt", 128, _H), ("mlist", 128, _U),
-    ("m2", 128, _I), ("i2", 128, _I), ("m2h", 128, _H), ("i2h", 128, _H),
+    ("m2", 512, _I), ("i2", 512, _I), ("m2h", 512, _H), ("i2h", 512, _H),
     ("bx32", 16, _I), ("bz32", 16, _I), ("bxl", 16, _U), ("bzl", 16, _U),
     ("gz", NB, _B), ("gy", NB, _B),
     ("ones", 1024, _B), ("idn", 128, _B), ("idm", 128, _B), ("ide", 128, _B), ("id3", 128, _B), ("idf", 128, _B),
     ("gk", 8, _B), ("gk2", 8, _B), ("gkm", 8, _B), ("gp", 20, _B), ("gm", 20, _B),
-    ("ej", 2048, _B), ("e4", 512, _B), ("sel", 1024, _B), ("tb", 128, _B),
-    ("pi", 8, _I), ("pa", 8, _I), ("pf", 8, _F), ("cor0", 8, _F), ("cor", 8, _F), ("pq", 8, _F),
-    ("i16", 128, _F), ("g8", 128, _F), ("p10", 160, _F), ("t0", 160, _F), ("t1", 160, _F), ("t2", 160, _F),
-    ("s8", 128, _F), ("s16", 128, _F), ("c1", 128, _F), ("mz", 160, _F), ("my", 160, _F), ("mv", 160, _F),
+    ("ej", 512, _B), ("sel", 1024, _B), ("tb", 128, _B),
+    ("pi", 8, _I), ("pa", 8, _I), ("pf", 8, _F), ("cor0", 8, _F), ("cor", 8, _F),
+    ("i16", 128, _F), ("t0", 128, _F), ("t1", 128, _F), ("gc", 320, _B),
+    ("s8", 128, _F), ("s16", 256, _F), ("c1", 128, _F), ("mz", 160, _F), ("my", 160, _F), ("mv", 160, _F),
     ("li", 16, _F), ("alt", 16, _F),
     ("vl", 8, _U), ("mvr", 128, _F), ("mvs", 128, _F), ("mvl", 8, _U),
     ("nbv", 128, _U), ("nzv", 128, _U), ("cat", 256, _H),
     ("zg", 2048, _B), ("yg", 2048, _B), ("rr", 2048, _B),
     ("mx", 128, _F), ("gap", 128, _F), ("d1", 256, _F), ("sc", 256, _H), ("ls", 128, _F),
-    ("l4", 32, _U), ("l4f", 32, _F), ("rw", 512, _F), ("ws", 256, _F), ("nm", 256, _H),
+    ("l4", 32, _U), ("l2", 32, _U), ("l4f", 16, _F), ("wp", 256, _F), ("rw", 512, _F), ("ws", 256, _F), ("nm", 256, _H),
     ("nba", 128, _U), ("nzq", 128, _U), ("nbw", 128, _U), ("nzp", 128, _U),
-    ("ga", 2048, _B), ("gw", 2048, _B), ("gb", 2048, _B), ("gc", 2048, _B),
+    ("ga", 2048, _B), ("gw", 2048, _B), ("gb", 2048, _B),
     ("m_1", 2048, _B), ("m_2", 2048, _B), ("m_3", 2048, _B), ("m_4", 2048, _B),
     ("ka", 1152, _B), ("kw", 1152, _B), ("zero", 160, _B), ("tc", 1024, _B), ("tk", 1024, _B),
     ("xg", 256, _B), ("zq", 256, _B), ("sg", 256, _B),
@@ -284,69 +285,65 @@ def rank_program(g, core, T, topo):
 
     dma("S", "d_mr", [(R("mr", 64 * h, 64 * h + 64), T.m[h::2, :]) for h in range(2)])
     dma("Y", "d_bz", [(R("bz32"), T.bz[:, :])])
+    dma("Y", "d_m2", [(R("m2", 0, 512, 1, 0, 32), T.m[:, :])])
     dma("Y", "d_z", [(own("z1"), T.z[:, :])])
     dma("Y", "d_bx", [(R("bx32"), T.bx[:, :])])
-    dma("Y", "d_m2", [(R("m2"), T.m[:, :])])
-    dma("Y", "d_i2", [(R("i2"), T.im[:, :])])
+    dma("Y", "d_i2", [(R("i2", 0, 512, 1, 0, 32), T.im[:, :])])
     dma("Y", "d_nz", [(R("nzt", 0, V), T.nz[:, :])])
 
     def load_nb(h):
         dma("Y", "d_nb%d" % h, [(R("nbt", 1024 * h, 1024 * h + 1024), T.nb[:, 1024 * h:1024 * h + 1024])])
 
-    I_, IM, G_, GM = [R("pf", k, k + 1) for k in (0, 1, 4, 6)]
-    iota(R("pi", 0, 4), [[112, 2], [15, 2]], 0, 1, False)
-    iota(R("pq", 0, 4), [[-4, 4]], 0, 1)
-    iota(R("e4"), [[1, 4], [16, 8], [0, 16]], 0, 0)
+    load_nb(0)
+
+    I_, IM = R("pf", 0, 1), R("pf", 1, 2)
+    iota(R("pi", 0, 4), [[0, 2], [15, 2]], 0, 1, False)
     iota(R("i16"), [[0, 8], [1, 16]], 0, 0)
-    iota(R("li"), [[128, 2], [16, 8]], 0, 0)
-    iota(R("g8"), [[0, 16], [1, 8]], 0, 0)
+    iota(R("li"), [[16, 8], [128, 2]], 0, 0)
+    ms(R("zero"), 0.0)
+    run("S", [R("it", NB + V)], [R("zero", 0, PAD)], lambda e: e.activation(ap(R("it", NB + V)), ap(R("zero", 0, PAD)), Fn.Silu))
     ms(R("ones"), 1.0)
-    aff(R("idn"), R("ones", 0, 128), [[-1, 128]], Op.is_equal, 0.0, 0, 1)
+    aff(R("ej", 0, 512, 1, 0, 32), R("ones", 0, 512, 1, 0, 32), [[-1, 4], [-4, 8], [0, 16]], Op.is_equal, 0.0, 0, 1)
     ts(R("pa", 0, 4), R("pi", 0, 4), 15, Op.bitwise_and)
-    ts(R("pa", 4, 8), R("pi", 0, 4), 4, Op.logical_shift_right, 7, Op.bitwise_and)
-    act(R("it", NB + V), R("ones", 0, PAD), Fn.Silu, scale=OFF)
-    ms(R("mt", NB + V), 0.0)
-    ms(R("nzt", V), 0)
+    ts(R("pa", 4, 8), R("pi", 0, 4), 4, Op.logical_shift_right)
     tc(R("pf"), R("pa"))
+    aff(R("idn"), R("ones", 0, 128), [[-1, 128]], Op.is_equal, 0.0, 0, 1)
+    ts(R("t0"), R("i16"), I_, Op.is_equal, BIG, Op.mult)
+    ts(R("t1"), R("i16"), IM, Op.is_equal, -2 * BIG, Op.mult)
     ts(R("cor0", 0, 2), R("pf", 0, 8, 4), 0.0, Op.is_equal, 2 * BIG, Op.mult)
-    ts(R("cor", 0, 2), R("cor0", 0, 2), -BIG, Op.add)
+    tt(R("s16", 0, 128), R("t0"), R("t1"), Op.add)
     C16, C8 = R("cor", 0, 1), R("cor", 1, 2)
-
-    def rows(jb):
-        ts(R("ej", 512 * jb, 512 * jb + 512), R("e4"), R("pq", jb, jb + 1), Op.is_equal)
-
-    def picks(o, it, at, before):
-        ts(R("t0", 0, 128), R(it), at, Op.is_equal, BIG, Op.mult)
-        ts(R("t1", 0, 128), R(it), before, Op.is_equal, -2 * BIG, Op.mult)
-        tt(R(o), R("t0", 0, 128), R("t1", 0, 128), Op.add)
-
-    rows(0)
-    tc(R("bzl"), R("bz32"))
+    act(R("bzl"), R("bz32"))
     for h in range(2):
         for b in range(4):
-            cp("VVVVVVSS"[4 * h + b], R("mlh", 32 * b + 16 * h, 32 * b + 16 * h + 16), R("mr", 64 * h + 16 * b, 64 * h + 16 * b + 16))
+            cp("VVVVVSSS"[4 * h + b], R("mlh", 32 * b + 16 * h, 32 * b + 16 * h + 16), R("mr", 64 * h + 16 * b, 64 * h + 16 * b + 16))
+    act(R("m2h", 0, 512, 1, 0, 32), R("m2", 0, 512, 1, 0, 32))
     tr(R("mlt"), R("mlh"))
     for b in range(4):
         tc(R("mlist", b, 128, 4), R("mlt", 32 * b, 32 * b + 32))
     act(R("gz"), ind(own("z1"), R("bzl")))
     send("z", 1, R("gz"))
-    iota(R("p10"), [[0, 16], [1, 10]], 0, 0)
+    GK, S8, MZ, GP = (0, 8), (8, 136), (136, 296), (296, 316)
+    aff(R("gc", *GK), R("ones", 0, 8), [[-4, 8]], Op.is_equal, 0.0, 0, 1)
+    for src, base, fill in ((R("zero", 0, 128), 0, BIG), (R("gc", *S8), -4, -2 * BIG), (R("gc", *S8), 28, -2 * BIG)):
+        aff(R("gc", *S8), src, [[0, 16], [-4, 8]], Op.not_equal, fill, base, 1)
     tc(R("y1", NB, NB + 1024), ind(own("z1"), R("mlist", 0, 64)))
     act(R("y1", NB + 1024, NB + V), ind(own("z1"), R("mlist", 64, 128)))
-    tc(R("bxl"), R("bx32"))
-    tc(R("m2h"), R("m2"))
-    for jb in range(1, 4):
-        rows(jb)
-    picks("s16", "i16", I_, IM)
+    act(R("bxl"), R("bx32"))
+    ts(R("cor", 0, 2), R("cor0", 0, 2), -BIG, Op.add)
     ts(R("alt"), R("li"), I_, Op.add)
-    ts(R("vl"), R("alt", 0, 8), 16.0, Op.mult)
+    ms(R("mt", NB + V), OFF)
+    ts(R("vl"), R("alt", 0, 16, 2), 16.0, Op.mult)
+    ms(R("nzt", V), 0)
     act(R("gy"), ind(own("y1"), R("bxl")))
     send("y", 1, R("gy"))
-    wait("Y", "S", count["S"])
-    for h in range(2):
-        load_nb(h)
+    aff(R("gc", *GP), R("ones", 0, 20), [[0, 2], [-4, 10]], Op.is_equal, 0.0, 4, 1)
+    wait("Y", "G", count["G"])
+    load_nb(1)
+    for src, base, fill in ((R("ones", 0, 160), 0, 0.0), (R("gc", *MZ), 4, 1 / EPS)):
+        aff(R("gc", *MZ), src, [[0, 16], [-4, 10]], Op.not_equal, fill, base, 1)
+    iota(R("idt", 0, 1040), [[1, 1040]], 0, 0)
     aff(R("sel"), R("ones"), [[-16, 8], [0, 8], [-1, 16]], Op.is_equal, 0.0, 0, 1)
-    iota(R("idt"), [[1, V + PAD]], 0, 0)
     wait("Y", "d_nb1", 16)
     dma("Y", "d_x", [(R("xt", 0, V), T.x[:, :])])
 
@@ -358,61 +355,61 @@ def rank_program(g, core, T, topo):
 
     def spread(q, half, tab, off, bk, jb):
         if q == "P":
-            for j in range(4):
-                mm(R(bk, 128 * j, 128 * j + 128), R("ej", 512 * jb + 128 * j, 512 * jb + 128 * j + 128), R(half))
+            mm(R(bk), R("ej", 128 * jb, 128 * jb + 128, 1, 0, 32), R(half, 0, 512, 1, 0, 32))
         else:
             plus(q, R(tab, NB + 512 * jb, NB + 512 * jb + 512), R(bk), off)
 
     for jb, bk in enumerate(("p_a", "p_b", "p_t0", "p_t1")):
-        spread("P", "m2h", "mt", 0.0, bk, jb)
-        spread("SSSV"[jb], "m2h", "mt", 0.0, bk, jb)
+        spread("P", "m2h", "mt", OFF, bk, jb)
+        spread("SVSV"[jb], "m2h", "mt", OFF, bk, jb)
+
+    def times(q, o, i, c):
+        if q == "V":
+            ts(o, i, c, Op.mult)
+        else:
+            act(o, i, scale=c)
 
     def naming_weights(q):
-        act(R("i2h"), R("i2"))
-        act(R("gk2"), R("gk"), scale=2.0)
-        act(R("gkm"), R("gk"), scale=-1.0)
         act(R("tb"), R("i16"), bias=480.0, scale=-32.0)
         act(R("idm"), R("idn"), scale=-1.0)
 
+    def group_weights(q):
+        for o, s in (("gkm", -KEY), ("gk", KEY), ("gk2", 2 * KEY)):
+            times(q, R(o), R("p_a", *GK), s)
+
+    def pick_weights(q):
+        cp(q, R("mz"), R("p_b", *MZ))
+        for o, s in (("gp", 2.0), ("gm", -2.0)):
+            times(q, R(o), R("p_b", *GP), s)
+
     def gain_weights(q):
         for o, s in (("ide", -EPS), ("id3", 3 * EPS), ("idf", -16 * FAR)):
-            act(R(o), R("idn"), scale=s)
-        for o in (R("nbt", V), R("zero")):
-            act(o, R("ones", 0, o[4] - o[3]), scale=0.0)
+            times(q, R(o), R("idn"), s)
+        times(q, R("nbt", V), R("zero", 0, PAD), 0.0)
+        cp(q, R("s16", 128, 256), R("s16", 0, 128))
 
     def commit_weights():
-        for o, s in (("gp", 2.0), ("gm", -2.0)):
-            ts(R(o), R("t0", 0, 20), s, Op.mult)
         for o in ("my", "mv"):
             act(R(o), R("mz"))
         for o in (R("xt", V), R("th")):
-            ms(o, 0.0)
-
-    def pick_constants(q):
-        picks("s8", "g8", G_, GM)
-        ts(R("c1"), R("i16"), 0.0, Op.not_equal)
-
-    def gain_constants(q):
-        ts(R("t0"), R("p10"), -1.0, Op.add, G_, Op.is_equal)
-        ts(R("t2"), R("p10"), G_, Op.not_equal)
-        ts(R("t1"), R("t0"), 1 / EPS - 1, Op.mult)
-        tt(R("mz"), R("t2"), R("t1"), Op.add)
+            act(o, R("zero", 0, o[4] - o[3]))
+        plus("V", R("idt", 1600, V + PAD), R("idt", 576, 1040), 1024.0)
 
     def own_row(tmp, row):
-        scan(tmp, row, R("s16"), Op.max, Op.add)
+        scan(tmp, row, R("s16", 0, row[4] - row[3]), Op.max, Op.add)
 
-    def to_list(o, tmp, shift=0.0):
-        ts(o, (tmp[0], 0, 128, tmp[3] + 15, tmp[4], 16), C16, Op.add, shift, Op.add)
+    def to_list(o, tmp):
+        ts(o, (tmp[0], 0, 128, tmp[3] + 15, tmp[4], 16), C16, Op.add, 0.25 - OFF, Op.add)
 
     def own_group(s, m):
         scan(R(s), R("p_l", 0, 160), R(m), Op.max, Op.mult)
 
     def offsets(o, s):
-        for r in range(2):
-            tt(R(o, 8 * r, 8 * r + 8), R(s, 9 + 10 * r, 160, 20), R("alt", 8 * r, 8 * r + 8), Op.max)
+        tt(R(o), R(s, 9, 160, 10), R("alt"), Op.max)
 
-    A_, W_, Q_, P_ = [R("l4", 8 * k, 8 * k + 8) for k in range(4)]
-    rA, rW, rQ, rP = [R("rw", 128 * k, 128 * k + 128) for k in range(4)]
+    A_, W_, P_, Q_ = [R("l4", 8 * k, 8 * k + 8) for k in range(4)]
+    AW, QP = R("l2", 0, 16), R("l2", 16, 32)
+    rW, rP = R("wp", 0, 128), R("wp", 128, 256)
 
     for t in range(1, RO + 1):
         Y, Z = "y%d" % t, "z%d" % t
@@ -422,12 +419,13 @@ def rank_program(g, core, T, topo):
         def nbv1(q, a, b):
             cp(q, R("nbv", a, b), R("nbt", 16 * a, 16 * b, 16))
 
-        def im(q):
-            if q == "V":
-                tc(ind(park("it"), R("oz")), R("rw", 0, 256))
-            else:
-                run("S", [ind(park("it"), R("oz"))], [R("rw", 0, 256)],
-                    lambda e: e.activation(ap(ind(park("it"), R("oz"))), ap(R("rw", 0, 256)), Fn.Silu))
+        def put(tab, off, src):
+            o = ind(park(tab), R(off))
+            run("S", [o], [src], lambda e: e.activation(ap(o), ap(src), Fn.Silu))
+
+        def whole(q, a, b):
+            if last:
+                ts(R("mw", NB + 16 * a, NB + 16 * b), R("mt", NB + 16 * a, NB + 16 * b), WHOLE - OFF, Op.add, WHOLE, Op.subtract)
 
         def th(q):
             cn, cq = R("cn", 0, 1), R("cq", 0, 1)
@@ -445,14 +443,19 @@ def rank_program(g, core, T, topo):
 
 
         phase(NAMING1 if first else NAMING, [
-            ("gk", lambda q: ts(R("gk"), R("g8", 0, 8), G_, Op.is_equal, KEY, Op.mult)),
-            ("wn", naming_weights), ("kp", pick_constants), ("kg", gain_constants), ("wg", gain_weights),
+            ("i2h", lambda q: cp(q, R("i2h", 0, 512, 1, 0, 32), R("i2", 0, 512, 1, 0, 32))),
+            ("gcP", lambda q: [mm(R("p_a", *c), R("ej", 0, 128, 1, 0, 32), R("gc", *c, 1, 0, 32)) for c in (GK, S8)]),
+            ("mzP", lambda q: [mm(R("p_b", *c), R("ej", 0, 128, 1, 0, 32), R("gc", *c, 1, 0, 32)) for c in (MZ, GP)]),
+            ("wn", naming_weights), ("wk", group_weights), ("wp", pick_weights), ("wg", gain_weights),
+            ("s8", lambda q: cp(q, R("s8"), R("p_a", *S8))),
+            ("c1", lambda q: act(R("c1"), R("i16"), Fn.Sign)),
+            ("idt", lambda q: plus(q, R("idt", 1040, 1600), R("idt", 16, 576), 1024.0)),
             [("imP", lambda q, a, b: spread(q, "i2h", "it", OFF, ("p_g", "p_l")[a % 2], a)),
              ("im1", lambda q, a, b: spread(q, "i2h", "it", OFF, ("p_g", "p_l")[a % 2], a))],
             ("sz", lambda q: own_group("sz", "mz")), ("oz", lambda q: offsets("oz", "sz")),
             ("sy", lambda q: own_group("sy", "my")), ("oy", lambda q: offsets("oy", "sy")),
-            ("rq", lambda q: cp(q, rQ, ind(R("idt"), Q_))),
-            ("ra", lambda q: plus(q, rA, R("nm", 0, 256, 2), OFF)),
+            ("rq", lambda q: plus(q, R("rw", 256, 512), ind(R("idt"), QP), OFF)),
+            ("ra", lambda q: plus(q, R("rw", 0, 256), ind(R("idt"), AW), OFF)),
             ("newz", lambda q: tt(ind(park(Z), R("oz")), R("zq"), R("sg"), Op.add)),
             ("newy", lambda q: tt(ind(park(Y), R("oy")), R("zq"), R("sg"), Op.add)),
             ("gz", lambda q: cp(q, R("gz"), ind(own(Z), R("bzl")))),
@@ -461,13 +464,14 @@ def rank_program(g, core, T, topo):
             ("sendy", lambda q: send("y", t, R("gy"))),
             ("sv", lambda q: own_group("sv", "mv")),
             ("vl", lambda q: tt(R("vl"), R("sv", 19, 160, 20), R("av"), Op.add)),
-            ("newm", lambda q: tc(ind(park("mt"), R("oy")), R("rw", 256, 512))),
+            ("newm", lambda q: put("mt", "oy", R("rw", 256, 512))),
             ("mv", lambda q: cp(q, R("mvr"), ind(full("mt"), R("vl")))),
             ("mvs", lambda q: own_row(R("mvs"), R("mvr"))), ("mvl", lambda q: to_list(R("mvl"), R("mvs"))),
             ("nbv1", nbv1),
             ("nbv", lambda q: first or cp(q, R("nbv"), ind(R("nbt"), R("vl")))),
             ("nzv", lambda q: cp(q, R("nzv"), ind(R("nzt"), R("mvl")))),
-            ("im", im),
+            ("im", lambda q: put("it", "oz", R("rw", 0, 256))),
+            ("whole", whole),
             ("cb", lambda q: cp(q, R("cb"), R("sv", 9, 160, 20))),
             ("count", lambda q: first or mm(R("p_l", 200, 208), R("ones", 0, 128), R("cb"))),
             ("th", th),
@@ -506,15 +510,17 @@ def rank_program(g, core, T, topo):
         act(R("void", 8, 24), R("sc", 15, 256, 16), Fn.Relu, 1.0 - V)
         if first:
             commit_weights()
+        whole("V", *PIECES[0])
         scan(R("ls"), R("p_l", 0, 128), R("s8"), Op.max, Op.add)
         ts(A_, R("ls", 7, 128, 16), C8, Op.add, float(V), Op.min)
         ts(Q_, R("ls", 15, 128, 16), C8, Op.add, float(V), Op.min)
 
-        def same(q):
-            for c in reversed(range(8)):
-                at = 16 * c * (c + 1)
-                for kk, s in (("ka", c), ("kw", 8 + c)):
-                    ts(R(kk, at, at + 32 * (c + 1)), R("nm", 0, 32 * (c + 1)), R("l4f", s, s + 1), Op.is_equal)
+        def same(kk, s):
+            def f(q, a, b):
+                for c in reversed(range(a, b)):
+                    at = 16 * c * (c + 1)
+                    ts(R(kk, at, at + 32 * (c + 1)), R("nm", 0, 32 * (c + 1)), R("l4f", s + c, s + c + 1), Op.is_equal)
+            return f
 
         def same_turned(q):
             for c in reversed(range(8)):
@@ -534,12 +540,6 @@ def rank_program(g, core, T, topo):
         def bank(x, a, b):
             return R((("p_a", "p_d"), ("p_b", "p_n"))[x][a // 32 % 2], 16 * (a % 32), 16 * (a % 32 + b - a))
 
-        def lift(x, src):
-            return lambda q, a, b: mm(bank(x, a, b), R("idn"), C(src, a, b))
-
-        def larger(mx, x, src):
-            return lambda q, a, b: tt(C(mx, a, b), bank(x, a, b), C(src, a, b), Op.max)
-
         def gain(mx, wgt):
             return lambda q, a, b, flag="": [mm(R("p_g", 0, 20, 1, a, b), R(mx, 16 * a + k, 16 * b, 16), R(wgt), False,
                                                 flag == "stop" and k == 15) for k in range(16)]
@@ -558,9 +558,8 @@ def rank_program(g, core, T, topo):
             mm(R("p_t0", 0, 256), R("idm"), R("zq"), False, True)
 
         def places(q):
-            for o, k in (("mz", 16), ("my", 0)):
-                for r in range(2):
-                    plus(q, R(o, 9 + 10 * r, 160, 20), R("l4", k + 8 * r, k + 8 * r + 8), float(NB))
+            for o, lst in (("mz", QP), ("my", AW)):
+                plus(q, R(o, 9, 160, 10), lst, float(NB))
 
         def lower(q, a, b):
             for c in range(a // 16, 8):
@@ -571,26 +570,23 @@ def rank_program(g, core, T, topo):
             ("a", lambda q: cp(q, R("nm", 0, 256, 2), ind(R("idt"), A_))),
             ("w", lambda q: cp(q, rW, ind(full("it"), Q_))),
             ("p", lambda q: cp(q, rP, ind(full("mt"), A_))),
-            ("ws", lambda q: own_row(R("ws", 0, 128), rW)), ("wl", lambda q: to_list(W_, R("ws", 0, 128), 0.25 - OFF)),
-            ("ps", lambda q: own_row(R("ws", 128, 256), rP)), ("pl", lambda q: to_list(P_, R("ws", 128, 256))),
+            ("ws", lambda q: own_row(R("ws"), R("wp"))), ("wl", lambda q: to_list(R("l4", 8, 24), R("ws"))),
             ("nzq", lambda q: cp(q, R("nzq"), ind(R("nzt"), Q_))),
             ("nbw", lambda q: cp(q, R("nbw"), ind(R("nbt"), W_))),
             ("nzp", lambda q: cp(q, R("nzp"), ind(R("nzt"), P_))),
-            ("aw", lambda q: cp(q, R("l4f", 0, 16), R("l4", 0, 16))),
+            ("af", lambda q: cp(q, R("l4f", 0, 8), A_)), ("wf", lambda q: cp(q, R("l4f", 8, 16), W_)),
             ("nm", lambda q: ts(R("nm", 1, 256, 2), rW, WHOLE - OFF, Op.add, WHOLE, Op.subtract)),
-            ("same", same), ("sameT", same_turned),
+            ("ka", same("ka", 0)), ("kw", same("kw", 8)), ("sameT", same_turned),
             ("tc0", lambda q: cp(q, R("tc", 0, 512), R("p_t0"))),
             ("tc1", lambda q: cp(q, R("tc", 512, 1024), R("p_t1"))),
             ("mask0", lambda q: mask(0)), ("mask1", lambda q: mask(1)),
-            ("A", fetch("ga", Y, "nba")), ("W", fetch("gw", Y, "nbw")), ("B", fetch("gb", Z, "nzp")), ("C", fetch("gc", Z, "nzq")),
-            [("cP", lift(0, "gc")), ("bP", lift(1, "gb")), ("m1", larger("m_1", 0, "ga")), ("m2", larger("m_2", 0, "gw")),
-             ("m3", larger("m_3", 1, "ga")), ("m4", larger("m_4", 1, "gw")),
-             ("d1", diff(0, "ga", "gc")), ("r1", relu(0, "m_1")), ("d2", diff(1, "gw", "gc")), ("r2", relu(1, "m_2")),
-             ("d3", diff(0, "ga", "gb")), ("r3", relu(0, "m_3")), ("d4", diff(1, "gw", "gb")), ("r4", relu(1, "m_4"))],
+            ("A", fetch("ga", Y, "nba")), ("W", fetch("gw", Y, "nbw")), ("B", fetch("gb", Z, "nzp")),
+            [("d3", diff(0, "ga", "gb")), ("r3", relu(0, "m_3")), ("d4", diff(1, "gw", "gb")), ("r4", relu(1, "m_4"))],
             ("f1", fused("m_1", "nzq", "ga")), ("f2", fused("m_2", "nzq", "gw")),
             ("f3", fused("m_3", "nzp", "ga")), ("f4", fused("m_4", "nzp", "gw")),
-            ("x", lambda q: cp(q, R("xg"), ind(R("xt"), R("l4", 0, 16)))),
-            ("zq", lambda q: cp(q, R("zq"), ind(full(Z), R("l4", 16, 32)))),
+            ("pairs", lambda q: [cp(q, R("l2", 16 * (k // 2) + k % 2, 16 * (k // 2) + 16, 2), x) for k, x in enumerate((A_, W_, Q_, P_))]),
+            ("x", lambda q: cp(q, R("xg"), ind(R("xt"), AW))),
+            ("zq", lambda q: cp(q, R("zq"), ind(full(Z), QP))),
             ("dz", moved),
             ("sign", lambda q: act(R("sg"), R("p_t0", 0, 256), Fn.Sign)),
             ("a0", lambda q: last or act(R("a0"), Q_, bias=-2047.5 * 2 * BIG, scale=2 * BIG)),
@@ -607,17 +603,18 @@ def rank_program(g, core, T, topo):
             ("lower", lower),
         ])
 
+    whole("V", *PIECES[1])
     own_group("sz", "mz")
     own_group("sy", "my")
     offsets("oz", "sz")
-    offsets("oy", "sy")
-    act(rQ, ind(R("idt"), Q_))
+    act(R("rw", 256, 512), ind(R("idt"), QP))
     tt(ind(park(Z), R("oz")), R("zq"), R("sg"), Op.add)
     dma("Y", "d_zo", [(T.zo[:, :], own(Z))])
-    tc(ind(park("mt"), R("oy")), R("rw", 256, 512))
-    order("Y", [own("mt")], [], ("d_mo", 16))
-    g.sync.dma_start(T.mo[:, :], T.mt[0:128:16, NB:NB + V]).then_inc(T.sem["d_mo"], 16)
+    offsets("oy", "sy")
+    tc(ind(park("mw"), R("oy")), R("rw", 256, 512))
+    order("Y", [own("mw")], [], ("d_mo", 16))
+    g.sync.dma_start(T.mo[:, :], T.mw[0:128:16, NB:NB + V]).then_inc(T.sem["d_mo"], 16)
     count["d_mo"] = 16
 
-    for e in sorted(count):
+    for e in sorted(count, key=lambda e: e in ("d_mo", "d_zo")):
         wait("G", e, count[e])

from concourse.mybir import AluOpType as Op, AxisListType, ActivationFunctionType as Fn

V, NB, L, RO = 2048, 256, 128, 3
WIN = NB + V + NB
PAD = 16
KEY = 65536.0
BIG = 4096.0
EPS = 2.0 ** -20
FAR = 2.0 ** 20
OFF = 32.0
WHOLE = 1.5 * 2 ** 23

NAMING1 = {
    "V": "i2h mv mvs mvl nzv|im1 1 2|Z 0 64|dY 0 64|relu 0 64|max 64 96|n6 idt",
    "S": "wn wk s8|im1 0 1|nbv1 0 64|c1 n5|Z 64 128|nbv1 64 128|Y 96 128|Y 64 96|abs 96 128|cat|im1 3 4|im1 2 3|wg wp",
    "P": "gcP|imP 0 1|imP 1 2|rank|imP 2 3|mzP|imP 3 4|zP 64 96|sumz 64 96|diff 96 128|sumy 0 64|sumy 64 96|summ 0 64|sum 96 128|summ 64 96|catT",
}
NAMING = {
    "V": "sz oz newz sy oy newy sv vl mv mvs mvl nzv|whole 0 68|Z 64 128|dY 64 128|relu 64 128|max 32 64|n6|whole 68 96",
    "S": "rq ra gz newm gy nbv cb n5|Z 0 64|Y 0 32|Y 32 64|abs 0 32|cat im th",
    "P": "count rank|zP 32 64|sumz 32 64|diff 0 32|sumy 32 64|sumy 64 128|sum 0 32|summ 64 128|summ 32 64|catT",
    "G": "sendz sendy",
}
PIECES = [(96, 112), (112, 128)]
GAINS = {
    "V": "w af nzq nm ws|ka 7 8|wl|ka 6 7|wf|ka 0 6|kw 0 8|f1 0 64|f3 0 64|f1 64 128|f2 64 128|f4 0 64|f2 0 64|a1 av dv|prop 0 128",
    "S": "p a nba|A 0 64|nbw nzp|A 64 128|W 64 128|B 64 128|W 0 64|tc1 tc0|r3 64 96|r3 96 128|r4 64 96|r4 96 128|"
         "a0 pairs x zq places sign",
    "P": "void sameT zero|d3 64 96|d3 96 128|g1 0 128|d4 64 96|d4 96 128|g3 0 128|g4 0 128|g2 0 128 stop|dz|lower 0 128",
    "G": "mask1 mask0",
}

_B, _F, _H, _I, _U = "bfloat16", "float32", "float16", "int32", "uint16"
SCRATCH = {}
for _n, _w, _t in [
    ("nbt", V + PAD, _I), ("nzt", V + PAD, _I), ("xt", V + PAD, _B), ("idt", V + PAD, _F),
    ("z1", WIN, _B), ("z2", WIN, _B), ("z3", WIN, _B), ("y1", WIN, _B), ("y2", WIN, _B), ("y3", WIN, _B),
    ("mt", NB + V + PAD, _F), ("it", NB + V + PAD, _F), ("mw", NB + V, _F),
    ("mr", 128, _I), ("mlh", 128, _H), ("mlt", 128, _H), ("mlist", 128, _U),
    ("m2", 512, _I), ("i2", 512, _I), ("m2h", 512, _H), ("i2h", 512, _H),
    ("bx32", 16, _I), ("bz32", 16, _I), ("bxl", 16, _U), ("bzl", 16, _U),
    ("gz", NB, _B), ("gy", NB, _B),
    ("ones", 1024, _B), ("idn", 128, _B), ("idm", 128, _B), ("ide", 128, _B), ("id3", 128, _B), ("idf", 128, _B),
    ("gk", 8, _B), ("gk2", 8, _B), ("gkm", 8, _B), ("gp", 20, _B), ("gm", 20, _B),
    ("ej", 512, _B), ("sel", 1024, _B), ("tb", 128, _B),
    ("pi", 8, _I), ("pa", 8, _I), ("pf", 8, _F), ("cor0", 8, _F), ("cor", 8, _F),
    ("i16", 128, _F), ("t0", 128, _F), ("t1", 128, _F), ("gc", 320, _B),
    ("s8", 128, _F), ("s16", 256, _F), ("c1", 128, _F), ("mz", 160, _F), ("my", 160, _F), ("mv", 160, _F),
    ("li", 16, _F), ("alt", 16, _F),
    ("vl", 8, _U), ("mvr", 128, _F), ("mvs", 128, _F), ("mvl", 8, _U),
    ("nbv", 128, _U), ("nzv", 128, _U), ("cat", 256, _H),
    ("zg", 2048, _B), ("yg", 2048, _B), ("rr", 2048, _B),
    ("mx", 128, _F), ("gap", 128, _F), ("d1", 256, _F), ("sc", 256, _H), ("ls", 128, _F),
    ("l4", 32, _U), ("l2", 32, _U), ("l4f", 16, _F), ("wp", 256, _F), ("rw", 512, _F), ("ws", 256, _F), ("nm", 256, _H),
    ("nba", 128, _U), ("nzq", 128, _U), ("nbw", 128, _U), ("nzp", 128, _U),
    ("ga", 2048, _B), ("gw", 2048, _B), ("gb", 2048, _B),
    ("m_1", 2048, _B), ("m_2", 2048, _B), ("m_3", 2048, _B), ("m_4", 2048, _B),
    ("ka", 1152, _B), ("kw", 1152, _B), ("zero", 160, _B), ("tc", 1024, _B), ("tk", 1024, _B),
    ("xg", 256, _B), ("zq", 256, _B), ("sg", 256, _B),
    ("void", 24, _B), ("cs", 8, _F), ("prop", 24, _B), ("th", 8, _F),
    ("sz", 160, _F), ("sy", 160, _F), ("sv", 160, _F), ("oz", 16, _U), ("oy", 16, _U),
    ("n5", 8, _I), ("n6", 8, _I), ("a0", 8, _F), ("a1", 8, _F), ("av", 8, _F), ("cb", 8, _B),
    ("cn", 8, _F), ("cq", 8, _I),
]:
    SCRATCH[_n] = ("sbuf", [128, _w], _t)
for _n in ["p_a", "p_b", "p_d", "p_g", "p_l", "p_n", "p_t0", "p_t1"]:
    SCRATCH[_n] = ("psum", [128, 512], "float32")

DMAS = ["d_mr", "d_z", "d_bz", "d_bx", "d_m2", "d_i2", "d_nb0", "d_nb1", "d_nz", "d_x", "d_z2", "d_y2", "d_z3", "d_y3", "d_mo", "d_zo"]
SEMAPHORES = ["V", "S", "P", "G"] + DMAS + ["%s%s%d" % (k, w, t) for k in ("arr", "snt") for w in ("z", "y") for t in (1, 2, 3)]


def steps_of(text):
    out = []
    for part in text.split("|"):
        w = part.split()
        out += [(w[0], int(w[1]), int(w[2])) + tuple(w[3:])] if len(w) > 1 and w[1].isdigit() else [(x,) for x in w]
    return out


def rank_program(g, core, T, topo):
    rank = T.rank_of(core)
    if rank is None:
        return
    n = len(T.cores)
    dst = T.cores[(rank - 1) % n]
    rid, pid = topo.addr(dst)[:2]
    src_core = T.cores[(rank + 1) % n]

    Q = {"V": g.vector, "S": g.scalar, "P": g.tensor, "G": g, "Y": g.sync}
    count = {"V": 0, "S": 0, "P": 0, "G": 0}
    known = {q: {} for q in Q}
    clock = {}
    acc = {}
    held = []

    def psum(name):
        return name[:2] == "p_"

    def meet(r1, r2):
        if r1[0] != r2[0] or r1[1] >= r2[2] or r2[1] >= r1[2] or r1[3] >= r2[4] or r2[3] >= r1[4]:
            return False
        s = r1[5]
        return not (s == r2[5] and s > 1 and (r1[3] - r2[3]) % s)

    def wait(q, e, idx):
        kn = known[q]
        if kn.get(e, 0) >= idx:
            return
        Q[q].wait_ge(T.sem[e], idx)
        for e2, i2 in clock.get((e, idx), {}).items():
            if kn.get(e2, 0) < i2:
                kn[e2] = i2
        kn[e] = idx

    def order(q, reads, writes, me):
        need = {}
        for kind, regs in (("r", reads), ("w", writes)):
            for r in regs:
                for (e, k2, r2), idx in acc.get(r[0], {}).items():
                    same = e == q
                    if same and q == "P":
                        continue
                    if same or not psum(r[0]):
                        if (kind == "r" and k2 == "r") or not meet(r, r2):
                            continue
                    if need.get(e, 0) < idx:
                        need[e] = idx
        kn = known[q]
        for e in sorted(need, key=lambda e: -len(clock.get((e, need[e]), {}))):
            wait(q, e, need[e])
        e, idx = me
        clock[(e, idx)] = dict(kn)
        for kind, regs in (("r", reads), ("w", writes)):
            for r in regs:
                a = acc.setdefault(r[0], {})
                if kind == "w" and r[5] == 1 and not psum(r[0]):
                    for key in [k for k in a if k[2][1] >= r[1] and k[2][2] <= r[2] and k[2][3] >= r[3] and k[2][4] <= r[4] and k[0] != e]:
                        if kn.get(key[0], 0) >= a[key]:
                            del a[key]
                a[(e, kind, r)] = idx

    def R(name, c0=0, c1=None, step=1, p0=0, p1=128):
        return (name, p0, p1, c0, SCRATCH[name][1][1] if c1 is None else c1, step)

    def ap(r):
        if r[0] == "ind":
            return ap(r[1]).indirect(ap(r[2]))
        t = T[r[0]]
        return t[r[1]:r[2], r[3]:r[4]] if r[5] == 1 else t[r[1]:r[2], r[3]:r[4]:r[5]]

    def ind(w, o):
        return ("ind", w, o)

    def split(outs, ins):
        rd, wr = [], []
        for r in outs:
            if r[0] == "ind":
                wr.append(r[1])
                rd.append(r[2])
            else:
                wr.append(r)
        for r in ins:
            if r[0] == "ind":
                rd += [r[1], r[2]]
            else:
                rd.append(r)
        return rd, wr

    def issue(q, rd, wr, call):
        count[q] += 1
        order(q, rd, wr, (q, count[q]))
        call(Q[q]).then_inc(T.sem[q], 1)

    def run(q, outs, ins, call):
        rd, wr = split(outs, ins)
        if held:
            held[-1].append((q, rd, wr, call))
        else:
            issue(q, rd, wr, call)

    def phase(plan, makers):
        lines = {q: steps_of(text) for q, text in plan.items()}
        made = []
        for block in makers:
            block = block if isinstance(block, list) else [block]
            todo = [(s[1:2], x, q, s, f) for x, (name, f) in enumerate(block) for q in lines for s in lines[q] if s[0] == name]
            for _, _, q, s, f in sorted(todo, key=lambda e: e[:2]):
                held.append([])
                f(q, *s[1:])
                made.append((q, s, held.pop()))
        before = {}
        for x, (q, s, calls) in enumerate(made):
            rd = [r for c in calls for r in c[1]]
            wr = [r for c in calls for r in c[2]]
            before[q, s] = [(q2, s2) for q2, s2, c2 in made[:x] if q2 != q and any(
                meet(a, b) for c in c2 for a, bs in [(a, rd + wr) for a in c[2]] + [(a, wr) for a in c[1]] for b in bs)]
        calls = {(q, s): c for q, s, c in made}
        done = set()
        while any(lines.values()):
            q = [q for q in lines if lines[q] and all(b in done for b in before[q, lines[q][0]])][0]
            s = lines[q].pop(0)
            for c in calls[q, s]:
                if c[0] == "send":
                    send(*c[3])
                else:
                    issue(*c)
            done.add((q, s))

    def val(s):
        return ap(s) if isinstance(s, tuple) else s

    def tc(o, i):
        run("V", [o], [i], lambda q: q.tensor_copy(ap(o), ap(i)))

    def tt(o, a, b, op):
        run("V", [o], [a, b], lambda q: q.tensor_tensor(ap(o), ap(a), ap(b), op))

    def ts(o, i, s1, op0, s2=None, op1=None):
        ins = [i] + [s for s in (s1, s2) if isinstance(s, tuple)]
        if op1 is None:
            run("V", [o], ins, lambda q: q.tensor_scalar(ap(o), ap(i), val(s1), None, op0))
        else:
            run("V", [o], ins, lambda q: q.tensor_scalar(ap(o), ap(i), val(s1), val(s2), op0, op1))

    def scan(o, a, b, op0, op1):
        run("V", [o], [a, b], lambda q: q.tensor_tensor_scan(ap(o), ap(a), ap(b), 0.0, op0, op1))

    def tr(o, i):
        run("V", [o], [i], lambda q: q.transpose(ap(o), ap(i)))

    def ms(o, c):
        run("V", [o], [], lambda q: q.memset(ap(o), c))

    def act(o, i, fn=Fn.Copy, bias=0.0, scale=1.0):
        run("S", [o], [i], lambda q: q.activation(ap(o), ap(i), fn, bias, scale))

    def cp(q, o, i):
        (tc if q == "V" else act)(o, i)

    def mm(o, a, b, start=True, stop=True):
        run("P", [o], [a, b], lambda q: q.matmul(ap(o), ap(a), ap(b), start, stop))

    def iota(o, pat, base, cmul, flag=True):
        if flag:
            run("G", [o], [], lambda q: q.iota(ap(o), pat, base, cmul, allow_small_or_imprecise_dtypes=True))
        else:
            run("G", [o], [], lambda q: q.iota(ap(o), pat, base, cmul))

    def aff(o, i, pat, op, fill, base, cmul):
        run("G", [o], [i], lambda q: q.affine_select(ap(o), ap(i), pat, op, fill, base, cmul))

    def dma(q, sem, pairs):
        tot = 16 * len(pairs)
        for o, i in pairs:
            rd, wr = split([o] if isinstance(o, tuple) else [], [i] if isinstance(i, tuple) else [])
            order(q, rd, wr, (sem, tot))
            Q[q].dma_start(val(o), val(i)).then_inc(T.sem[sem], 16)
        count[sem] = tot

    def send(w, t, src):
        win = "%s%d" % (w, t)
        if held:
            held[-1].append(("send", [src], [R(win, NB + V, WIN)], (w, t, src)))
            return
        snt, arr = "snt" + win, "arr" + win
        mine, theirs = topo.engines(core, dst), topo.engines(src_core, core)
        order("G", [src], [], (snt, len(mine)))
        g.remote_dma(T[win][:, NB + V:WIN], ap(src), T.sem[arr], T.sem[snt], pid, rid, sum(1 << e for e in mine))
        count[snt], count[arr] = len(mine), len(theirs)
        acc.setdefault(win, {})[(arr, "w", R(win, NB + V, WIN))] = len(theirs)
        clock[(arr, len(theirs))] = {}

    def own(name):
        return R(name, NB, NB + V)

    def full(name):
        return R(name, NB)

    def park(name):
        return R(name, 0, NB + V)

    def C(name, a, b):
        return R(name, 16 * a, 16 * b)

    dma("S", "d_mr", [(R("mr", 64 * h, 64 * h + 64), T.m[h::2, :]) for h in range(2)])
    dma("Y", "d_bz", [(R("bz32"), T.bz[:, :])])
    dma("Y", "d_m2", [(R("m2", 0, 512, 1, 0, 32), T.m[:, :])])
    dma("Y", "d_z", [(own("z1"), T.z[:, :])])
    dma("Y", "d_bx", [(R("bx32"), T.bx[:, :])])
    dma("Y", "d_i2", [(R("i2", 0, 512, 1, 0, 32), T.im[:, :])])
    dma("Y", "d_nz", [(R("nzt", 0, V), T.nz[:, :])])

    def load_nb(h):
        dma("Y", "d_nb%d" % h, [(R("nbt", 1024 * h, 1024 * h + 1024), T.nb[:, 1024 * h:1024 * h + 1024])])

    load_nb(0)

    I_, IM = R("pf", 0, 1), R("pf", 1, 2)
    iota(R("pi", 0, 4), [[0, 2], [15, 2]], 0, 1, False)
    iota(R("i16"), [[0, 8], [1, 16]], 0, 0)
    iota(R("li"), [[16, 8], [128, 2]], 0, 0)
    ms(R("zero"), 0.0)
    run("S", [R("it", NB + V)], [R("zero", 0, PAD)], lambda e: e.activation(ap(R("it", NB + V)), ap(R("zero", 0, PAD)), Fn.Silu))
    ms(R("ones"), 1.0)
    aff(R("ej", 0, 512, 1, 0, 32), R("ones", 0, 512, 1, 0, 32), [[-1, 4], [-4, 8], [0, 16]], Op.is_equal, 0.0, 0, 1)
    ts(R("pa", 0, 4), R("pi", 0, 4), 15, Op.bitwise_and)
    ts(R("pa", 4, 8), R("pi", 0, 4), 4, Op.logical_shift_right)
    tc(R("pf"), R("pa"))
    aff(R("idn"), R("ones", 0, 128), [[-1, 128]], Op.is_equal, 0.0, 0, 1)
    ts(R("t0"), R("i16"), I_, Op.is_equal, BIG, Op.mult)
    ts(R("t1"), R("i16"), IM, Op.is_equal, -2 * BIG, Op.mult)
    ts(R("cor0", 0, 2), R("pf", 0, 8, 4), 0.0, Op.is_equal, 2 * BIG, Op.mult)
    tt(R("s16", 0, 128), R("t0"), R("t1"), Op.add)
    C16, C8 = R("cor", 0, 1), R("cor", 1, 2)
    act(R("bzl"), R("bz32"))
    for h in range(2):
        for b in range(4):
            cp("VVVVVSSS"[4 * h + b], R("mlh", 32 * b + 16 * h, 32 * b + 16 * h + 16), R("mr", 64 * h + 16 * b, 64 * h + 16 * b + 16))
    act(R("m2h", 0, 512, 1, 0, 32), R("m2", 0, 512, 1, 0, 32))
    tr(R("mlt"), R("mlh"))
    for b in range(4):
        tc(R("mlist", b, 128, 4), R("mlt", 32 * b, 32 * b + 32))
    act(R("gz"), ind(own("z1"), R("bzl")))
    send("z", 1, R("gz"))
    GK, S8, MZ, GP = (0, 8), (8, 136), (136, 296), (296, 316)
    aff(R("gc", *GK), R("ones", 0, 8), [[-4, 8]], Op.is_equal, 0.0, 0, 1)
    for src, base, fill in ((R("zero", 0, 128), 0, BIG), (R("gc", *S8), -4, -2 * BIG), (R("gc", *S8), 28, -2 * BIG)):
        aff(R("gc", *S8), src, [[0, 16], [-4, 8]], Op.not_equal, fill, base, 1)
    tc(R("y1", NB, NB + 1024), ind(own("z1"), R("mlist", 0, 64)))
    act(R("y1", NB + 1024, NB + V), ind(own("z1"), R("mlist", 64, 128)))
    act(R("bxl"), R("bx32"))
    ts(R("cor", 0, 2), R("cor0", 0, 2), -BIG, Op.add)
    ts(R("alt"), R("li"), I_, Op.add)
    ms(R("mt", NB + V), OFF)
    ts(R("vl"), R("alt", 0, 16, 2), 16.0, Op.mult)
    ms(R("nzt", V), 0)
    act(R("gy"), ind(own("y1"), R("bxl")))
    send("y", 1, R("gy"))
    aff(R("gc", *GP), R("ones", 0, 20), [[0, 2], [-4, 10]], Op.is_equal, 0.0, 4, 1)
    wait("Y", "G", count["G"])
    load_nb(1)
    for src, base, fill in ((R("ones", 0, 160), 0, 0.0), (R("gc", *MZ), 4, 1 / EPS)):
        aff(R("gc", *MZ), src, [[0, 16], [-4, 10]], Op.not_equal, fill, base, 1)
    iota(R("idt", 0, 1040), [[1, 1040]], 0, 0)
    aff(R("sel"), R("ones"), [[-16, 8], [0, 8], [-1, 16]], Op.is_equal, 0.0, 0, 1)
    wait("Y", "d_nb1", 16)
    dma("Y", "d_x", [(R("xt", 0, V), T.x[:, :])])

    def plus(q, o, i, c):
        if q == "V":
            ts(o, i, c, Op.add)
        else:
            act(o, i, bias=c)

    def spread(q, half, tab, off, bk, jb):
        if q == "P":
            mm(R(bk), R("ej", 128 * jb, 128 * jb + 128, 1, 0, 32), R(half, 0, 512, 1, 0, 32))
        else:
            plus(q, R(tab, NB + 512 * jb, NB + 512 * jb + 512), R(bk), off)

    for jb, bk in enumerate(("p_a", "p_b", "p_t0", "p_t1")):
        spread("P", "m2h", "mt", OFF, bk, jb)
        spread("SVSV"[jb], "m2h", "mt", OFF, bk, jb)

    def times(q, o, i, c):
        if q == "V":
            ts(o, i, c, Op.mult)
        else:
            act(o, i, scale=c)

    def naming_weights(q):
        act(R("tb"), R("i16"), bias=480.0, scale=-32.0)
        act(R("idm"), R("idn"), scale=-1.0)

    def group_weights(q):
        for o, s in (("gkm", -KEY), ("gk", KEY), ("gk2", 2 * KEY)):
            times(q, R(o), R("p_a", *GK), s)

    def pick_weights(q):
        cp(q, R("mz"), R("p_b", *MZ))
        for o, s in (("gp", 2.0), ("gm", -2.0)):
            times(q, R(o), R("p_b", *GP), s)

    def gain_weights(q):
        for o, s in (("ide", -EPS), ("id3", 3 * EPS), ("idf", -16 * FAR)):
            times(q, R(o), R("idn"), s)
        times(q, R("nbt", V), R("zero", 0, PAD), 0.0)
        cp(q, R("s16", 128, 256), R("s16", 0, 128))

    def commit_weights():
        for o in ("my", "mv"):
            act(R(o), R("mz"))
        for o in (R("xt", V), R("th")):
            act(o, R("zero", 0, o[4] - o[3]))
        plus("V", R("idt", 1600, V + PAD), R("idt", 576, 1040), 1024.0)

    def own_row(tmp, row):
        scan(tmp, row, R("s16", 0, row[4] - row[3]), Op.max, Op.add)

    def to_list(o, tmp):
        ts(o, (tmp[0], 0, 128, tmp[3] + 15, tmp[4], 16), C16, Op.add, 0.25 - OFF, Op.add)

    def own_group(s, m):
        scan(R(s), R("p_l", 0, 160), R(m), Op.max, Op.mult)

    def offsets(o, s):
        tt(R(o), R(s, 9, 160, 10), R("alt"), Op.max)

    A_, W_, P_, Q_ = [R("l4", 8 * k, 8 * k + 8) for k in range(4)]
    AW, QP = R("l2", 0, 16), R("l2", 16, 32)
    rW, rP = R("wp", 0, 128), R("wp", 128, 256)

    for t in range(1, RO + 1):
        Y, Z = "y%d" % t, "z%d" % t
        Yn, Zn = ("y%d" % (t + 1), "z%d" % (t + 1)) if t < RO else (Y, Z)
        first, last = t == 1, t == RO

        def nbv1(q, a, b):
            cp(q, R("nbv", a, b), R("nbt", 16 * a, 16 * b, 16))

        def put(tab, off, src):
            o = ind(park(tab), R(off))
            run("S", [o], [src], lambda e: e.activation(ap(o), ap(src), Fn.Silu))

        def whole(q, a, b):
            if last:
                ts(R("mw", NB + 16 * a, NB + 16 * b), R("mt", NB + 16 * a, NB + 16 * b), WHOLE - OFF, Op.add, WHOLE, Op.subtract)

        def th(q):
            cn, cq = R("cn", 0, 1), R("cq", 0, 1)
            run("S", [R("cs"), cn], [R("p_l", 200, 208)],
                lambda e: e.activation(ap(R("cs")), ap(R("p_l", 200, 208)), Fn.Copy, 0.0, 1.0, accum_out=ap(cn)))
            act(cq, cn, bias=-31.0 / 64, scale=1.0 / 32)
            run("S", [R("th", 0, 1)], [cq, cn], lambda e: e.activation(ap(R("th", 0, 1)), ap(cq), Fn.Identity, ap(cn), -32.0))

        def sums(src, wgt, a, b, stop):
            for k in range(16):
                mm(R("p_d", k, 128, 16, a, b), R(src, 16 * a + k, 16 * b, 16), R(wgt), False, stop and k == 15)

        def nbank(a, b):
            return R(("p_a", "p_b", "p_t0", "p_t1")[a // 32], 16 * (a % 32), 16 * (a % 32 + b - a))


        phase(NAMING1 if first else NAMING, [
            ("i2h", lambda q: cp(q, R("i2h", 0, 512, 1, 0, 32), R("i2", 0, 512, 1, 0, 32))),
            ("gcP", lambda q: [mm(R("p_a", *c), R("ej", 0, 128, 1, 0, 32), R("gc", *c, 1, 0, 32)) for c in (GK, S8)]),
            ("mzP", lambda q: [mm(R("p_b", *c), R("ej", 0, 128, 1, 0, 32), R("gc", *c, 1, 0, 32)) for c in (MZ, GP)]),
            ("wn", naming_weights), ("wk", group_weights), ("wp", pick_weights), ("wg", gain_weights),
            ("s8", lambda q: cp(q, R("s8"), R("p_a", *S8))),
            ("c1", lambda q: act(R("c1"), R("i16"), Fn.Sign)),
            ("idt", lambda q: plus(q, R("idt", 1040, 1600), R("idt", 16, 576), 1024.0)),
            [("imP", lambda q, a, b: spread(q, "i2h", "it", OFF, ("p_g", "p_l")[a % 2], a)),
             ("im1", lambda q, a, b: spread(q, "i2h", "it", OFF, ("p_g", "p_l")[a % 2], a))],
            ("sz", lambda q: own_group("sz", "mz")), ("oz", lambda q: offsets("oz", "sz")),
            ("sy", lambda q: own_group("sy", "my")), ("oy", lambda q: offsets("oy", "sy")),
            ("rq", lambda q: plus(q, R("rw", 256, 512), ind(R("idt"), QP), OFF)),
            ("ra", lambda q: plus(q, R("rw", 0, 256), ind(R("idt"), AW), OFF)),
            ("newz", lambda q: tt(ind(park(Z), R("oz")), R("zq"), R("sg"), Op.add)),
            ("newy", lambda q: tt(ind(park(Y), R("oy")), R("zq"), R("sg"), Op.add)),
            ("gz", lambda q: cp(q, R("gz"), ind(own(Z), R("bzl")))),
            ("gy", lambda q: cp(q, R("gy"), ind(own(Y), R("bxl")))),
            ("sendz", lambda q: send("z", t, R("gz"))),
            ("sendy", lambda q: send("y", t, R("gy"))),
            ("sv", lambda q: own_group("sv", "mv")),
            ("vl", lambda q: tt(R("vl"), R("sv", 19, 160, 20), R("av"), Op.add)),
            ("newm", lambda q: put("mt", "oy", R("rw", 256, 512))),
            ("mv", lambda q: cp(q, R("mvr"), ind(full("mt"), R("vl")))),
            ("mvs", lambda q: own_row(R("mvs"), R("mvr"))), ("mvl", lambda q: to_list(R("mvl"), R("mvs"))),
            ("nbv1", nbv1),
            ("nbv", lambda q: first or cp(q, R("nbv"), ind(R("nbt"), R("vl")))),
            ("nzv", lambda q: cp(q, R("nzv"), ind(R("nzt"), R("mvl")))),
            ("im", lambda q: put("it", "oz", R("rw", 0, 256))),
            ("whole", whole),
            ("cb", lambda q: cp(q, R("cb"), R("sv", 9, 160, 20))),
            ("count", lambda q: first or mm(R("p_l", 200, 208), R("ones", 0, 128), R("cb"))),
            ("th", th),
            ("cat", lambda q: [cp(q, R("cat", 128 * x, 128 * x + 128), R(s)) for x, s in enumerate(("nbv", "nzv"))]),
            ("catT", lambda q: [mm(R("p_n", 128 * x, 128 * x + 128), R("cat", 128 * x, 128 * x + 128), R("idn")) for x in range(2)]),
            ("rank", lambda q: mm(R("p_d", 0, 128), R("ones", 0, 128), R("tb"), True, False)),
            ("Z", lambda q, a, b: cp(q, C("zg", a, b), ind(full(Z), R("nzv", a, b)))),
            ("Y", lambda q, a, b: cp(q, C("yg", a, b), ind(full(Y), R("nbv", a, b)))),
            ("diff", lambda q, a, b: [mm(nbank(a, b), R("idn"), C("yg", a, b), True, False), mm(nbank(a, b), R("idm"), C("zg", a, b), False, True)]),
            ("abs", lambda q, a, b: act(C("rr", a, b), nbank(a, b), Fn.Abs)),
            ("dY", lambda q, a, b: tt(C("yg", a, b), ind(full(Y), R("nbv", a, b)), C("zg", a, b), Op.subtract)),
            ("absd", lambda q, a, b: act(C("rr", a, b), C("yg", a, b), Fn.Abs)),
            ("relu", lambda q, a, b: ts(C("rr", a, b), C("yg", a, b), 0.0, Op.max)),
            ("sum", lambda q, a, b: sums("rr", "gk", a, b, True)),
            ("zP", lambda q, a, b: mm(nbank(a, b), R("idn"), C("zg", a, b))),
            ("max", lambda q, a, b: tt(C("rr", a, b), nbank(a, b), C("yg", a, b), Op.max)),
            ("sumz", lambda q, a, b: sums("zg", "gkm", a, b, False)),
            ("sumy", lambda q, a, b: sums("yg", "gkm", a, b, False)),
            ("summ", lambda q, a, b: sums("rr", "gk2", a, b, True)),
            ("n5", lambda q: last or act(R("n5"), R("vl"), bias=1.0, scale=5.0)),
            ("n6", lambda q: last or ts(R("n6"), R("n5"), 2047, Op.bitwise_and)),
        ])
        if not last:
            wait("Y", "snt" + Y, count["snt" + Y])
            dma("Y", "d_" + Zn, [(own(Zn), own(Z))])
            dma("Y", "d_" + Yn, [(own(Yn), own(Y))])
        scan(R("mx"), R("c1"), R("p_d", 0, 128), Op.mult, Op.max)
        tt(R("gap"), R("mx"), R("p_d", 0, 128), Op.subtract)
        for x in range(2):
            tt(R("d1", 128 * x, 128 * x + 128), R("p_n", 128 * x, 128 * x + 128), R("gap"), Op.subtract)
        for x in range(2):
            scan(R("sc", 128 * x, 128 * x + 128), R("gap"), R("d1", 128 * x, 128 * x + 128), Op.min, Op.max)
        for c in range(8):
            mm(R("p_l", 16 * c, 16 * c + 16), R("sel", 128 * c, 128 * c + 128), R("sc", 15, 256, 16))
        act(R("void", 0, 8), R("mx", 15, 128, 16), Fn.Relu, 1.0, -1.0 / KEY)
        act(R("void", 8, 24), R("sc", 15, 256, 16), Fn.Relu, 1.0 - V)
        if first:
            commit_weights()
        whole("V", *PIECES[0])
        scan(R("ls"), R("p_l", 0, 128), R("s8"), Op.max, Op.add)
        ts(A_, R("ls", 7, 128, 16), C8, Op.add, float(V), Op.min)
        ts(Q_, R("ls", 15, 128, 16), C8, Op.add, float(V), Op.min)

        def same(kk, s):
            def f(q, a, b):
                for c in reversed(range(a, b)):
                    at = 16 * c * (c + 1)
                    ts(R(kk, at, at + 32 * (c + 1)), R("nm", 0, 32 * (c + 1)), R("l4f", s + c, s + c + 1), Op.is_equal)
            return f

        def same_turned(q):
            for c in reversed(range(8)):
                o = R("p_t%d" % (c // 4), 128 * (c % 4), 128 * (c % 4) + 128)
                at = 16 * c * (c + 1)
                mm(o, R("id3"), R("sel", 128 * c, 128 * c + 128), True, False)
                for x, (kk, y) in enumerate((("ka", 0), ("ka", 1), ("kw", 0), ("kw", 1))):
                    mm(o, R(kk, at + y, at + 256, 2), R("ide"), False, x == 3)

        def mask(x):
            h = (512 * x, 512 * x + 512)
            aff(R("tk", *h), R("tc", *h), [[16, 4], [0, 8], [1, 16]], Op.is_ge, 0.0, 64 * x, -1)

        def fetch(o, win, lst):
            return lambda q, a, b: cp(q, C(o, a, b), ind(full(win), R(lst, a, b)))

        def bank(x, a, b):
            return R((("p_a", "p_d"), ("p_b", "p_n"))[x][a // 32 % 2], 16 * (a % 32), 16 * (a % 32 + b - a))

        def gain(mx, wgt):
            return lambda q, a, b, flag="": [mm(R("p_g", 0, 20, 1, a, b), R(mx, 16 * a + k, 16 * b, 16), R(wgt), False,
                                                flag == "stop" and k == 15) for k in range(16)]

        def fused(mx, lst, src):
            return lambda q, a, b: tt(C(mx, a, b), ind(full(Z), R(lst, a, b)), C(src, a, b), Op.max)

        def diff(x, src, sub):
            return lambda q, a, b: [mm(bank(x, a, b), R("idn"), C(src, a, b), True, False), mm(bank(x, a, b), R("idm"), C(sub, a, b), False, True)]

        def relu(x, mx):
            return lambda q, a, b: act(C(mx, a, b), bank(x, a, b), Fn.Relu)

        def moved(q):
            mm(R("p_t0", 0, 256), R("idn"), R("xg"), True, False)
            mm(R("p_t0", 0, 256), R("idm"), R("zq"), False, True)

        def places(q):
            for o, lst in (("mz", QP), ("my", AW)):
                plus(q, R(o, 9, 160, 10), lst, float(NB))

        def lower(q, a, b):
            for c in range(a // 16, 8):
                mm(R("p_l", 20 * c, 20 * c + 20), R("tk", 128 * c, 128 * c + 128, 1, a, b), R("prop", 0, 20, 1, a, b), False, b == L and c == 7)

        phase(GAINS, [
            ("nba", lambda q: cp(q, R("nba"), ind(R("nbt"), A_))),
            ("a", lambda q: cp(q, R("nm", 0, 256, 2), ind(R("idt"), A_))),
            ("w", lambda q: cp(q, rW, ind(full("it"), Q_))),
            ("p", lambda q: cp(q, rP, ind(full("mt"), A_))),
            ("ws", lambda q: own_row(R("ws"), R("wp"))), ("wl", lambda q: to_list(R("l4", 8, 24), R("ws"))),
            ("nzq", lambda q: cp(q, R("nzq"), ind(R("nzt"), Q_))),
            ("nbw", lambda q: cp(q, R("nbw"), ind(R("nbt"), W_))),
            ("nzp", lambda q: cp(q, R("nzp"), ind(R("nzt"), P_))),
            ("af", lambda q: cp(q, R("l4f", 0, 8), A_)), ("wf", lambda q: cp(q, R("l4f", 8, 16), W_)),
            ("nm", lambda q: ts(R("nm", 1, 256, 2), rW, WHOLE - OFF, Op.add, WHOLE, Op.subtract)),
            ("ka", same("ka", 0)), ("kw", same("kw", 8)), ("sameT", same_turned),
            ("tc0", lambda q: cp(q, R("tc", 0, 512), R("p_t0"))),
            ("tc1", lambda q: cp(q, R("tc", 512, 1024), R("p_t1"))),
            ("mask0", lambda q: mask(0)), ("mask1", lambda q: mask(1)),
            ("A", fetch("ga", Y, "nba")), ("W", fetch("gw", Y, "nbw")), ("B", fetch("gb", Z, "nzp")),
            [("d3", diff(0, "ga", "gb")), ("r3", relu(0, "m_3")), ("d4", diff(1, "gw", "gb")), ("r4", relu(1, "m_4"))],
            ("f1", fused("m_1", "nzq", "ga")), ("f2", fused("m_2", "nzq", "gw")),
            ("f3", fused("m_3", "nzp", "ga")), ("f4", fused("m_4", "nzp", "gw")),
            ("pairs", lambda q: [cp(q, R("l2", 16 * (k // 2) + k % 2, 16 * (k // 2) + 16, 2), x) for k, x in enumerate((A_, W_, Q_, P_))]),
            ("x", lambda q: cp(q, R("xg"), ind(R("xt"), AW))),
            ("zq", lambda q: cp(q, R("zq"), ind(full(Z), QP))),
            ("dz", moved),
            ("sign", lambda q: act(R("sg"), R("p_t0", 0, 256), Fn.Sign)),
            ("a0", lambda q: last or act(R("a0"), Q_, bias=-2047.5 * 2 * BIG, scale=2 * BIG)),
            ("places", places),
            ("a1", lambda q: last or tt(R("a1"), R("a0"), R("n6"), Op.min)),
            ("av", lambda q: last or tt(R("av"), R("a1"), R("l4f", 8, 16), Op.max)),
            ("dv", lambda q: last or tt(R("mv", 19, 160, 20), R("l4f", 0, 8), R("av"), Op.subtract)),
            ("void", lambda q: [mm(R("p_g", 0, 20), R("idn"), R("zero", 0, 20), True, False)]
             + [mm(R("p_g", 1 + 10 * r, 9 + 10 * r), R("idf"), R("void", 8 * x, 8 * x + 8), False, False) for r in range(2) for x in range(3)]),
            ("g1", gain("m_1", "gm")),
            ("g2", gain("m_2", "gp")), ("g3", gain("m_3", "gp")), ("g4", gain("m_4", "gm")),
            ("zero", lambda q: mm(R("p_l", 0, 160), R("idn"), R("zero"), True, False)),
            ("prop", lambda q, a, b: ts(R("prop", 0, 20, 1, a, b), R("p_g", 0, 20, 1, a, b), R("th", 0, 1, 1, a, b), Op.is_gt)),
            ("lower", lower),
        ])

    whole("V", *PIECES[1])
    own_group("sz", "mz")
    own_group("sy", "my")
    offsets("oz", "sz")
    act(R("rw", 256, 512), ind(R("idt"), QP))
    tt(ind(park(Z), R("oz")), R("zq"), R("sg"), Op.add)
    dma("Y", "d_zo", [(T.zo[:, :], own(Z))])
    offsets("oy", "sy")
    tc(ind(park("mw"), R("oy")), R("rw", 256, 512))
    order("Y", [own("mw")], [], ("d_mo", 16))
    g.sync.dma_start(T.mo[:, :], T.mw[0:128:16, NB:NB + V]).then_inc(T.sem["d_mo"], 16)
    count["d_mo"] = 16

    for e in sorted(count, key=lambda e: e in ("d_mo", "d_zo")):
        wait("G", e, count[e])
